import numpy as np, ml_dtypes
CORES = [2,6,10,14,18,22,26,30]
N = 8
import mx_ref
BF = ml_dtypes.bfloat16
def gentries(a):
    return np.ascontiguousarray(a.reshape(8, 16, -1).transpose(0, 2, 1)).reshape(8, -1)
def gtable(e):
    e = np.asarray(e); return np.ascontiguousarray(e.reshape(8, -1, 16).transpose(0, 2, 1)).reshape(128, -1).astype(np.int32)
def gcols(t, e):
    v = np.concatenate([t.reshape(8, 16, -1, 4), np.zeros((8, 16, 1, 4), BF)], axis=2)
    return np.ascontiguousarray(np.stack([v[g][:, e[g]] for g in range(8)])).reshape(128, -1)
def tile(rs):
    return np.stack(rs, axis=2).reshape(128, -1).astype(BF)
def pick(q, e):
    c = np.concatenate([q[0].reshape(128, -1, 4), np.zeros((128, 1, 4), np.uint8)], axis=1); s = np.concatenate([q[1], np.ones((16, 1), np.uint8)], axis=1)
    return (np.ascontiguousarray(c[:, e].reshape(128, -1)), np.ascontiguousarray(s[:, e]))
def join(*qs):
    return (np.concatenate([q[0] for q in qs], axis=1), np.concatenate([q[1] for q in qs], axis=1))
def put(q, e, v):
    c, s = q[0].reshape(128, -1, 4).copy(), q[1].copy(); c[:, e] = v[0].reshape(128, -1, 4); s[:, e] = v[1]
    return (c.reshape(128, -1), s)
def pk(c, s):
    return (np.ascontiguousarray(c), mx_ref.live(s))
def emit(q):
    return q[0], q[1]
def packed(v, rng):
    q = [mx_ref.quantize(np.ascontiguousarray(v[r])) for r in range(N)]
    return np.stack([a for a, b in q]), np.stack([mx_ref.plane(b, rng) for a, b in q])
def values_of_codes():
    e, c = np.zeros((128, 128, 4), np.float32), np.zeros((128, 2, 4), np.uint8)
    e[np.arange(128), np.arange(128), 0] = 1
    c[:127, :, 0] = np.arange(256).reshape(2, 128).T[:127]
    return mx_ref.matmul(mx_ref.quantize(e.reshape(128, 512).astype(BF)), (c.reshape(128, 8), np.full((16, 2), 127, np.uint8))).T.reshape(-1).astype(np.float64)
CODE_VALUE, SCALE_VALUE = values_of_codes(), 2.0 ** (np.arange(256) - 127.0)
def decode(q):
    return (CODE_VALUE[q[0]].reshape(16, 8, -1, 4) * SCALE_VALUE[q[1]][:, None, :, None] + 0.0).reshape(128, -1).astype(np.float32)
def f(rng, *shape):
    return mx_ref.flush((rng.standard_normal(shape, dtype=np.float32) * np.exp2(rng.integers(-2, 3, shape[:-1] + (1,)))).astype(BF))
def wide(rng, *shape, cols=0):
    v = rng.standard_normal(shape, dtype=np.float32) * np.exp2(rng.integers(-12, 13, shape)).astype(np.float32)
    if cols: v *= np.repeat(np.exp2(rng.integers(-cols, cols + 1, shape[:-2] + (1, shape[-1] // 4))) * (rng.random(shape[:-2] + (1, shape[-1] // 4)) > 0.0625), 4, axis=-1).astype(np.float32)
    return mx_ref.flush(v.astype(BF))
C = 384
STEP = [1, 2, 4]
def big(v):
    v = v.astype(np.float32)
    v[np.abs(v) < np.float32(2.0 ** -16)] = 0
    return v.astype(BF)
def numbers_of(rng):
    return {"x": big(f(rng, N, 128, 4 * C)), "u": np.array(f(rng, N, 128, 512)), "v": np.array(f(rng, N, 128, 512))}
def stored(k, t):
    return {"gl": np.stack([gtable(k[r]) for r in range(N)]), "ht": np.stack([gtable(t[r]) for r in range(N)])}
def lists(rng):
    e = np.tile(np.arange(C), (N, 8, 1))
    k = np.stack([rng.permuted(e, axis=2), rng.permuted(e, axis=2)], axis=3).reshape(N, 8, 2 * C)
    return stored(k, rng.integers(0, C, (N, 8, C)))
def layers(rng):
    return big(f(rng, N, 128, 2048)).reshape(N, 8, 16, 4, 8, 16, 4)
def weights(rng, w):
    c, p = packed(np.ascontiguousarray(w).reshape(N, 128, 2048), rng)
    return {"wc": c, "ws": p}
def setup_inputs(rng):
    return {**numbers_of(rng), **lists(rng), **weights(rng, layers(rng))}
def setup_inputs_ties(rng):
    d = numbers_of(rng)
    o = rng.permutation(N)
    k = rng.integers(-1, 2, (N, 8, C)).astype(np.float32)
    k[o[1]] = 1
    x = d["x"].reshape(N, 8, 16, C, 4)
    x[:, :, 0] = 0
    x[:, :, 0, :, 0] = k.astype(BF)
    c = np.ones(N, np.float32)
    c[o[0]] = 0
    c[o[2]] = -1
    u = d["u"].reshape(N, 128, 128, 4)
    u[:, :, ::16] = 0
    for h in range(0, 128, 16): u[:, h, h, 0] = c.astype(BF)
    w = layers(rng)
    w[:, :, :, :, :, :8] = 0
    return {"x": x.reshape(N, 128, 4 * C), "u": u.reshape(N, 128, 512), "v": d["v"], **lists(rng), **weights(rng, w)}
def setup_inputs_near(rng):
    d = numbers_of(rng)
    o = rng.permutation(N) % 2
    k = np.where(o == 0, 2.0 ** -30, 1.0).astype(np.float32)
    x = np.zeros((N, 8, 16, C, 4), np.float32)
    s = rng.integers(-1, 2, (N, 8, C)) * k[:, None, None]
    x[:, :, 0, :, 0] = 1.125 * s
    x[:, :, 1, :, 0] = -1.25 * s
    for r in range(N):
        for g in rng.permutation(8)[:4]: x[r, g, 0, rng.integers(C), 0] = 2.0 ** 30 * rng.choice([-1.0, 1.0])
    i = np.arange(N)
    e = ((i ^ (i >> 1) ^ (i >> 2))[:, None] + rng.permutation(8)) % 2
    a = (1 + (2 * rng.integers(0, 64, (N, 8, 8, C, 4)) + 1) * 2.0 ** -7) * np.exp2(12.0 - rng.integers(8, 15, (N, 8, 8, C, 4)))
    a[:, :, 0, :, 0] = -1.96875 * 2.0 ** 12
    a = np.where(e[:, :, None, None, None] == 0, -2.0 ** 26, a)
    x[:, :, 8:] = np.where(rng.random((N, 8, 1, C, 1)) < 0.5, a, 0.0)
    u = d["u"].reshape(N, 128, 128, 4)
    u[:, :, ::16] = 0
    for h in range(0, 128, 16):
        u[:, h, h, 0] = (1.125 * k).astype(BF)
        u[:, h + 1, h, 0] = k.astype(BF)
    w = layers(rng)
    w[:, :, :8] = 0
    w[:, :, :, :, :, :8] = 0
    return {"x": x.reshape(N, 128, 4 * C).astype(BF), "u": u.reshape(N, 128, 512), "v": d["v"], **lists(rng), **weights(rng, w)}
def setup_inputs_late(rng):
    d = numbers_of(rng)
    c = (rng.permutation(N) % 2 * 2.0 - 1.0).astype(np.float32).astype(BF)
    x = d["x"].reshape(N, 8, 16, C, 4)
    x[:, :, 0] = c[:, None, None, None]
    u = d["u"].reshape(N, 128, 128, 4)
    u[:, :, ::16] = 0
    for h in range(0, 128, 16): u[:, h, h, 0] = 1
    w = layers(rng)
    w[:, :, :, :, :, 0] = (w[:, :, :, :, :, 0].astype(np.float32) * 4).astype(BF)
    return {"x": x.reshape(N, 128, 4 * C), "u": u.reshape(N, 128, 512), "v": d["v"], **lists(rng), **weights(rng, w)}
def setup_inputs_ends(rng):
    d = numbers_of(rng)
    o, e = rng.permutation(N) % 4, rng.permutation(N) % 4
    s = rng.choice([-1.0, 1.0], (N, 128, C, 4))
    s[o == 0] = -1
    s[o == 1] = rng.choice([-1.0, 1.0], (N, 1, C, 1))[o == 1]
    x = s * (0.955 + 0.02 * rng.random((N, 128, C, 4))) * 2.0 ** 30
    x[:, :8] = 0
    x[:, 13] = -240 * 2.0 ** 22
    x[:, 14] = -249 * 2.0 ** 22
    x[:, 15] = 0
    x[o == 3] = 2.0 ** -30
    size = np.where(o == 3, 2.0 ** -30, 2.0 ** 30)
    a = np.stack([rng.permutation(8) % 2 * 2.0 - 1.0 for r in range(N)]) * size[:, None]
    u = d["u"].reshape(N, 128, 128, 4)
    u[:, :, ::16] = a.astype(np.float32).astype(BF)[:, None, :, None]
    v = rng.choice([-1.0, 1.0], (N, 128, 512)) * size[:, None, None]
    t = rng.integers(0, C, (N, 8, C))
    t[o == 0] = C - 1
    t[o == 1] = 0
    t[o == 2] = rng.integers(0, 2, (8, C)) * (C - 1)
    k = rng.integers(0, C, (N, 8, 2 * C))
    k[e == 0] = C - 1
    k[e == 1] = 0
    k[e == 1, 7] = C - 1
    k[e == 2] = np.arange(2 * C) % 2 * (C - 1)
    w = np.zeros((N, 128, 4, 128, 4), np.float32)
    i = np.arange(128)
    for b in range(4):
        w[:, i, b, i, b] = np.where(o == 3, 16.0, -0.25)[:, None]
        for r in range(N):
            if o[r] < 3:
                w[r, :8, b, :8, b] = 64 * np.eye(8)
                w[r, 13:16, b, 13:16, b] = [[0, 0, -64], [0, 0, 64], [0, 0, 0]]
    return {"x": x.astype(np.float32).reshape(N, 128, 4 * C).astype(BF), "u": u.reshape(N, 128, 512), "v": v.astype(np.float32).astype(BF), **stored(k, t), **weights(rng, w.astype(BF))}
def setup_inputs_spread(rng):
    d = setup_inputs(rng)
    d["x"] = big(wide(rng, N, 128, 4 * C, cols=6))
    return d
def check_inputs(d):
    b = []
    for k in ("x", "u", "v"):
        a = np.abs(d[k].astype(np.float32))
        if not (np.isfinite(a).all() and ((a == 0) | (a >= 2.0 ** -30) & (a <= 2.0 ** 30)).all()): b.append("a value of " + k)
    for k in ("gl", "ht"):
        if not ((d[k] >= 0) & (d[k] < C)).all(): b.append("an entry of " + k)
    none, least, most = [emit(mx_ref.quantize(np.full((128, 16), k, np.float32).astype(BF)))[1][0, 0] for k in (0.0, 2.0 ** -30, 2.0 ** 30)]
    for r in range(N):
        if ((d["wc"][r] == 0x7F) | (d["wc"][r] == 0xFF)).any(): b.append("wc: a code that is no number")
        s = mx_ref.live(d["ws"][r])
        if ((s != none) & ((s < least) | (s > most))).any(): b.append("ws: a scale out of range")
        if (((d["wc"][r].reshape(16, 8, 512, 4) & 0x7F) != 0) & (s == none)[:, None, :, None]).any(): b.append("wc: a code other than zero under the scale of zeros")
    return b
def reference(x, u, v, gl, ht, wc, ws):
    qu = [mx_ref.quantize(u[r]) for r in range(N)]
    lay = [pk(wc[r], ws[r]) for r in range(N)]
    guest, host = [gentries(gl[r]) for r in range(N)], [gentries(ht[r]) for r in range(N)]
    now = [x[r] for r in range(N)]
    y, pl = np.zeros((N, 128, C), np.float32), np.zeros((N, 8, C), np.float32)
    for step in STEP:
        q = [mx_ref.quantize(now[r]) for r in range(N)]
        bit = [(mx_ref.matmul(qu[r], q[r])[::16] > 0).astype(np.int64) for r in range(N)]
        made = []
        for r in range(N):
            p = r ^ step
            at, there = np.zeros((9, C), np.int64), np.zeros((8, C), np.int64)
            at[0] = np.arange(C)
            for g in range(8):
                there[g] = host[p][g][at[g]]
                at[g + 1] = guest[r][g][2 * at[g] + bit[p][g][there[g]]]
            far = gcols(decode(q[p]).astype(BF), there)
            z = mx_ref.quantize(np.maximum(gcols(now[r], at[:8]).astype(np.float32), far.astype(np.float32)).astype(BF))
            made.append(tile([mx_ref.matmul(pick(lay[r], np.arange(128 * b, 128 * b + 128)), z) * np.float32(0.015625) + now[r][:, b::4].astype(np.float32) for b in range(4)]))
            pl[r] = at[1:]
        now = made
    oc, osc = np.zeros((N, 128, 4 * C), np.uint8), np.zeros((N, 16, C), np.uint8)
    for r in range(N):
        q = mx_ref.quantize(now[r])
        y[r] = mx_ref.matmul(mx_ref.quantize(v[r]), q)
        oc[r], osc[r] = emit(q)
    return {"y": y, "pl": pl, "oc": oc, "osc": osc}

@@ -1,0 +1,356 @@
+import numpy as np
+from concourse.mybir import dt, AluOpType, ActivationFunctionType
+
+C = 384
+H = 192
+NH = 2
+STEP = [1, 2, 4]
+ALU = AluOpType
+COPY = ActivationFunctionType.Copy
+
+SCRATCH = {
+    "ut": ("sbuf", [128, 512], "bfloat16"), "vt": ("sbuf", [128, 512], "bfloat16"),
+    "uq": ("sbuf", [128, 128], "float8_e4m3fn_x4"), "us": ("sbuf", [128, 128], "uint8"),
+    "uqr": ("sbuf", [128, 128], "float8_e4m3fn_x4"), "usr": ("sbuf", [128, 128], "uint8"),
+    "vq": ("sbuf", [128, 128], "float8_e4m3fn_x4"), "vs": ("sbuf", [128, 128], "uint8"),
+    "wq": ("sbuf", [128, 512], "float8_e4m3fn_x4"), "wsp": ("sbuf", [128, 512], "uint8"),
+    "e0": ("sbuf", [128, 2048], "bfloat16"), "et": ("sbuf", [128, 2048], "bfloat16"),
+    "eq": ("sbuf", [128, 512], "float8_e4m3fn_x4"), "es": ("sbuf", [128, 512], "uint8"),
+    "x64": ("sbuf", [128, 4 * C], "bfloat16"), "lx": ("sbuf", [128, 4 * C], "bfloat16"),
+    "m": ("sbuf", [128, 4 * C], "bfloat16"), "z": ("sbuf", [128, 4 * C], "bfloat16"),
+    "zq": ("sbuf", [128, C], "float8_e4m3fn_x4"), "zs": ("sbuf", [128, C], "uint8"),
+    "xq": ("sbuf", [128, C], "float8_e4m3fn_x4"), "xs": ("sbuf", [128, C], "uint8"),
+    "uu": ("sbuf", [128, 8 * H], "float32"),
+    "gli": ("sbuf", [128, 48], "int32"), "gl16": ("sbuf", [128, 48], "uint16"),
+    "hti": ("sbuf", [128, 24], "int32"), "ht16": ("sbuf", [128, 24], "uint16"), "ht4": ("sbuf", [128, 96], "uint16"),
+    "glf": ("sbuf", [128, 768], "float32"),
+    "bits": ("sbuf", [128, C], "bfloat16"), "t1": ("sbuf", [128, C], "float32"),
+    "ft": ("sbuf", [128, 8 * C], "bfloat16"),
+    "w1": ("sbuf", [128, 48], "float32"), "w2": ("sbuf", [128, 48], "float32"),
+    "ov0": ("sbuf", [128, 4], "uint16"), "ov": ("sbuf", [128, 4], "uint16"), "vo": ("sbuf", [128, 32], "uint16"),
+    "ident": ("sbuf", [128, 768], "float32"), "ip": ("sbuf", [128, 1], "int32"), "k8": ("sbuf", [128, 8], "int32"),
+    "row": ("sbuf", [128, 48], "float32"), "c16": ("sbuf", [128, 24], "float32"), "upi": ("sbuf", [128, 8], "int32"),
+    "up": ("sbuf", [128, 8], "uint16"), "ia": ("sbuf", [128, 4], "int32"), "fa": ("sbuf", [128, 4], "float32"),
+    "kk": ("sbuf", [128, 8], "int32"), "kf": ("sbuf", [128, 8], "float32"), "jl": ("sbuf", [128, 24], "uint16"),
+    "jw": ("sbuf", [128, 4], "float32"), "mask": ("sbuf", [128, 48], "float32"), "keep": ("sbuf", [128, 48], "float32"),
+    "ysb": ("sbuf", [128, C], "float32"), "plb": ("sbuf", [128, C], "float32"), "plc": ("sbuf", [128, C], "float32"),
+    "vl8": ("dram", [128, 24], "uint16"), "vland8": ("sbuf", [128, 24], "uint16"),
+    "psa": ("psum", [128, 2048], "float32"), "psb": ("psum", [128, 2048], "float32"),
+}
+for _r in range(3):
+    SCRATCH["lq%d" % _r] = ("sbuf", [128, C], "float8_e4m3fn_x4")
+    SCRATCH["ls%d" % _r] = ("sbuf", [128, C], "uint8")
+    SCRATCH["landq%d" % _r] = ("sbuf", [128, C], "float8_e4m3fn_x4")
+    SCRATCH["lands%d" % _r] = ("sbuf", [128, C], "uint8")
+    SCRATCH["glr%d" % _r] = ("sbuf", [128, 48], "uint16")
+    SCRATCH["ge%d" % _r] = ("sbuf", [128, C], "float32")
+    SCRATCH["gd%d" % _r] = ("sbuf", [128, C], "float32")
+    SCRATCH["vl%d" % _r] = ("dram", [128, 24], "uint16")
+    SCRATCH["vland%d" % _r] = ("sbuf", [128, 24], "uint16")
+for _r in range(4):
+    SCRATCH["x_%d" % _r] = ("sbuf", [128, 4 * C], "bfloat16")
+
+SEMAPHORES = ["cv", "cs", "ct", "cg", "sent", "arrl8",
+              "ld_gl", "ld_ht", "ld_u", "ld_w", "ld_v", "ld_x0", "ld_x1", "pre", "v8",
+              "st0", "st1", "stp", "stq"]
+for _r in range(3):
+    SEMAPHORES += ["arrq%d" % _r, "arrl%d" % _r, "arrg%d" % _r, "fb%d" % _r, "vla%d" % _r, "vlb%d" % _r]
+
+
+def tracker(g, T):
+    queue = {"v": g.vector, "s": g.scalar, "t": g.tensor, "g": g, "y": g.sync}
+    csem = {"v": "cv", "s": "cs", "t": "ct", "g": "cg"}
+    count = {k: 0 for k in csem}
+    know = {k: {} for k in queue}
+    clock, writer, readers = {}, {}, {}
+    total, waited = {}, {}
+
+    def merge(a, b):
+        for s, n in b.items():
+            if a.get(s, 0) < n:
+                a[s] = n
+
+    def need(e, toks):
+        todo = {}
+        for s, n in toks:
+            if know[e].get(s, 0) < n:
+                todo[s] = max(todo.get(s, 0), n)
+        for s in list(todo):
+            for s2 in list(todo):
+                if s2 != s and s in todo and clock.get((s2, todo[s2]), {}).get(s, 0) >= todo[s]:
+                    del todo[s]
+        for s, n in todo.items():
+            queue[e].wait_ge(T.sem[s], n)
+            waited[s] = max(waited.get(s, 0), n)
+            merge(know[e], clock.get((s, n), {}))
+            merge(know[e], {s: n})
+
+    def deps(e, reads, writes):
+        own = csem.get(e)
+        toks = [writer[k] for k in list(reads) + list(writes) if k in writer]
+        for k in writes:
+            toks += [t for t in readers.get(k, []) if t[0] != own]
+        return toks
+
+    def record(tok, reads, writes):
+        for k in reads:
+            readers.setdefault(k, []).append(tok)
+        for k in writes:
+            writer[k] = tok
+            readers[k] = []
+
+    def op(e, fn, reads, writes):
+        need(e, deps(e, reads, writes))
+        count[e] += 1
+        tok = (csem[e], count[e])
+        fn(queue[e]).then_inc(T.sem[csem[e]], 1)
+        total[csem[e]] = count[e]
+        clock[tok] = dict(know[e])
+        clock[tok][tok[0]] = tok[1]
+        record(tok, reads, writes)
+
+    def dma(e, sem, n, out, in_, reads, writes):
+        d = deps(e, reads, writes)
+        need(e, [t for t in d if t[0] != sem])
+        tok = (sem, 16 * n)
+        queue[e].dma_start(out, in_).then_inc(T.sem[sem], 16)
+        total[sem] = 16 * n
+        c = clock.setdefault(tok, dict(know[e]))
+        for s in list(c):
+            c[s] = max(c[s], know[e].get(s, 0))
+        record(tok, reads, writes)
+
+    def arrives(sem, n, keys):
+        total[sem] = n
+        for k in keys:
+            writer[k] = (sem, n)
+
+    def before(e, reads):
+        need(e, [writer[k] for k in reads])
+
+    def finish():
+        for s, n in total.items():
+            if waited.get(s, 0) < n:
+                g.wait_ge(T.sem[s], n)
+    return op, dma, arrives, before, finish, total
+
+
+def rank_program(g, core, T, topo):
+    rank = T.rank_of(core)
+    if rank is None:
+        return
+    op, dma, arrives, before, finish, total = tracker(g, T)
+    partner = [T.cores[rank ^ s] for s in STEP]
+
+    def send(dst, out, in_, sem):
+        e = topo.engines(core, dst)[:8]
+        rid, pid = topo.addr(dst)[:2]
+        g.remote_dma(out, in_, T.sem[sem], T.sem.sent, pid, rid, sum(1 << k for k in e))
+        total["sent"] = total.get("sent", 0) + len(e)
+        return len(e)
+
+    ne = [len(topo.engines(core, p)[:8]) for p in partner]
+    for r in range(3):
+        arrives("arrq%d" % r, 2 * ne[r], ["landq%d" % r])
+        arrives("arrl%d" % r, ne[r], ["vland%d" % r])
+        arrives("arrg%d" % r, ne[r], ["glr%d" % r])
+    arrives("arrl8", ne[2], ["vland8"])
+
+    def half(name, h):
+        return ["%s.%d.%d" % (name, b, h) for b in range(4)]
+
+    def whole(name):
+        return half(name, 0) + half(name, 1)
+
+    dma("y", "ld_gl", 1, T.gli[:], T.gl[:], [], ["gli"])
+    dma("s", "ld_u", 1, T.ut[:], T.u[:], [], ["ut"])
+    dma("y", "ld_x0", 1, T.x_0[:, 0:4 * H], T.x[:, 0:4 * H], [], half("x_0", 0))
+    dma("s", "ld_x1", 1, T.x_0[:, 4 * H:], T.x[:, 4 * H:], [], half("x_0", 1))
+    dma("y", "ld_ht", 1, T.hti[:], T.ht[:], [], ["hti"])
+    dma("y", "ld_w", 2, T.wq[:].bitcast(dt.uint8), T.wc[:], [], ["wq"])
+    dma("y", "ld_w", 2, T.wsp[:], T.ws[:], [], ["wsp"])
+    dma("y", "ld_v", 1, T.vt[:], T.v[:], [], ["vt"])
+
+    op("g", lambda q: q.iota(T.upi[:], [[16, 8]], 0, 0), [], ["upi"])
+    op("g", lambda q: q.iota(T.ip[:], [[0, 1]], 0, 1), [], ["ip"])
+    op("g", lambda q: q.iota(T.k8[:], [[-16, 8]], 128, 1), [], ["k8"])
+    op("g", lambda q: q.iota(T.row[:], [[0, 3], [1, 16]], 0, 0, allow_small_or_imprecise_dtypes=True), [], ["row"])
+    op("g", lambda q: q.iota(T.c16[:], [[16, 24]], 0, 0, allow_small_or_imprecise_dtypes=True), [], ["c16"])
+    op("g", lambda q: q.iota(T.ident[:], [[1, 768]], 0, 0, allow_small_or_imprecise_dtypes=True), [], ["ident"])
+    V = lambda fn, r, w: op("v", fn, r, w)
+    S = lambda fn, r, w: op("s", fn, r, w)
+    V(lambda q: q.memset(T.e0[:], 1.0), [], ["e0"])
+    V(lambda q: q.tensor_copy(T.up[:], T.upi[:]), ["upi"], ["up"])
+    V(lambda q: q.tensor_scalar(T.ia[:, 0:1], T.ip[:], 15, None, ALU.bitwise_and), ["ip"], ["ia0"])
+    V(lambda q: q.tensor_scalar(T.ia[:, 1:2], T.ip[:], 7, None, ALU.bitwise_and), ["ip"], ["ia1"])
+    V(lambda q: q.tensor_scalar(T.ia[:, 2:3], T.ip[:], 3, None, ALU.arith_shift_right), ["ip"], ["ia2"])
+    V(lambda q: q.tensor_scalar(T.kk[:], T.k8[:], 4, 7, ALU.arith_shift_right, ALU.bitwise_and), ["k8"], ["kk"])
+    V(lambda q: q.tensor_copy(T.fa[:, 0:1], T.ia[:, 0:1]), ["ia0"], ["fa0"])
+    V(lambda q: q.tensor_scalar(T.fa[:, 1:2], T.ia[:, 1:2], 48.0, None, ALU.mult), ["ia1"], ["fa1"])
+    V(lambda q: q.tensor_copy(T.fa[:, 2:3], T.ia[:, 2:3]), ["ia2"], ["fa2"])
+    V(lambda q: q.tensor_scalar(T.kf[:], T.kk[:], 384.0, 192.0, ALU.mult, ALU.add), ["kk"], ["kf"])
+    V(lambda q: q.tensor_scalar(T.keep[:], T.row[:], 0.0, None, ALU.not_equal), ["row"], ["keep"])
+    V(lambda q: q.tensor_scalar(T.mask[:], T.row[:], T.fa[:, 0:1], None, ALU.is_equal), ["row", "fa0"], ["mask"])
+    V(lambda q: q.tensor_scalar(T.jl[:], T.c16[:], T.fa[:, 0:1], None, ALU.add), ["c16", "fa0"], ["jl"])
+    V(lambda q: q.tensor_scalar(T.jw[:, 0:3], T.c16[:, 0:3], T.fa[:, 1:2], T.fa[:, 2:3], ALU.add, ALU.add),
+      ["c16", "fa1", "fa2"], ["jw"])
+    V(lambda q: q.tensor_scalar(T.ov0[:, 0:3], T.jw[:, 0:3], T.kf[:, 0:1], -192.0, ALU.add, ALU.add), ["jw", "kf"], ["ov0"])
+    V(lambda q: q.tensor_copy(T.gl16[:], T.gli[:]), ["gli"], ["gl16"])
+
+    def send_table(r):
+        before("g", ["gl16"])
+        send(partner[r], T["glr%d" % r][:], T.gl16[:], "arrg%d" % r)
+    send_table(0)
+    op("g", lambda q: q.affine_select(T.et[:], T.e0[:], [[-1, 4], [8, 128], [1, 4]], ALU.is_equal, 0.0, 0, -8), ["e0"], ["et"])
+    send_table(1)
+    send_table(2)
+
+    V(lambda q: q.quantize_mx(T.uq[:], T.us[:], T.ut[:]), ["ut"], ["uq"])
+    V(lambda q: q.tensor_copy(T.uqr[:].bitcast(dt.uint32), T.uq[:].bitcast(dt.uint32).indirect(T.up[:])), ["uq", "up"], ["uqr"])
+    V(lambda q: q.tensor_copy(T.usr[:], T.us[:].indirect(T.up[:])), ["uq", "up"], ["usr"])
+    V(lambda q: q.tensor_copy(T.ht16[:], T.hti[:]), ["hti"], ["ht16"])
+    for t in range(4):
+        V(lambda q, t=t: q.tensor_scalar(T.ht4[:, 24 * t:24 * t + 24], T.hti[:], 4.0, float(t), ALU.mult, ALU.add),
+          ["hti"], ["ht4.%d" % t])
+    for k in range(3):
+        dma("y", "pre", 4, T["vl%d" % k][:], T.jl[:], ["jl"], ["vl%d.%d" % (k, b) for b in range(8)])
+    dma("y", "pre", 4, T.vl8[:], T.jl[:], ["jl"], ["vl8"])
+
+    def quantise_state(r, h):
+        X = T["x_%d" % r]
+        V(lambda q: q.quantize_mx(T.xq[:, H * h:H * h + H], T.xs[:, H * h:H * h + H], X[:, 4 * H * h:4 * H * h + 4 * H]),
+          half("x_%d" % r, h), ["xq.%d" % h])
+
+    def signs(h):
+        op("t", lambda q: q.matmul_mx(T.psb[:, 512 * h:512 * h + H], T.uqr[:], T.usr[:], T.xq[:, H * h:H * h + H],
+                                      T.xs[:, H * h:H * h + H], True, True), ["uqr", "usr", "xq.%d" % h], ["psb.%d" % h])
+        V(lambda q: q.tensor_scalar(T.bits[:, H * h:H * h + H], T.psb[:, 512 * h:512 * h + H], 0.0, None, ALU.is_gt),
+          ["psb.%d" % h], ["bits.%d" % h])
+
+    def lay_table(r):
+        S(lambda q: q.activation(T.glf[:], T.ident[:].indirect(T["glr%d" % r][:]), COPY), ["ident", "glr%d" % r], ["glf"])
+
+    def split_table(r):
+        V(lambda q: q.tensor_scalar(T["ge%d" % r][:], T.glf[:, 0:768:2], -192.0, None, ALU.add), ["glf"], ["ge%d" % r])
+        V(lambda q: q.tensor_tensor(T["gd%d" % r][:], T.glf[:, 1:768:2], T.glf[:, 0:768:2], ALU.subtract), ["glf"], ["gd%d" % r])
+
+    for h in range(NH):
+        quantise_state(0, h)
+        signs(h)
+    lay_table(0)
+    split_table(0)
+
+    for r in range(3):
+        last = r == 2
+        xn, X, Y = "x_%d" % r, T["x_%d" % r], T["x_%d" % (r + 1)]
+        lq, ls = T["lq%d" % r], T["ls%d" % r]
+
+        def lay(e, t):
+            fn = {"v": lambda q: q.tensor_copy(T.lx[:, t:4 * C:4], X[:].indirect(T.ht4[:, 24 * t:24 * t + 24])),
+                  "s": lambda q: q.activation(T.lx[:, t:4 * C:4], X[:].indirect(T.ht4[:, 24 * t:24 * t + 24]), COPY)}[e]
+            op(e, fn, whole(xn) + ["ht4.%d" % t], ["lx.%d" % t])
+        lay("s", 0)
+        lay("s", 1)
+        V(lambda q: q.tensor_tensor(T.t1[:], T.bits[:].indirect(T.ht16[:]), T["gd%d" % r][:], ALU.mult),
+          ["bits.0", "bits.1", "ht16", "gd%d" % r], ["t1"])
+        V(lambda q: q.tensor_tensor(T.ft[:, 0:C], T.t1[:], T["ge%d" % r][:], ALU.add), ["t1", "ge%d" % r], ["ft.0"])
+        for k in range(1, 8):
+            a, b = 16 * k, C * k
+            dma("y", "fb%d" % r, 14, T.ft[a:128, b:b + C], T.ft[0:128 - a, 0:C], ["ft.0"], ["ft.%d.a" % k])
+            dma("s", "fb%d" % r, 14, T.ft[0:a, b:b + C], T.ft[128 - a:128, 0:C], ["ft.0"], ["ft.%d.b" % k])
+        lay("v", 2)
+        lay("v", 3)
+        V(lambda q: q.quantize_mx(lq[:], ls[:], T.lx[:]), ["lx.%d" % t for t in range(4)], ["lq%d" % r])
+        before("g", ["lq%d" % r])
+        send(partner[r], T["landq%d" % r][:].bitcast(dt.uint8), lq[:].bitcast(dt.uint8), "arrq%d" % r)
+        send(partner[r], T["lands%d" % r][:], ls[:], "arrq%d" % r)
+        S(lambda q: q.activation(T.x64[:], X[:], COPY, scale=64.0), whole(xn), whole("x64"))
+        if not last:
+            lay_table(r + 1)
+        if r == 0:
+            V(lambda q: q.quantize_mx(T.eq[:], T.es[:], T.et[:]), ["et"], ["eq"])
+            V(lambda q: q.quantize_mx(T.vq[:], T.vs[:], T.vt[:]), ["vt"], ["vq"])
+        tables = ["ft.0"] + ["ft.%d.%s" % (k, c) for k in range(1, 8) for c in "ab"]
+
+        def step(s):
+            o, ok = (T.ov0, "ov0") if s == 0 else (T.ov, "ov")
+            V(lambda q: q.tensor_tensor(T.w1[:], T.ft[:].indirect(o[:, 0:3]), T.mask[:], ALU.mult), tables + [ok, "mask"], ["w1"])
+            V(lambda q: q.tensor_tensor_scan(T.w2[:], T.keep[:], T.w1[:], 0.0, ALU.mult, ALU.add), ["keep", "w1"], ["w2"])
+            top = 7 if last else 6
+
+            def offsets():
+                V(lambda q: q.tensor_scalar(T.ov[:, 0:3], T.w2[:, 15:48:16], T.kf[:, s + 1:s + 2], None, ALU.add),
+                  ["w2", "kf"], ["ov"])
+
+            def places():
+                V(lambda q: q.tensor_scalar(T.vo[:, 4 * s:4 * s + 3], T.w2[:, 15:48:16], 192.0, None, ALU.add), ["w2"], ["vo.%d" % s])
+                if s < 7:
+                    sem, n = ("vla%d" % r, 6) if s < 6 else ("vlb%d" % r, 1)
+                    dma("y", sem, n, T["vl%d" % r][16 * s + 16:16 * s + 32, :], T.vo[:, 4 * s:4 * s + 3], ["vo.%d" % s],
+                        ["vl%d.%d" % (r, s + 1)])
+                else:
+                    dma("y", "v8", 1, T.vl8[0:16, :], T.vo[:, 28:31], ["vo.7"], ["vl8"])
+            if s >= 6:
+                places()
+                if s < top:
+                    offsets()
+            else:
+                offsets()
+                places()
+        for s in range(7):
+            step(s)
+        before("g", ["vl%d.%d" % (r, b) for b in range(8)])
+        send(partner[r], T["vland%d" % r][:], T["vl%d" % r][:], "arrl%d" % r)
+        if last:
+            step(7)
+            before("g", ["vl8"])
+            send(partner[r], T.vland8[:], T.vl8[:], "arrl8")
+        else:
+            split_table(r + 1)
+        for b in range(4):
+            op("t", lambda q, b=b: q.matmul_mx(T.psa[:, 512 * b:512 * b + C], T.eq[:, 128 * b:128 * b + 128], T.es[:, 128 * b:128 * b + 128],
+                                               T["landq%d" % r][:], T["lands%d" % r][:], True, True), ["eq", "landq%d" % r], ["psa.%d" % b])
+            V(lambda q, b=b: q.tensor_tensor(T.m[:, C * b:C * b + C], T.psa[:, 512 * b:512 * b + C], X[:, b:4 * C:4], ALU.max),
+              ["psa.%d" % b] + whole(xn), ["m.%d" % b])
+        for h in range(NH):
+            off = T["vland%d" % r][:, 12 * h:12 * h + 12]
+            for b in range(4):
+                e = "v" if b < 2 else "s"
+                win, out = T.m[:, C * b:C * b + C].indirect(off), T.z[:, 4 * H * h + b:4 * H * h + 4 * H:4]
+                fn = {"v": lambda q: q.tensor_copy(out, win), "s": lambda q: q.activation(out, win, COPY)}[e]
+                op(e, fn, ["m.%d" % b, "vland%d" % r], ["z.%d.%d" % (b, h)])
+        for h in range(NH):
+            V(lambda q: q.quantize_mx(T.zq[:, H * h:H * h + H], T.zs[:, H * h:H * h + H], T.z[:, 4 * H * h:4 * H * h + 4 * H]),
+              half("z", h), ["zq.%d" % h])
+            ps, pn = (T.psb, "psb") if h == 0 else (T.psa, "psa")
+            for b in range(4):
+                op("t", lambda q: q.matmul_mx(ps[:, 512 * b:512 * b + H], T.wq[:, 128 * b:128 * b + 128], T.wsp[:, 128 * b:128 * b + 128],
+                                              T.zq[:, H * h:H * h + H], T.zs[:, H * h:H * h + H], True, True),
+                   ["wq", "wsp", "zq.%d" % h], ["%s.%d" % (pn, b)])
+        for h in range(NH):
+            ps, pn = (T.psb, "psb") if h == 0 else (T.psa, "psa")
+            for b in range(4):
+                u = T.uu[:, (4 * h + b) * H:(4 * h + b + 1) * H]
+                s0 = slice(4 * H * h + b, 4 * H * h + 4 * H, 4)
+                V(lambda q: q.tensor_tensor(u, ps[:, 512 * b:512 * b + H], T.x64[:, s0], ALU.add),
+                  ["%s.%d" % (pn, b), "x64.%d.%d" % (b, h)], ["uu.%d.%d" % (b, h)])
+                S(lambda q: q.activation(Y[:, s0], u, COPY, scale=0.015625), ["uu.%d.%d" % (b, h)], ["x_%d.%d.%d" % (r + 1, b, h)])
+        for h in range(NH):
+            quantise_state(r + 1, h)
+            if not last:
+                signs(h)
+    for h in range(NH):
+        c0, c1 = H * h, H * h + H
+        op("t", lambda q: q.matmul_mx(T.psb[:, 512 * h:512 * h + H], T.vq[:], T.vs[:], T.xq[:, c0:c1], T.xs[:, c0:c1], True, True),
+           ["vq", "xq.%d" % h], ["psb.%d" % h])
+        sem = "st%d" % h
+        dma("y", sem, 6, T.oc[:, 4 * c0:4 * c1], T.xq[:, c0:c1].bitcast(dt.uint8), ["xq.%d" % h], [])
+        for k in range(4):
+            dma("s" if k % 2 else "y", sem, 6, T.osc[4 * k:4 * k + 4, c0:c1], T.xs[32 * k:32 * k + 4, c0:c1], ["xq.%d" % h], [])
+        V(lambda q: q.tensor_copy(T.ysb[:, c0:c1], T.psb[:, 512 * h:512 * h + H]), ["psb.%d" % h], ["ysb.%d" % h])
+        dma("y", sem, 6, T.y[:, c0:c1], T.ysb[:, c0:c1], ["ysb.%d" % h], [])
+    S(lambda q: q.activation(T.plb[:], T.ident[:, 0:C].indirect(T.vland2[:]), COPY), ["ident", "vland2"], ["plb"])
+    dma("s", "stp", 1, T.pl[0:7, :], T.plb[16:128:16, :], ["plb"], [])
+    S(lambda q: q.activation(T.plc[:], T.ident[:, 0:C].indirect(T.vland8[:]), COPY), ["ident", "vland8"], ["plc"])
+    dma("s", "stq", 1, T.pl[7:8, :], T.plc[0:1, :], ["plc"], [])
+    finish()

@@ -1,10 +1,9 @@
-import numpy as np
 from concourse.mybir import dt, AluOpType, ActivationFunctionType
 
 C = 384
-H = 192
-NH = 2
+PIECES = [(0, 192), (192, 384)]
 STEP = [1, 2, 4]
+FIRST = 2
 ALU = AluOpType
 COPY = ActivationFunctionType.Copy
 
@@ -14,27 +13,24 @@ SCRATCH = {
     "uqr": ("sbuf", [128, 128], "float8_e4m3fn_x4"), "usr": ("sbuf", [128, 128], "uint8"),
     "vq": ("sbuf", [128, 128], "float8_e4m3fn_x4"), "vs": ("sbuf", [128, 128], "uint8"),
     "wq": ("sbuf", [128, 512], "float8_e4m3fn_x4"), "wsp": ("sbuf", [128, 512], "uint8"),
-    "e0": ("sbuf", [128, 2048], "bfloat16"), "et": ("sbuf", [128, 2048], "bfloat16"),
+    "e0": ("sbuf", [128, 516], "bfloat16"), "et": ("sbuf", [128, 516], "bfloat16"),
     "eq": ("sbuf", [128, 512], "float8_e4m3fn_x4"), "es": ("sbuf", [128, 512], "uint8"),
     "x64": ("sbuf", [128, 4 * C], "bfloat16"), "lx": ("sbuf", [128, 4 * C], "bfloat16"),
     "m": ("sbuf", [128, 4 * C], "bfloat16"), "z": ("sbuf", [128, 4 * C], "bfloat16"),
     "zq": ("sbuf", [128, C], "float8_e4m3fn_x4"), "zs": ("sbuf", [128, C], "uint8"),
     "xq": ("sbuf", [128, C], "float8_e4m3fn_x4"), "xs": ("sbuf", [128, C], "uint8"),
-    "uu": ("sbuf", [128, 8 * H], "float32"),
-    "gli": ("sbuf", [128, 48], "int32"), "gl16": ("sbuf", [128, 48], "uint16"),
+    "gli": ("sbuf", [128, 48], "int32"), "glb": ("sbuf", [128, 48], "int32"),
+    "gt": ("sbuf", [128, 48], "float32"), "gu": ("sbuf", [128, 48], "float32"), "gl16": ("sbuf", [128, 48], "uint16"),
     "hti": ("sbuf", [128, 24], "int32"), "ht16": ("sbuf", [128, 24], "uint16"), "ht4": ("sbuf", [128, 96], "uint16"),
-    "glf": ("sbuf", [128, 768], "float32"),
     "bits": ("sbuf", [128, C], "bfloat16"), "t1": ("sbuf", [128, C], "float32"),
-    "ft": ("sbuf", [128, 8 * C], "bfloat16"),
-    "w1": ("sbuf", [128, 48], "float32"), "w2": ("sbuf", [128, 48], "float32"),
-    "ov0": ("sbuf", [128, 4], "uint16"), "ov": ("sbuf", [128, 4], "uint16"), "vo": ("sbuf", [128, 32], "uint16"),
-    "ident": ("sbuf", [128, 768], "float32"), "ip": ("sbuf", [128, 1], "int32"), "k8": ("sbuf", [128, 8], "int32"),
-    "row": ("sbuf", [128, 48], "float32"), "c16": ("sbuf", [128, 24], "float32"), "upi": ("sbuf", [128, 8], "int32"),
-    "up": ("sbuf", [128, 8], "uint16"), "ia": ("sbuf", [128, 4], "int32"), "fa": ("sbuf", [128, 4], "float32"),
-    "kk": ("sbuf", [128, 8], "int32"), "kf": ("sbuf", [128, 8], "float32"), "jl": ("sbuf", [128, 24], "uint16"),
-    "jw": ("sbuf", [128, 4], "float32"), "mask": ("sbuf", [128, 48], "float32"), "keep": ("sbuf", [128, 48], "float32"),
-    "ysb": ("sbuf", [128, C], "float32"), "plb": ("sbuf", [128, C], "float32"), "plc": ("sbuf", [128, C], "float32"),
-    "vl8": ("dram", [128, 24], "uint16"), "vland8": ("sbuf", [128, 24], "uint16"),
+    "ft": ("sbuf", [128, C], "bfloat16"), "tab": ("sbuf", [128, 2 * C], "bfloat16"),
+    "w1": ("sbuf", [128, 64], "bfloat16"), "w2": ("sbuf", [128, 7 * 64], "bfloat16"),
+    "coll": ("sbuf", [128, 32], "bfloat16"), "lt": ("sbuf", [128, 32], "bfloat16"),
+    "ov0": ("sbuf", [128, 4], "uint16"), "ov": ("sbuf", [128, 4], "uint16"),
+    "ident": ("sbuf", [128, 768], "float32"), "ip": ("sbuf", [128, 1], "int32"),
+    "kcol": ("sbuf", [128, 4], "float32"), "upi": ("sbuf", [128, 8], "int32"),
+    "up": ("sbuf", [128, 8], "uint16"), "ia": ("sbuf", [128, 4], "int32"), "fa": ("sbuf", [128, 8], "float32"),
+    "ysb": ("sbuf", [128, C], "float32"), "plb": ("sbuf", [128, C], "float32"), "fland": ("sbuf", [128, C], "bfloat16"),
     "psa": ("psum", [128, 2048], "float32"), "psb": ("psum", [128, 2048], "float32"),
 }
 for _r in range(3):
@@ -43,18 +39,17 @@ for _r in range(3):
     SCRATCH["landq%d" % _r] = ("sbuf", [128, C], "float8_e4m3fn_x4")
     SCRATCH["lands%d" % _r] = ("sbuf", [128, C], "uint8")
     SCRATCH["glr%d" % _r] = ("sbuf", [128, 48], "uint16")
-    SCRATCH["ge%d" % _r] = ("sbuf", [128, C], "float32")
-    SCRATCH["gd%d" % _r] = ("sbuf", [128, C], "float32")
-    SCRATCH["vl%d" % _r] = ("dram", [128, 24], "uint16")
+    SCRATCH["glf%d" % _r] = ("sbuf", [128, 2 * C], "float32")
+    SCRATCH["vl%d" % _r] = ("sbuf", [128, 24], "uint16")
     SCRATCH["vland%d" % _r] = ("sbuf", [128, 24], "uint16")
 for _r in range(4):
     SCRATCH["x_%d" % _r] = ("sbuf", [128, 4 * C], "bfloat16")
 
-SEMAPHORES = ["cv", "cs", "ct", "cg", "sent", "arrl8",
-              "ld_gl", "ld_ht", "ld_u", "ld_w", "ld_v", "ld_x0", "ld_x1", "pre", "v8",
-              "st0", "st1", "stp", "stq"]
+SEMAPHORES = ["cv", "cs", "ct", "cg", "sent", "arrf",
+              "ld_gl", "ld_ht", "ld_u", "ld_w", "ld_v", "ld_x0", "ld_x1",
+              "st0", "st1", "st2", "stp"]
 for _r in range(3):
-    SEMAPHORES += ["arrq%d" % _r, "arrl%d" % _r, "arrg%d" % _r, "fb%d" % _r, "vla%d" % _r, "vlb%d" % _r]
+    SEMAPHORES += ["arrq%d" % _r, "arrl%d" % _r, "arrg%d" % _r, "fa%d" % _r, "fb%d" % _r]
 
 
 def tracker(g, T):
@@ -141,216 +136,248 @@ def rank_program(g, core, T, topo):
         return
     op, dma, arrives, before, finish, total = tracker(g, T)
     partner = [T.cores[rank ^ s] for s in STEP]
+    NP = len(PIECES)
 
     def send(dst, out, in_, sem):
         e = topo.engines(core, dst)[:8]
         rid, pid = topo.addr(dst)[:2]
         g.remote_dma(out, in_, T.sem[sem], T.sem.sent, pid, rid, sum(1 << k for k in e))
         total["sent"] = total.get("sent", 0) + len(e)
-        return len(e)
 
     ne = [len(topo.engines(core, p)[:8]) for p in partner]
     for r in range(3):
         arrives("arrq%d" % r, 2 * ne[r], ["landq%d" % r])
         arrives("arrl%d" % r, ne[r], ["vland%d" % r])
         arrives("arrg%d" % r, ne[r], ["glr%d" % r])
-    arrives("arrl8", ne[2], ["vland8"])
+    arrives("arrf", ne[2], ["fland"])
 
-    def half(name, h):
+    def piece(name, h):
         return ["%s.%d.%d" % (name, b, h) for b in range(4)]
 
     def whole(name):
-        return half(name, 0) + half(name, 1)
+        return [k for h in range(NP) for k in piece(name, h)]
 
-    dma("y", "ld_gl", 1, T.gli[:], T.gl[:], [], ["gli"])
-    dma("s", "ld_u", 1, T.ut[:], T.u[:], [], ["ut"])
-    dma("y", "ld_x0", 1, T.x_0[:, 0:4 * H], T.x[:, 0:4 * H], [], half("x_0", 0))
-    dma("s", "ld_x1", 1, T.x_0[:, 4 * H:], T.x[:, 4 * H:], [], half("x_0", 1))
-    dma("y", "ld_ht", 1, T.hti[:], T.ht[:], [], ["hti"])
-    dma("y", "ld_w", 2, T.wq[:].bitcast(dt.uint8), T.wc[:], [], ["wq"])
-    dma("y", "ld_w", 2, T.wsp[:], T.ws[:], [], ["wsp"])
-    dma("y", "ld_v", 1, T.vt[:], T.v[:], [], ["vt"])
-
-    op("g", lambda q: q.iota(T.upi[:], [[16, 8]], 0, 0), [], ["upi"])
-    op("g", lambda q: q.iota(T.ip[:], [[0, 1]], 0, 1), [], ["ip"])
-    op("g", lambda q: q.iota(T.k8[:], [[-16, 8]], 128, 1), [], ["k8"])
-    op("g", lambda q: q.iota(T.row[:], [[0, 3], [1, 16]], 0, 0, allow_small_or_imprecise_dtypes=True), [], ["row"])
-    op("g", lambda q: q.iota(T.c16[:], [[16, 24]], 0, 0, allow_small_or_imprecise_dtypes=True), [], ["c16"])
-    op("g", lambda q: q.iota(T.ident[:], [[1, 768]], 0, 0, allow_small_or_imprecise_dtypes=True), [], ["ident"])
     V = lambda fn, r, w: op("v", fn, r, w)
     S = lambda fn, r, w: op("s", fn, r, w)
+
+    def copy(e, out, in_, r, w):
+        op(e, {"v": lambda q: q.tensor_copy(out, in_), "s": lambda q: q.activation(out, in_, COPY)}[e], r, w)
+
+    cut = 4 * PIECES[0][1]
+    dma("y", "ld_gl", 3, T.gli[:], T.gl[:], [], ["gli"])
+    dma("s", "ld_gl", 3, T.glb[1:128, :], T.gl[0:127, :], [], ["glb"])
+    dma("s", "ld_gl", 3, T.glb[0:1, :], T.gl[0:1, :], [], ["glb0"])
+    dma("y", "ld_u", 1, T.ut[:], T.u[:], [], ["ut"])
+    dma("s", "ld_ht", 1, T.hti[:], T.ht[:], [], ["hti"])
+    dma("y", "ld_x0", 1, T.x_0[:, 0:cut], T.x[:, 0:cut], [], piece("x_0", 0))
+    dma("s", "ld_x1", 1, T.x_0[:, cut:], T.x[:, cut:], [], [k for h in range(1, NP) for k in piece("x_0", h)])
+
+    op("g", lambda q: q.iota(T.ip[:], [[0, 1]], 0, 1), [], ["ip"])
+    op("g", lambda q: q.iota(T.upi[:], [[16, 8]], 0, 0), [], ["upi"])
+    op("g", lambda q: q.iota(T.kcol[:], [[2, 2], [256, 2]], 0, 0, allow_small_or_imprecise_dtypes=True), [], ["kcol"])
+    op("g", lambda q: q.iota(T.ident[:], [[1, 768]], 1 - C, 0, allow_small_or_imprecise_dtypes=True), [], ["ident"])
     V(lambda q: q.memset(T.e0[:], 1.0), [], ["e0"])
-    V(lambda q: q.tensor_copy(T.up[:], T.upi[:]), ["upi"], ["up"])
+    V(lambda q: q.tensor_scalar(T.ia[:, 3:4], T.ip[:], 1, None, ALU.bitwise_and), ["ip"], ["ia3"])
     V(lambda q: q.tensor_scalar(T.ia[:, 0:1], T.ip[:], 15, None, ALU.bitwise_and), ["ip"], ["ia0"])
-    V(lambda q: q.tensor_scalar(T.ia[:, 1:2], T.ip[:], 7, None, ALU.bitwise_and), ["ip"], ["ia1"])
-    V(lambda q: q.tensor_scalar(T.ia[:, 2:3], T.ip[:], 3, None, ALU.arith_shift_right), ["ip"], ["ia2"])
-    V(lambda q: q.tensor_scalar(T.kk[:], T.k8[:], 4, 7, ALU.arith_shift_right, ALU.bitwise_and), ["k8"], ["kk"])
-    V(lambda q: q.tensor_copy(T.fa[:, 0:1], T.ia[:, 0:1]), ["ia0"], ["fa0"])
-    V(lambda q: q.tensor_scalar(T.fa[:, 1:2], T.ia[:, 1:2], 48.0, None, ALU.mult), ["ia1"], ["fa1"])
-    V(lambda q: q.tensor_copy(T.fa[:, 2:3], T.ia[:, 2:3]), ["ia2"], ["fa2"])
-    V(lambda q: q.tensor_scalar(T.kf[:], T.kk[:], 384.0, 192.0, ALU.mult, ALU.add), ["kk"], ["kf"])
-    V(lambda q: q.tensor_scalar(T.keep[:], T.row[:], 0.0, None, ALU.not_equal), ["row"], ["keep"])
-    V(lambda q: q.tensor_scalar(T.mask[:], T.row[:], T.fa[:, 0:1], None, ALU.is_equal), ["row", "fa0"], ["mask"])
-    V(lambda q: q.tensor_scalar(T.jl[:], T.c16[:], T.fa[:, 0:1], None, ALU.add), ["c16", "fa0"], ["jl"])
-    V(lambda q: q.tensor_scalar(T.jw[:, 0:3], T.c16[:, 0:3], T.fa[:, 1:2], T.fa[:, 2:3], ALU.add, ALU.add),
-      ["c16", "fa1", "fa2"], ["jw"])
-    V(lambda q: q.tensor_scalar(T.ov0[:, 0:3], T.jw[:, 0:3], T.kf[:, 0:1], -192.0, ALU.add, ALU.add), ["jw", "kf"], ["ov0"])
-    V(lambda q: q.tensor_copy(T.gl16[:], T.gli[:]), ["gli"], ["gl16"])
+    V(lambda q: q.tensor_scalar(T.ia[:, 1:2], T.ip[:], 5, None, ALU.arith_shift_right), ["ip"], ["ia1"])
+    V(lambda q: q.tensor_scalar(T.ia[:, 2:3], T.ip[:], 4, 1, ALU.arith_shift_right, ALU.bitwise_and), ["ip"], ["ia2"])
+    V(lambda q: q.tensor_scalar(T.fa[:, 3:4], T.ia[:, 3:4], -1.0, None, ALU.mult), ["ia3"], ["fa3"])
+    V(lambda q: q.tensor_scalar(T.fa[:, 4:5], T.ia[:, 3:4], 192.0, 191.0, ALU.mult, ALU.add), ["ia3"], ["fa4"])
+    V(lambda q: q.tensor_scalar(T.fa[:, 0:1], T.ia[:, 0:1], 16.0, None, ALU.mult), ["ia0"], ["fa0"])
+    V(lambda q: q.tensor_copy(T.up[:], T.upi[:]), ["upi"], ["up"])
+    V(lambda q: q.tensor_scalar(T.fa[:, 1:2], T.ia[:, 1:2], 4.0, T.fa[:, 0:1], ALU.mult, ALU.add), ["ia1", "fa0"], ["fa1"])
+    V(lambda q: q.tensor_scalar(T.fa[:, 2:3], T.ia[:, 2:3], T.fa[:, 1:2], None, ALU.add), ["ia2", "fa1"], ["fa2"])
+    V(lambda q: q.tensor_scalar(T.ov0[:], T.kcol[:], T.fa[:, 2:3], float(C - 1), ALU.add, ALU.min), ["kcol", "fa2"], ["ov0"])
+
+    V(lambda q: q.tensor_scalar(T.gt[:], T.glb[:], T.fa[:, 3:4], T.fa[:, 4:5], ALU.mult, ALU.add), ["glb", "glb0", "fa3", "fa4"], ["gt"])
+    V(lambda q: q.tensor_tensor(T.gu[:], T.gt[:], T.gli[:], ALU.add), ["gt", "gli"], ["gu"])
+    V(lambda q: q.tensor_copy(T.gl16[:], T.gu[:]), ["gu"], ["gl16"])
 
     def send_table(r):
         before("g", ["gl16"])
         send(partner[r], T["glr%d" % r][:], T.gl16[:], "arrg%d" % r)
     send_table(0)
-    op("g", lambda q: q.affine_select(T.et[:], T.e0[:], [[-1, 4], [8, 128], [1, 4]], ALU.is_equal, 0.0, 0, -8), ["e0"], ["et"])
+    op("g", lambda q: q.affine_select(T.et[:], T.e0[:], [[1, 516]], ALU.is_equal, 0.0, -3, -4), ["e0"], ["et"])
+    op("g", lambda q: q.iota(T.tab[:], [[0, 2], [1, C]], -192, 0, allow_small_or_imprecise_dtypes=True), [],
+       ["tab.%d" % s for s in range(7)])
     send_table(1)
     send_table(2)
 
     V(lambda q: q.quantize_mx(T.uq[:], T.us[:], T.ut[:]), ["ut"], ["uq"])
     V(lambda q: q.tensor_copy(T.uqr[:].bitcast(dt.uint32), T.uq[:].bitcast(dt.uint32).indirect(T.up[:])), ["uq", "up"], ["uqr"])
-    V(lambda q: q.tensor_copy(T.usr[:], T.us[:].indirect(T.up[:])), ["uq", "up"], ["usr"])
-    V(lambda q: q.tensor_copy(T.ht16[:], T.hti[:]), ["hti"], ["ht16"])
+    copy("s", T.usr[:], T.us[:].indirect(T.up[:]), ["uq", "up"], ["usr"])
     for t in range(4):
-        V(lambda q, t=t: q.tensor_scalar(T.ht4[:, 24 * t:24 * t + 24], T.hti[:], 4.0, float(t), ALU.mult, ALU.add),
-          ["hti"], ["ht4.%d" % t])
-    for k in range(3):
-        dma("y", "pre", 4, T["vl%d" % k][:], T.jl[:], ["jl"], ["vl%d.%d" % (k, b) for b in range(8)])
-    dma("y", "pre", 4, T.vl8[:], T.jl[:], ["jl"], ["vl8"])
+        V(lambda q: q.tensor_scalar(T.ht4[:, 24 * t:24 * t + 24], T.hti[:], 4.0, float(t), ALU.mult, ALU.add), ["hti"], ["ht4.%d" % t])
+    V(lambda q: q.tensor_copy(T.ht16[:], T.hti[:]), ["hti"], ["ht16"])
+    dma("y", "ld_w", 2, T.wq[:].bitcast(dt.uint8), T.wc[:], [], ["wq"])
+    dma("y", "ld_w", 2, T.wsp[:], T.ws[:], [], ["wsp"])
+    dma("y", "ld_v", 1, T.vt[:], T.v[:], [], ["vt"])
+
+    def bank(h):
+        return (T.psb, "psb") if h % 2 == 0 else (T.psa, "psa")
 
     def quantise_state(r, h):
-        X = T["x_%d" % r]
-        V(lambda q: q.quantize_mx(T.xq[:, H * h:H * h + H], T.xs[:, H * h:H * h + H], X[:, 4 * H * h:4 * H * h + 4 * H]),
-          half("x_%d" % r, h), ["xq.%d" % h])
+        a, b = PIECES[h]
+        V(lambda q: q.quantize_mx(T.xq[:, a:b], T.xs[:, a:b], T["x_%d" % r][:, 4 * a:4 * b]), piece("x_%d" % r, h), ["xq.%d" % h])
+
+    def score(h, wq, ws, keys):
+        a, b = PIECES[h]
+        ps, pn = bank(h)
+        op("t", lambda q: q.matmul_mx(ps[:, 0:b - a], wq[:], ws[:], T.xq[:, a:b], T.xs[:, a:b], True, True),
+           keys + ["xq.%d" % h], [pn + ".0"])
 
     def signs(h):
-        op("t", lambda q: q.matmul_mx(T.psb[:, 512 * h:512 * h + H], T.uqr[:], T.usr[:], T.xq[:, H * h:H * h + H],
-                                      T.xs[:, H * h:H * h + H], True, True), ["uqr", "usr", "xq.%d" % h], ["psb.%d" % h])
-        V(lambda q: q.tensor_scalar(T.bits[:, H * h:H * h + H], T.psb[:, 512 * h:512 * h + H], 0.0, None, ALU.is_gt),
-          ["psb.%d" % h], ["bits.%d" % h])
+        a, b = PIECES[h]
+        ps, pn = bank(h)
+        V(lambda q: q.tensor_scalar(T.bits[:, a:b], ps[:, 0:b - a], 0.0, None, ALU.is_gt), [pn + ".0"], ["bits.%d" % h])
 
-    def lay_table(r):
-        S(lambda q: q.activation(T.glf[:], T.ident[:].indirect(T["glr%d" % r][:]), COPY), ["ident", "glr%d" % r], ["glf"])
+    def lay_table(e, r, a, b):
+        copy(e, T["glf%d" % r][:, 16 * a:16 * b], T.ident[:].indirect(T["glr%d" % r][:, a:b]), ["ident", "glr%d" % r],
+             ["glf%d.%d" % (r, k) for k in range(a // 24, b // 24)])
 
-    def split_table(r):
-        V(lambda q: q.tensor_scalar(T["ge%d" % r][:], T.glf[:, 0:768:2], -192.0, None, ALU.add), ["glf"], ["ge%d" % r])
-        V(lambda q: q.tensor_tensor(T["gd%d" % r][:], T.glf[:, 1:768:2], T.glf[:, 0:768:2], ALU.subtract), ["glf"], ["gd%d" % r])
+    def lay(e, r, t):
+        copy(e, T.lx[:, t:4 * C:4], T["x_%d" % r][:].indirect(T.ht4[:, 24 * t:24 * t + 24]), whole("x_%d" % r) + ["ht4.%d" % t],
+             ["lx.%d" % t])
 
-    for h in range(NH):
+    for h in range(NP):
         quantise_state(0, h)
+        score(h, T.uqr, T.usr, ["uqr", "usr"])
+    lay("s", 0, 0)
+    for h in range(NP):
         signs(h)
-    lay_table(0)
-    split_table(0)
+    for b in range(4):
+        V(lambda q: q.quantize_mx(T.eq[:, 128 * b:128 * b + 128], T.es[:, 128 * b:128 * b + 128], T.et[:, 3 - b:515 - b]),
+          ["et"], ["eq.%d" % b])
+    lay_table("s", 0, 24, 48)
+    lay_table("v", 0, 0, 24)
 
     for r in range(3):
         last = r == 2
         xn, X, Y = "x_%d" % r, T["x_%d" % r], T["x_%d" % (r + 1)]
-        lq, ls = T["lq%d" % r], T["ls%d" % r]
-
-        def lay(e, t):
-            fn = {"v": lambda q: q.tensor_copy(T.lx[:, t:4 * C:4], X[:].indirect(T.ht4[:, 24 * t:24 * t + 24])),
-                  "s": lambda q: q.activation(T.lx[:, t:4 * C:4], X[:].indirect(T.ht4[:, 24 * t:24 * t + 24]), COPY)}[e]
-            op(e, fn, whole(xn) + ["ht4.%d" % t], ["lx.%d" % t])
-        lay("s", 0)
-        lay("s", 1)
-        V(lambda q: q.tensor_tensor(T.t1[:], T.bits[:].indirect(T.ht16[:]), T["gd%d" % r][:], ALU.mult),
-          ["bits.0", "bits.1", "ht16", "gd%d" % r], ["t1"])
-        V(lambda q: q.tensor_tensor(T.ft[:, 0:C], T.t1[:], T["ge%d" % r][:], ALU.add), ["t1", "ge%d" % r], ["ft.0"])
-        for k in range(1, 8):
-            a, b = 16 * k, C * k
-            dma("y", "fb%d" % r, 14, T.ft[a:128, b:b + C], T.ft[0:128 - a, 0:C], ["ft.0"], ["ft.%d.a" % k])
-            dma("s", "fb%d" % r, 14, T.ft[0:a, b:b + C], T.ft[128 - a:128, 0:C], ["ft.0"], ["ft.%d.b" % k])
-        lay("v", 2)
-        lay("v", 3)
+        lq, ls, glf = T["lq%d" % r], T["ls%d" % r], T["glf%d" % r]
+        for t in range(1 if r == 0 else 0, 3):
+            lay("s", r, t)
+        gk = ["glf%d.0" % r, "glf%d.1" % r]
+        V(lambda q: q.tensor_tensor(T.t1[:], T.bits[:].indirect(T.ht16[:]), glf[:, 1:2 * C:2], ALU.mult),
+          ["bits.%d" % h for h in range(NP)] + ["ht16"] + gk, ["t1"])
+        V(lambda q: q.tensor_tensor(T.ft[:], T.t1[:], glf[:, 0:2 * C:2], ALU.add), ["t1"] + gk, ["ft"])
+        for s in range(7):
+            w = 0 if s < FIRST else C
+            sem, n = ("fa%d" % r, FIRST) if s < FIRST else ("fb%d" % r, 7 - FIRST)
+            dma("y", sem, n, T.tab[s:128:16, w:w + C], T.ft[16 * s:16 * s + 8, :], ["ft"], ["tab.%d" % s])
+        lay("v", r, 3)
         V(lambda q: q.quantize_mx(lq[:], ls[:], T.lx[:]), ["lx.%d" % t for t in range(4)], ["lq%d" % r])
         before("g", ["lq%d" % r])
         send(partner[r], T["landq%d" % r][:].bitcast(dt.uint8), lq[:].bitcast(dt.uint8), "arrq%d" % r)
         send(partner[r], T["lands%d" % r][:], ls[:], "arrq%d" % r)
-        S(lambda q: q.activation(T.x64[:], X[:], COPY, scale=64.0), whole(xn), whole("x64"))
         if not last:
-            lay_table(r + 1)
-        if r == 0:
-            V(lambda q: q.quantize_mx(T.eq[:], T.es[:], T.et[:]), ["et"], ["eq"])
-            V(lambda q: q.quantize_mx(T.vq[:], T.vs[:], T.vt[:]), ["vt"], ["vq"])
-        tables = ["ft.0"] + ["ft.%d.%s" % (k, c) for k in range(1, 8) for c in "ab"]
-
-        def step(s):
-            o, ok = (T.ov0, "ov0") if s == 0 else (T.ov, "ov")
-            V(lambda q: q.tensor_tensor(T.w1[:], T.ft[:].indirect(o[:, 0:3]), T.mask[:], ALU.mult), tables + [ok, "mask"], ["w1"])
-            V(lambda q: q.tensor_tensor_scan(T.w2[:], T.keep[:], T.w1[:], 0.0, ALU.mult, ALU.add), ["keep", "w1"], ["w2"])
-            top = 7 if last else 6
-
-            def offsets():
-                V(lambda q: q.tensor_scalar(T.ov[:, 0:3], T.w2[:, 15:48:16], T.kf[:, s + 1:s + 2], None, ALU.add),
-                  ["w2", "kf"], ["ov"])
-
-            def places():
-                V(lambda q: q.tensor_scalar(T.vo[:, 4 * s:4 * s + 3], T.w2[:, 15:48:16], 192.0, None, ALU.add), ["w2"], ["vo.%d" % s])
-                if s < 7:
-                    sem, n = ("vla%d" % r, 6) if s < 6 else ("vlb%d" % r, 1)
-                    dma("y", sem, n, T["vl%d" % r][16 * s + 16:16 * s + 32, :], T.vo[:, 4 * s:4 * s + 3], ["vo.%d" % s],
-                        ["vl%d.%d" % (r, s + 1)])
-                else:
-                    dma("y", "v8", 1, T.vl8[0:16, :], T.vo[:, 28:31], ["vo.7"], ["vl8"])
-            if s >= 6:
-                places()
-                if s < top:
-                    offsets()
-            else:
-                offsets()
-                places()
+            lay_table("s", r + 1, 0, 48)
         for s in range(7):
-            step(s)
-        before("g", ["vl%d.%d" % (r, b) for b in range(8)])
+            o, ok = (T.ov0, "ov0") if s == 0 else (T.ov, "ov")
+            w, keys = (0, range(FIRST)) if s < FIRST else (C, range(FIRST, 7))
+            a = 64 * s
+            V(lambda q: q.tensor_copy(T.w1[:], T.tab[:, w:w + C].indirect(o[:])), ["tab.%d" % k for k in keys] + [ok], ["w1"])
+            V(lambda q: q.transpose(T.w2[:, a:a + 64], T.w1[:]), ["w1"], ["w2.%d" % s])
+            if s < 6:
+                V(lambda q: q.tensor_scalar(T.ov[:], T.w2[:, a + s:a + 64:16], 192.0, None, ALU.add), ["w2.%d" % s], ["ov"])
+            if s % 2 == 0:
+                for half, slot in ((1, s), (0, 8)):
+                    if s == 0 and half == 0 and r > 0:
+                        continue
+                    for Q in range(4):
+                        c = 16 * half + 4 * Q
+                        copy("v" if s == 6 and half == 1 else "s", T.coll[16 * s:16 * s + 32, c:c + 4],
+                             T.w2[32 * Q:32 * Q + 32, a + slot:a + 64:16], ["w2.%d" % s], ["coll.%d.%d" % (s, c)])
+        V(lambda q: q.transpose(T.lt[:], T.coll[:]), ["coll.%d.%d" % (s, c) for s in range(0, 8, 2) for c in range(0, 32, 4)], ["lt"])
+        V(lambda q: q.tensor_scalar(T["vl%d" % r][:], T.lt[:, 0:24], 192.0, None, ALU.add), ["lt"], ["vl%d" % r])
+        before("g", ["vl%d" % r])
         send(partner[r], T["vland%d" % r][:], T["vl%d" % r][:], "arrl%d" % r)
         if last:
-            step(7)
-            before("g", ["vl8"])
-            send(partner[r], T.vland8[:], T.vl8[:], "arrl8")
-        else:
-            split_table(r + 1)
+            send(partner[r], T.fland[:], T.ft[:], "arrf")
+        if r == 0:
+            S(lambda q: q.activation(T.x64[:], X[:], COPY, scale=64.0), whole(xn), whole("x64"))
+        if r == 1:
+            V(lambda q: q.quantize_mx(T.vq[:], T.vs[:], T.vt[:]), ["vt"], ["vq"])
         for b in range(4):
-            op("t", lambda q, b=b: q.matmul_mx(T.psa[:, 512 * b:512 * b + C], T.eq[:, 128 * b:128 * b + 128], T.es[:, 128 * b:128 * b + 128],
-                                               T["landq%d" % r][:], T["lands%d" % r][:], True, True), ["eq", "landq%d" % r], ["psa.%d" % b])
-            V(lambda q, b=b: q.tensor_tensor(T.m[:, C * b:C * b + C], T.psa[:, 512 * b:512 * b + C], X[:, b:4 * C:4], ALU.max),
+            op("t", lambda q: q.matmul_mx(T.psa[:, 512 * b:512 * b + C], T.eq[:, 128 * b:128 * b + 128], T.es[:, 128 * b:128 * b + 128],
+                                          T["landq%d" % r][:], T["lands%d" % r][:], True, True), ["eq.%d" % b, "landq%d" % r], ["psa.%d" % b])
+            V(lambda q: q.tensor_tensor(T.m[:, C * b:C * b + C], T.psa[:, 512 * b:512 * b + C], X[:, b:4 * C:4], ALU.max),
               ["psa.%d" % b] + whole(xn), ["m.%d" % b])
-        for h in range(NH):
-            off = T["vland%d" % r][:, 12 * h:12 * h + 12]
+
+        def pick(e, h, b):
+            a, c = PIECES[h]
+            copy(e, T.z[:, 4 * a + b:4 * c:4], T.m[:, C * b:C * b + C].indirect(T["vland%d" % r][:, a // 16:c // 16]),
+                 ["m.%d" % b, "vland%d" % r], ["z.%d.%d" % (b, h)])
+
+        def product(h):
+            a, c = PIECES[h]
+            ps, pn = bank(h)
+            V(lambda q: q.quantize_mx(T.zq[:, a:c], T.zs[:, a:c], T.z[:, 4 * a:4 * c]), piece("z", h), ["zq.%d" % h])
             for b in range(4):
-                e = "v" if b < 2 else "s"
-                win, out = T.m[:, C * b:C * b + C].indirect(off), T.z[:, 4 * H * h + b:4 * H * h + 4 * H:4]
-                fn = {"v": lambda q: q.tensor_copy(out, win), "s": lambda q: q.activation(out, win, COPY)}[e]
-                op(e, fn, ["m.%d" % b, "vland%d" % r], ["z.%d.%d" % (b, h)])
-        for h in range(NH):
-            V(lambda q: q.quantize_mx(T.zq[:, H * h:H * h + H], T.zs[:, H * h:H * h + H], T.z[:, 4 * H * h:4 * H * h + 4 * H]),
-              half("z", h), ["zq.%d" % h])
-            ps, pn = (T.psb, "psb") if h == 0 else (T.psa, "psa")
-            for b in range(4):
-                op("t", lambda q: q.matmul_mx(ps[:, 512 * b:512 * b + H], T.wq[:, 128 * b:128 * b + 128], T.wsp[:, 128 * b:128 * b + 128],
-                                              T.zq[:, H * h:H * h + H], T.zs[:, H * h:H * h + H], True, True),
-                   ["wq", "wsp", "zq.%d" % h], ["%s.%d" % (pn, b)])
-        for h in range(NH):
-            ps, pn = (T.psb, "psb") if h == 0 else (T.psa, "psa")
-            for b in range(4):
-                u = T.uu[:, (4 * h + b) * H:(4 * h + b + 1) * H]
-                s0 = slice(4 * H * h + b, 4 * H * h + 4 * H, 4)
-                V(lambda q: q.tensor_tensor(u, ps[:, 512 * b:512 * b + H], T.x64[:, s0], ALU.add),
-                  ["%s.%d" % (pn, b), "x64.%d.%d" % (b, h)], ["uu.%d.%d" % (b, h)])
-                S(lambda q: q.activation(Y[:, s0], u, COPY, scale=0.015625), ["uu.%d.%d" % (b, h)], ["x_%d.%d.%d" % (r + 1, b, h)])
-        for h in range(NH):
+                op("t", lambda q: q.matmul_mx(ps[:, 512 * b:512 * b + c - a], T.wq[:, 128 * b:128 * b + 128], T.wsp[:, 128 * b:128 * b + 128],
+                                              T.zq[:, a:c], T.zs[:, a:c], True, True), ["wq", "wsp", "zq.%d" % h], ["%s.%d" % (pn, b)])
+
+        def add(h, b):
+            a, c = PIECES[h]
+            ps, pn = bank(h)
+            key = ["x64.%d.%d" % (b, h)]
+            V(lambda q: q.tensor_tensor(T.x64[:, 4 * a + b:4 * c:4], ps[:, 512 * b:512 * b + c - a], T.x64[:, 4 * a + b:4 * c:4], ALU.add),
+              ["%s.%d" % (pn, b)] + key, key)
+
+        def scale(e, h, b):
+            a, c = PIECES[h]
+            out, in_ = Y[:, 4 * a + b:4 * c:4], T.x64[:, 4 * a + b:4 * c:4]
+            op(e, {"v": lambda q: q.tensor_scalar(out, in_, 0.015625, None, ALU.mult),
+                   "s": lambda q: q.activation(out, in_, COPY, scale=0.015625)}[e],
+               ["x64.%d.%d" % (b, h)], ["x_%d.%d.%d" % (r + 1, b, h)])
+
+        def state(h):
             quantise_state(r + 1, h)
+            if last:
+                score(h, T.vq, T.vs, ["vq"])
+            else:
+                score(h, T.uqr, T.usr, ["uqr", "usr"])
+
+        def store(h):
+            a, c = PIECES[h]
+            dma("y", "st%d" % h, 6, T.oc[:, 4 * a:4 * c], T.xq[:, a:c].bitcast(dt.uint8), ["xq.%d" % h], [])
+            for k in range(4):
+                dma("y", "st%d" % h, 6, T.osc[4 * k:4 * k + 4, a:c], T.xs[32 * k:32 * k + 4, a:c], ["xq.%d" % h], [])
+
+        def read(h):
             if not last:
-                signs(h)
-    for h in range(NH):
-        c0, c1 = H * h, H * h + H
-        op("t", lambda q: q.matmul_mx(T.psb[:, 512 * h:512 * h + H], T.vq[:], T.vs[:], T.xq[:, c0:c1], T.xs[:, c0:c1], True, True),
-           ["vq", "xq.%d" % h], ["psb.%d" % h])
-        sem = "st%d" % h
-        dma("y", sem, 6, T.oc[:, 4 * c0:4 * c1], T.xq[:, c0:c1].bitcast(dt.uint8), ["xq.%d" % h], [])
-        for k in range(4):
-            dma("s" if k % 2 else "y", sem, 6, T.osc[4 * k:4 * k + 4, c0:c1], T.xs[32 * k:32 * k + 4, c0:c1], ["xq.%d" % h], [])
-        V(lambda q: q.tensor_copy(T.ysb[:, c0:c1], T.psb[:, 512 * h:512 * h + H]), ["psb.%d" % h], ["ysb.%d" % h])
-        dma("y", sem, 6, T.y[:, c0:c1], T.ysb[:, c0:c1], ["ysb.%d" % h], [])
-    S(lambda q: q.activation(T.plb[:], T.ident[:, 0:C].indirect(T.vland2[:]), COPY), ["ident", "vland2"], ["plb"])
-    dma("s", "stp", 1, T.pl[0:7, :], T.plb[16:128:16, :], ["plb"], [])
-    S(lambda q: q.activation(T.plc[:], T.ident[:, 0:C].indirect(T.vland8[:]), COPY), ["ident", "vland8"], ["plc"])
-    dma("s", "stq", 1, T.pl[7:8, :], T.plc[0:1, :], ["plc"], [])
+                return signs(h)
+            a, c = PIECES[h]
+            ps, pn = bank(h)
+            copy("v", T.ysb[:, a:c], ps[:, 0:c - a], [pn + ".0"], ["ysb.%d" % h])
+            dma("s", "st%d" % h, 6, T.y[:, a:c], T.ysb[:, a:c], ["ysb.%d" % h], [])
+
+        for b in range(4):
+            pick("sv"[b // 2], 0, b)
+        product(0)
+        for b in range(4):
+            pick("v" if b == 0 else "s", 1, b)
+        for b in range(3):
+            add(0, b)
+        product(1)
+        add(0, 3)
+        for b in range(4):
+            scale("s", 0, b)
+        add(1, 0)
+        add(1, 1)
+        state(0)
+        if last:
+            store(0)
+        add(1, 2)
+        add(1, 3)
+        for b in range(4):
+            scale("s" if b < 3 else "v", 1, b)
+        state(1)
+        if last:
+            S(lambda q: q.activation(T.plb[:], T.fland[:].indirect(T.vland2[:]), ActivationFunctionType.Identity, bias=192.0),
+              ["fland", "vland2"], ["plb"])
+            dma("s", "stp", 1, T.pl[:], T.plb[0:128:16, :], ["plb"], [])
+            store(1)
+        read(0)
+        read(1)
     finish()

@@ -4,52 +4,58 @@ C = 384
 PIECES = [(0, 192), (192, 384)]
 STEP = [1, 2, 4]
 FIRST = 2
+WALK = [(0, [(1, 0), (0, 8)]), (1, []), (3, [(2, 8), (3, 2), (4, 3)]), (4, []), (None, [(5, 8), (6, 5), (7, 6)])]
 ALU = AluOpType
 COPY = ActivationFunctionType.Copy
 
 SCRATCH = {
     "ut": ("sbuf", [128, 512], "bfloat16"), "vt": ("sbuf", [128, 512], "bfloat16"),
     "uq": ("sbuf", [128, 128], "float8_e4m3fn_x4"), "us": ("sbuf", [128, 128], "uint8"),
-    "uqr": ("sbuf", [128, 128], "float8_e4m3fn_x4"), "usr": ("sbuf", [128, 128], "uint8"),
     "vq": ("sbuf", [128, 128], "float8_e4m3fn_x4"), "vs": ("sbuf", [128, 128], "uint8"),
     "wq": ("sbuf", [128, 512], "float8_e4m3fn_x4"), "wsp": ("sbuf", [128, 512], "uint8"),
     "e0": ("sbuf", [128, 516], "bfloat16"), "et": ("sbuf", [128, 516], "bfloat16"),
     "eq": ("sbuf", [128, 512], "float8_e4m3fn_x4"), "es": ("sbuf", [128, 512], "uint8"),
     "x64": ("sbuf", [128, 4 * C], "bfloat16"), "lx": ("sbuf", [128, 4 * C], "bfloat16"),
+    "ht4": ("sbuf", [128, 96], "uint16"),
     "m": ("sbuf", [128, 4 * C], "bfloat16"), "z": ("sbuf", [128, 4 * C], "bfloat16"),
     "zq": ("sbuf", [128, C], "float8_e4m3fn_x4"), "zs": ("sbuf", [128, C], "uint8"),
-    "xq": ("sbuf", [128, C], "float8_e4m3fn_x4"), "xs": ("sbuf", [128, C], "uint8"),
-    "gli": ("sbuf", [128, 48], "int32"), "glb": ("sbuf", [128, 48], "int32"),
-    "gt": ("sbuf", [128, 48], "float32"), "gu": ("sbuf", [128, 48], "float32"), "gl16": ("sbuf", [128, 48], "uint16"),
-    "hti": ("sbuf", [128, 24], "int32"), "ht16": ("sbuf", [128, 24], "uint16"), "ht4": ("sbuf", [128, 96], "uint16"),
-    "bits": ("sbuf", [128, C], "bfloat16"), "t1": ("sbuf", [128, C], "float32"),
-    "ft": ("sbuf", [128, C], "bfloat16"), "tab": ("sbuf", [128, 2 * C], "bfloat16"),
+    "gli": ("sbuf", [128, 48], "int32"), "glb": ("sbuf", [128, 48], "int32"), "hti": ("sbuf", [128, 24], "int32"),
+    "gt": ("sbuf", [128, 48], "float32"), "gu": ("sbuf", [128, 48], "float32"), "own": ("sbuf", [128, 72], "uint16"),
+    "bits": ("sbuf", [128, C], "bfloat16"), "bl": ("sbuf", [128, C], "bfloat16"), "bland": ("sbuf", [128, C], "bfloat16"),
+    "t1": ("sbuf", [128, C], "float32"), "ft": ("sbuf", [128, C + 32], "bfloat16"), "tab": ("sbuf", [128, 2 * C], "bfloat16"),
+    "ta": ("sbuf", [128, C], "bfloat16"), "tb": ("sbuf", [128, C + 32], "bfloat16"), "fl": ("sbuf", [128, 24], "uint16"),
+    "fg": ("sbuf", [128, C], "bfloat16"),
+    "gout": ("dram", [128, 48], "int32"), "gin": ("dram", [128, 48], "int32"),
+    "fout": ("dram", [128, 24], "bfloat16"), "fin": ("dram", [128, 24], "bfloat16"),
+    "upi": ("sbuf", [128, 8], "int32"), "up": ("sbuf", [128, 8], "uint16"),
+    "uq0": ("sbuf", [128, 128], "float8_e4m3fn_x4"), "us0": ("sbuf", [128, 128], "uint8"),
     "w1": ("sbuf", [128, 64], "bfloat16"), "w2": ("sbuf", [128, 7 * 64], "bfloat16"),
     "coll": ("sbuf", [128, 32], "bfloat16"), "lt": ("sbuf", [128, 32], "bfloat16"),
     "ov0": ("sbuf", [128, 4], "uint16"), "ov": ("sbuf", [128, 4], "uint16"),
-    "ident": ("sbuf", [128, 768], "float32"), "ip": ("sbuf", [128, 1], "int32"),
-    "kcol": ("sbuf", [128, 4], "float32"), "upi": ("sbuf", [128, 8], "int32"),
-    "up": ("sbuf", [128, 8], "uint16"), "ia": ("sbuf", [128, 4], "int32"), "fa": ("sbuf", [128, 8], "float32"),
+    "ident": ("sbuf", [128, 2 * C], "float32"), "ip": ("sbuf", [128, 1], "int32"),
+    "kcol": ("sbuf", [128, 4], "float32"), "ia": ("sbuf", [128, 4], "int32"), "fa": ("sbuf", [128, 8], "float32"),
     "ysb": ("sbuf", [128, C], "float32"), "plb": ("sbuf", [128, C], "float32"), "fland": ("sbuf", [128, C], "bfloat16"),
     "psa": ("psum", [128, 2048], "float32"), "psb": ("psum", [128, 2048], "float32"),
 }
 for _r in range(3):
-    SCRATCH["lq%d" % _r] = ("sbuf", [128, C], "float8_e4m3fn_x4")
-    SCRATCH["ls%d" % _r] = ("sbuf", [128, C], "uint8")
     SCRATCH["landq%d" % _r] = ("sbuf", [128, C], "float8_e4m3fn_x4")
     SCRATCH["lands%d" % _r] = ("sbuf", [128, C], "uint8")
-    SCRATCH["glr%d" % _r] = ("sbuf", [128, 48], "uint16")
+    SCRATCH["lq%d" % _r] = ("sbuf", [128, C], "float8_e4m3fn_x4")
+    SCRATCH["ls%d" % _r] = ("sbuf", [128, C], "uint8")
+    SCRATCH["far%d" % _r] = ("sbuf", [128, 48], "uint16")
     SCRATCH["glf%d" % _r] = ("sbuf", [128, 2 * C], "float32")
     SCRATCH["vl%d" % _r] = ("sbuf", [128, 24], "uint16")
     SCRATCH["vland%d" % _r] = ("sbuf", [128, 24], "uint16")
 for _r in range(4):
     SCRATCH["x_%d" % _r] = ("sbuf", [128, 4 * C], "bfloat16")
+    SCRATCH["xq%d" % _r] = ("sbuf", [128, C], "float8_e4m3fn_x4")
+    SCRATCH["xs%d" % _r] = ("sbuf", [128, C], "uint8")
 
-SEMAPHORES = ["cv", "cs", "ct", "cg", "sent", "arrf",
+SEMAPHORES = ["cv", "cs", "ct", "cg", "sent", "arrf", "arrb", "fo", "fi", "ld_go", "ld_g2",
               "ld_gl", "ld_ht", "ld_u", "ld_w", "ld_v", "ld_x0", "ld_x1",
               "st0", "st1", "st2", "stp"]
 for _r in range(3):
-    SEMAPHORES += ["arrq%d" % _r, "arrl%d" % _r, "arrg%d" % _r, "fa%d" % _r, "fb%d" % _r]
+    SEMAPHORES += ["arrq%d" % _r, "arrl%d" % _r, "arrg%d" % _r, "fa%d" % _r, "fb%d" % _r, "fc%d" % _r]
 
 
 def tracker(g, T):
@@ -138,18 +144,21 @@ def rank_program(g, core, T, topo):
     partner = [T.cores[rank ^ s] for s in STEP]
     NP = len(PIECES)
 
-    def send(dst, out, in_, sem):
-        e = topo.engines(core, dst)[:8]
-        rid, pid = topo.addr(dst)[:2]
-        g.remote_dma(out, in_, T.sem[sem], T.sem.sent, pid, rid, sum(1 << k for k in e))
-        total["sent"] = total.get("sent", 0) + len(e)
+    engines = [topo.engines(core, p)[:8] for p in partner]
 
-    ne = [len(topo.engines(core, p)[:8]) for p in partner]
+    def send(r, out, in_, sem, keys):
+        before("g", keys)
+        rid, pid = topo.addr(partner[r])[:2]
+        g.remote_dma(out, in_, T.sem[sem], T.sem.sent, pid, rid, sum(1 << k for k in engines[r]))
+        total["sent"] = total.get("sent", 0) + len(engines[r])
+
     for r in range(3):
-        arrives("arrq%d" % r, 2 * ne[r], ["landq%d" % r])
-        arrives("arrl%d" % r, ne[r], ["vland%d" % r])
-        arrives("arrg%d" % r, ne[r], ["glr%d" % r])
-    arrives("arrf", ne[2], ["fland"])
+        arrives("arrq%d" % r, 2 * len(engines[r]), ["landq%d" % r])
+        if r > 0:
+            arrives("arrl%d" % r, len(engines[r]), ["vland%d" % r])
+            arrives("arrg%d" % r, len(engines[r]), ["far1" if r == 1 else "gin"])
+    arrives("arrb", len(engines[0]), ["bland"])
+    arrives("arrf", len(engines[2]), ["fin"])
 
     def piece(name, h):
         return ["%s.%d.%d" % (name, b, h) for b in range(4)]
@@ -164,19 +173,32 @@ def rank_program(g, core, T, topo):
         op(e, {"v": lambda q: q.tensor_copy(out, in_), "s": lambda q: q.activation(out, in_, COPY)}[e], r, w)
 
     cut = 4 * PIECES[0][1]
-    dma("y", "ld_gl", 3, T.gli[:], T.gl[:], [], ["gli"])
-    dma("s", "ld_gl", 3, T.glb[1:128, :], T.gl[0:127, :], [], ["glb"])
-    dma("s", "ld_gl", 3, T.glb[0:1, :], T.gl[0:1, :], [], ["glb0"])
-    dma("y", "ld_u", 1, T.ut[:], T.u[:], [], ["ut"])
-    dma("s", "ld_ht", 1, T.hti[:], T.ht[:], [], ["hti"])
-    dma("y", "ld_x0", 1, T.x_0[:, 0:cut], T.x[:, 0:cut], [], piece("x_0", 0))
-    dma("s", "ld_x1", 1, T.x_0[:, cut:], T.x[:, cut:], [], [k for h in range(1, NP) for k in piece("x_0", h)])
+    def load_table(e, sem, src, keys):
+        dma(e, sem, 3, T.gli[:], src[:], keys, ["gli"])
+        dma(e, sem, 3, T.glb[1:128, :], src[0:127, :], keys, ["glb"])
+        dma(e, sem, 3, T.glb[0:1, :], src[0:1, :], keys, ["glb0"])
 
-    op("g", lambda q: q.iota(T.ip[:], [[0, 1]], 0, 1), [], ["ip"])
+    dma("y", "ld_go", 1, T.gout[:], T.gl[:], [], ["gout"])
+    dma("s", "ld_u", 1, T.ut[:], T.u[:], [], ["ut"])
+    dma("y", "ld_ht", 1, T.hti[:], T.ht[:], [], ["hti"])
+    dma("s", "ld_x0", 1, T.x_0[:, 0:cut], T.x[:, 0:cut], [], piece("x_0", 0))
+    dma("y", "ld_x1", 1, T.x_0[:, cut:], T.x[:, cut:], [], [k for h in range(1, NP) for k in piece("x_0", h)])
+    load_table("y", "ld_gl", T.gl, [])
+
     op("g", lambda q: q.iota(T.upi[:], [[16, 8]], 0, 0), [], ["upi"])
+    op("g", lambda q: q.iota(T.ip[:], [[0, 1]], 0, 1), [], ["ip"])
     op("g", lambda q: q.iota(T.kcol[:], [[2, 2], [256, 2]], 0, 0, allow_small_or_imprecise_dtypes=True), [], ["kcol"])
-    op("g", lambda q: q.iota(T.ident[:], [[1, 768]], 1 - C, 0, allow_small_or_imprecise_dtypes=True), [], ["ident"])
+    op("g", lambda q: q.iota(T.ident[:, 0:256], [[1, 256]], 1 - C, 0, allow_small_or_imprecise_dtypes=True), [], ["ident.0"])
+    for k in (1, 2):
+        S(lambda q: q.activation(T.ident[:, 256 * k:256 * k + 256], T.ident[:, 0:256], COPY, bias=256.0 * k), ["ident.0"], ["ident.%d" % k])
+    ik = ["ident.%d" % k for k in range(3)]
+    send(2, T.gin[:], T.gout[:], "arrg2", ["gout"])
     V(lambda q: q.memset(T.e0[:], 1.0), [], ["e0"])
+    V(lambda q: q.memset(T.fland[:], 0.0), [], ["fland"])
+    V(lambda q: q.memset(T.ft[:, 0:16], 0.0), [], ["pad0"])
+    V(lambda q: q.memset(T.ft[:, 16 + C:], 0.0), [], ["pad1"])
+    V(lambda q: q.memset(T.fl[:], 0), [], ["fl"] + ["fl.%d" % k for k in range(4)])
+    V(lambda q: q.tensor_copy(T.up[:], T.upi[:]), ["upi"], ["up"])
     V(lambda q: q.tensor_scalar(T.ia[:, 3:4], T.ip[:], 1, None, ALU.bitwise_and), ["ip"], ["ia3"])
     V(lambda q: q.tensor_scalar(T.ia[:, 0:1], T.ip[:], 15, None, ALU.bitwise_and), ["ip"], ["ia0"])
     V(lambda q: q.tensor_scalar(T.ia[:, 1:2], T.ip[:], 5, None, ALU.arith_shift_right), ["ip"], ["ia1"])
@@ -184,130 +206,167 @@ def rank_program(g, core, T, topo):
     V(lambda q: q.tensor_scalar(T.fa[:, 3:4], T.ia[:, 3:4], -1.0, None, ALU.mult), ["ia3"], ["fa3"])
     V(lambda q: q.tensor_scalar(T.fa[:, 4:5], T.ia[:, 3:4], 192.0, 191.0, ALU.mult, ALU.add), ["ia3"], ["fa4"])
     V(lambda q: q.tensor_scalar(T.fa[:, 0:1], T.ia[:, 0:1], 16.0, None, ALU.mult), ["ia0"], ["fa0"])
-    V(lambda q: q.tensor_copy(T.up[:], T.upi[:]), ["upi"], ["up"])
     V(lambda q: q.tensor_scalar(T.fa[:, 1:2], T.ia[:, 1:2], 4.0, T.fa[:, 0:1], ALU.mult, ALU.add), ["ia1", "fa0"], ["fa1"])
     V(lambda q: q.tensor_scalar(T.fa[:, 2:3], T.ia[:, 2:3], T.fa[:, 1:2], None, ALU.add), ["ia2", "fa1"], ["fa2"])
     V(lambda q: q.tensor_scalar(T.ov0[:], T.kcol[:], T.fa[:, 2:3], float(C - 1), ALU.add, ALU.min), ["kcol", "fa2"], ["ov0"])
 
-    V(lambda q: q.tensor_scalar(T.gt[:], T.glb[:], T.fa[:, 3:4], T.fa[:, 4:5], ALU.mult, ALU.add), ["glb", "glb0", "fa3", "fa4"], ["gt"])
-    V(lambda q: q.tensor_tensor(T.gu[:], T.gt[:], T.gli[:], ALU.add), ["gt", "gli"], ["gu"])
-    V(lambda q: q.tensor_copy(T.gl16[:], T.gu[:]), ["gu"], ["gl16"])
+    def places(out, key):
+        V(lambda q: q.tensor_scalar(T.gt[:], T.glb[:], T.fa[:, 3:4], T.fa[:, 4:5], ALU.mult, ALU.add), ["glb", "glb0", "fa3", "fa4"], ["gt"])
+        V(lambda q: q.tensor_tensor(T.gu[:], T.gt[:], T.gli[:], ALU.add), ["gt", "gli"], ["gu"])
+        V(lambda q: q.tensor_copy(out, T.gu[:]), ["gu"], [key])
 
-    def send_table(r):
-        before("g", ["gl16"])
-        send(partner[r], T["glr%d" % r][:], T.gl16[:], "arrg%d" % r)
-    send_table(0)
-    op("g", lambda q: q.affine_select(T.et[:], T.e0[:], [[1, 516]], ALU.is_equal, 0.0, -3, -4), ["e0"], ["et"])
-    op("g", lambda q: q.iota(T.tab[:], [[0, 2], [1, C]], -192, 0, allow_small_or_imprecise_dtypes=True), [],
-       ["tab.%d" % s for s in range(7)])
-    send_table(1)
-    send_table(2)
-
-    V(lambda q: q.quantize_mx(T.uq[:], T.us[:], T.ut[:]), ["ut"], ["uq"])
-    V(lambda q: q.tensor_copy(T.uqr[:].bitcast(dt.uint32), T.uq[:].bitcast(dt.uint32).indirect(T.up[:])), ["uq", "up"], ["uqr"])
-    copy("s", T.usr[:], T.us[:].indirect(T.up[:]), ["uq", "up"], ["usr"])
+    V(lambda q: q.quantize_mx(T.uq0[:], T.us0[:], T.ut[:]), ["ut"], ["uq0"])
+    V(lambda q: q.tensor_copy(T.uq[:].bitcast(dt.uint32), T.uq0[:].bitcast(dt.uint32).indirect(T.up[:])), ["uq0", "up"], ["uq"])
+    copy("s", T.us[:], T.us0[:].indirect(T.up[:]), ["uq0", "up"], ["us"])
     for t in range(4):
         V(lambda q: q.tensor_scalar(T.ht4[:, 24 * t:24 * t + 24], T.hti[:], 4.0, float(t), ALU.mult, ALU.add), ["hti"], ["ht4.%d" % t])
-    V(lambda q: q.tensor_copy(T.ht16[:], T.hti[:]), ["hti"], ["ht16"])
-    dma("y", "ld_w", 2, T.wq[:].bitcast(dt.uint8), T.wc[:], [], ["wq"])
-    dma("y", "ld_w", 2, T.wsp[:], T.ws[:], [], ["wsp"])
-    dma("y", "ld_v", 1, T.vt[:], T.v[:], [], ["vt"])
+    V(lambda q: q.tensor_copy(T.own[:, 48:72], T.hti[:]), ["hti"], ["ht16"])
 
     def bank(h):
         return (T.psb, "psb") if h % 2 == 0 else (T.psa, "psa")
 
     def quantise_state(r, h):
         a, b = PIECES[h]
-        V(lambda q: q.quantize_mx(T.xq[:, a:b], T.xs[:, a:b], T["x_%d" % r][:, 4 * a:4 * b]), piece("x_%d" % r, h), ["xq.%d" % h])
+        V(lambda q: q.quantize_mx(T["xq%d" % r][:, a:b], T["xs%d" % r][:, a:b], T["x_%d" % r][:, 4 * a:4 * b]),
+          piece("x_%d" % r, h), ["xq%d.%d" % (r, h)])
 
-    def score(h, wq, ws, keys):
+    def score(r, h, wq, ws, keys):
         a, b = PIECES[h]
         ps, pn = bank(h)
-        op("t", lambda q: q.matmul_mx(ps[:, 0:b - a], wq[:], ws[:], T.xq[:, a:b], T.xs[:, a:b], True, True),
-           keys + ["xq.%d" % h], [pn + ".0"])
+        op("t", lambda q: q.matmul_mx(ps[:, 0:b - a], wq[:], ws[:], T["xq%d" % r][:, a:b], T["xs%d" % r][:, a:b], True, True),
+           keys + ["xq%d.%d" % (r, h)], [pn + ".0"])
 
     def signs(h):
         a, b = PIECES[h]
         ps, pn = bank(h)
         V(lambda q: q.tensor_scalar(T.bits[:, a:b], ps[:, 0:b - a], 0.0, None, ALU.is_gt), [pn + ".0"], ["bits.%d" % h])
 
-    def lay_table(e, r, a, b):
-        copy(e, T["glf%d" % r][:, 16 * a:16 * b], T.ident[:].indirect(T["glr%d" % r][:, a:b]), ["ident", "glr%d" % r],
-             ["glf%d.%d" % (r, k) for k in range(a // 24, b // 24)])
+    def lay_table(r, at, key):
+        copy("s", T["glf%d" % r][:], T.ident[:].indirect(at), ik + [key], ["glf%d" % r])
 
     def lay(e, r, t):
         copy(e, T.lx[:, t:4 * C:4], T["x_%d" % r][:].indirect(T.ht4[:, 24 * t:24 * t + 24]), whole("x_%d" % r) + ["ht4.%d" % t],
              ["lx.%d" % t])
 
+    def send_laid(r, after):
+        lq, ls = T["lq%d" % r], T["ls%d" % r]
+        V(lambda q: q.quantize_mx(lq[:], ls[:], T.lx[:]), ["lx.%d" % t for t in range(4)], ["lq%d" % r])
+        send(r, T["landq%d" % r][:].bitcast(dt.uint8), lq[:].bitcast(dt.uint8), "arrq%d" % r, ["lq%d" % r] + after)
+        send(r, T["lands%d" % r][:], ls[:], "arrq%d" % r, ["lq%d" % r])
+
+    def constants(codes, scales, tile, keys, name):
+        for b in range(4):
+            V(lambda q: q.quantize_mx(codes[:, 128 * b:128 * b + 128], scales[:, 128 * b:128 * b + 128], tile[:, 3 - b:515 - b]),
+              keys, ["%s.%d" % (name, b)])
+
     for h in range(NP):
         quantise_state(0, h)
-        score(h, T.uqr, T.usr, ["uqr", "usr"])
-    lay("s", 0, 0)
+        score(0, h, T.uq, T.us, ["uq", "us"])
+    for t in range(3):
+        lay("s", 0, t)
     for h in range(NP):
         signs(h)
-    for b in range(4):
-        V(lambda q: q.quantize_mx(T.eq[:, 128 * b:128 * b + 128], T.es[:, 128 * b:128 * b + 128], T.et[:, 3 - b:515 - b]),
-          ["et"], ["eq.%d" % b])
-    lay_table("s", 0, 24, 48)
-    lay_table("v", 0, 0, 24)
 
     for r in range(3):
         last = r == 2
         xn, X, Y = "x_%d" % r, T["x_%d" % r], T["x_%d" % (r + 1)]
-        lq, ls, glf = T["lq%d" % r], T["ls%d" % r], T["glf%d" % r]
-        for t in range(1 if r == 0 else 0, 3):
-            lay("s", r, t)
-        gk = ["glf%d.0" % r, "glf%d.1" % r]
-        V(lambda q: q.tensor_tensor(T.t1[:], T.bits[:].indirect(T.ht16[:]), glf[:, 1:2 * C:2], ALU.mult),
-          ["bits.%d" % h for h in range(NP)] + ["ht16"] + gk, ["t1"])
-        V(lambda q: q.tensor_tensor(T.ft[:], T.t1[:], glf[:, 0:2 * C:2], ALU.add), ["t1"] + gk, ["ft"])
-        for s in range(7):
-            w = 0 if s < FIRST else C
-            sem, n = ("fa%d" % r, FIRST) if s < FIRST else ("fb%d" % r, 7 - FIRST)
-            dma("y", sem, n, T.tab[s:128:16, w:w + C], T.ft[16 * s:16 * s + 8, :], ["ft"], ["tab.%d" % s])
-        lay("v", r, 3)
-        V(lambda q: q.quantize_mx(lq[:], ls[:], T.lx[:]), ["lx.%d" % t for t in range(4)], ["lq%d" % r])
-        before("g", ["lq%d" % r])
-        send(partner[r], T["landq%d" % r][:].bitcast(dt.uint8), lq[:].bitcast(dt.uint8), "arrq%d" % r)
-        send(partner[r], T["lands%d" % r][:], ls[:], "arrq%d" % r)
-        if not last:
-            lay_table("s", r + 1, 0, 48)
-        for s in range(7):
-            o, ok = (T.ov0, "ov0") if s == 0 else (T.ov, "ov")
-            w, keys = (0, range(FIRST)) if s < FIRST else (C, range(FIRST, 7))
-            a = 64 * s
-            V(lambda q: q.tensor_copy(T.w1[:], T.tab[:, w:w + C].indirect(o[:])), ["tab.%d" % k for k in keys] + [ok], ["w1"])
-            V(lambda q: q.transpose(T.w2[:, a:a + 64], T.w1[:]), ["w1"], ["w2.%d" % s])
-            if s < 6:
-                V(lambda q: q.tensor_scalar(T.ov[:], T.w2[:, a + s:a + 64:16], 192.0, None, ALU.add), ["w2.%d" % s], ["ov"])
-            if s % 2 == 0:
-                for half, slot in ((1, s), (0, 8)):
-                    if s == 0 and half == 0 and r > 0:
-                        continue
-                    for Q in range(4):
-                        c = 16 * half + 4 * Q
-                        copy("v" if s == 6 and half == 1 else "s", T.coll[16 * s:16 * s + 32, c:c + 4],
-                             T.w2[32 * Q:32 * Q + 32, a + slot:a + 64:16], ["w2.%d" % s], ["coll.%d.%d" % (s, c)])
-        V(lambda q: q.transpose(T.lt[:], T.coll[:]), ["coll.%d.%d" % (s, c) for s in range(0, 8, 2) for c in range(0, 32, 4)], ["lt"])
-        V(lambda q: q.tensor_scalar(T["vl%d" % r][:], T.lt[:, 0:24], 192.0, None, ALU.add), ["lt"], ["vl%d" % r])
-        before("g", ["vl%d" % r])
-        send(partner[r], T["vland%d" % r][:], T["vl%d" % r][:], "arrl%d" % r)
-        if last:
-            send(partner[r], T.fland[:], T.ft[:], "arrf")
-        if r == 0:
-            S(lambda q: q.activation(T.x64[:], X[:], COPY, scale=64.0), whole(xn), whole("x64"))
-        if r == 1:
-            V(lambda q: q.quantize_mx(T.vq[:], T.vs[:], T.vt[:]), ["vt"], ["vq"])
-        for b in range(4):
+        signed, sk = T.bits[:].indirect(T.own[:, 48:72]), ["bits.%d" % h for h in range(NP)] + ["ht16"]
+        tk = ["tab.%d" % s for s in range(7)]
+        glf, gk = T["glf%d" % r], ["glf%d" % r]
+
+        def unpack(b):
             op("t", lambda q: q.matmul_mx(T.psa[:, 512 * b:512 * b + C], T.eq[:, 128 * b:128 * b + 128], T.es[:, 128 * b:128 * b + 128],
                                           T["landq%d" % r][:], T["lands%d" % r][:], True, True), ["eq.%d" % b, "landq%d" % r], ["psa.%d" % b])
-            V(lambda q: q.tensor_tensor(T.m[:, C * b:C * b + C], T.psa[:, 512 * b:512 * b + C], X[:, b:4 * C:4], ALU.max),
-              ["psa.%d" % b] + whole(xn), ["m.%d" % b])
+
+        def larger(b, a, c):
+            V(lambda q: q.tensor_tensor(T.m[:, C * b + a:C * b + c], T.psa[:, 512 * b + a:512 * b + c], X[:, 4 * a + b:4 * c:4], ALU.max),
+              ["psa.%d" % b] + whole(xn), ["m.%d.%d" % (b, k) for k in range(2 * a // C, 2 * c // C)])
+
+        if r == 0:
+            V(lambda q: q.tensor_copy(T.bl[:], signed), sk, ["bl"])
+            send(r, T.bland[:], T.bl[:], "arrb", ["bl"])
+            op("g", lambda q: q.affine_select(T.et[:], T.e0[:], [[1, 516]], ALU.is_equal, 0.0, -3, -4), ["e0"], ["et"])
+            places(T.own[:, 0:48], "gl16")
+            lay_table(0, T.own[:, 0:48], "gl16")
+            lay("v", r, 3)
+            send_laid(r, [])
+            send(1, T.far1[:], T.own[:, 0:48], "arrg1", ["gl16"])
+            for w in range(2):
+                copy("v", T.tab[:, C * w:C * w + C], T.ident[:, 191:191 + C], ik, tk[:FIRST] if w == 0 else tk[FIRST:])
+            constants(T.eq, T.es, T.et, ["et"], "eq")
+            S(lambda q: q.activation(T.x64[:], T.x_0[:], COPY, scale=64.0), whole("x_0"), whole("x64"))
+            V(lambda q: q.tensor_tensor(T.t1[:], T.bland[:], glf[:, 1:2 * C:2], ALU.mult), ["bland"] + gk, ["t1"])
+        else:
+            V(lambda q: q.tensor_tensor(T.t1[:], signed, glf[:, 1:2 * C:2], ALU.mult), sk + gk, ["t1"])
+        V(lambda q: q.tensor_tensor(T.ft[:, 16:16 + C], T.t1[:], glf[:, 0:2 * C:2], ALU.add), ["t1"] + gk, ["ft"])
+
+        def spread(s, key, a, sem, n):
+            w = 0 if s < FIRST else C
+            dma("y", sem, n, T.tab[s:128:16, w:w + C], T[key][16 * s:16 * s + 8, a:a + C], [key], ["tab.%d" % s])
+        for s in (0, 1):
+            spread(s, "ft", 16, "fa%d" % r, 2)
+        for s in (2, 4, 5):
+            spread(s, "ft", 16, "fb%d" % r, 3)
+        V(lambda q: q.transpose(T.ta[:], T.ft[:, 16:16 + C]), ["ft"], ["ta"])
+        V(lambda q: q.transpose(T.tb[:], T.ft[:]), ["ft", "pad0", "pad1"], ["tb"])
+        for k, (out, in_) in enumerate(((T.fl[32:64, 1:24:2], T.ta[32:64, 0:C:32]), (T.fl[96:128, 0:24:2], T.ta[64:96, 16:C:32]),
+                                        (T.fl[32:64, 0:24:2], T.tb[32:64, 0:C:32]), (T.fl[96:128, 1:24:2], T.tb[64:96, 48:C + 32:32]))):
+            V(lambda q: q.tensor_scalar(out, in_, 192.0, None, ALU.add), ["ta" if k < 2 else "tb"], ["fl.%d" % k])
+        copy("s", T.fg[:], T.ft[:, 16:16 + C].indirect(T.fl[:]), ["ft", "fl"] + ["fl.%d" % k for k in range(4)], ["fg"])
+        for s in (3, 6):
+            spread(s, "fg", 0, "fc%d" % r, 2)
+        fill = []
+        if r == 0:
+            dma("y", "ld_w", 2, T.wq[:].bitcast(dt.uint8), T.wc[:], tk, ["wq"])
+            dma("y", "ld_w", 2, T.wsp[:], T.ws[:], [], ["wsp"])
+            dma("y", "ld_v", 1, T.vt[:], T.v[:], [], ["vt"])
+            load_table("y", "ld_g2", T.gin, ["gin"])
+            for b in range(4):
+                unpack(b)
+                fill += [lambda b=b: larger(b, 0, C // 2), lambda b=b: larger(b, C // 2, C)]
+        else:
+            send_laid(r, ["fg"])
+        if r == 1:
+            places(T.far2[:], "far2")
+        if last:
+            dma("y", "fo", 1, T.fout[:], T.ft[0:128:16, 16:16 + C], ["ft"], ["fout"])
+            send(r, T.fin[:], T.fout[:], "arrf", ["fout"])
+            dma("y", "fi", 1, T.fland[0:128:16, :], T.fin[:], ["fin"], ["fland"])
+            fill.append(lambda: V(lambda q: q.quantize_mx(T.vq[:], T.vs[:], T.vt[:]), ["vt"], ["vq"]))
+        for s, (onward, found) in enumerate(WALK):
+            def gap():
+                if s > 0 and fill:
+                    fill.pop(0)()
+            o, ok = (T.ov0, "ov0") if s == 0 else (T.ov, "ov")
+            a = 64 * s
+            w, keys = (0, tk[:FIRST]) if s < FIRST else (C, tk[FIRST:])
+            V(lambda q: q.tensor_copy(T.w1[:], T.tab[:, w:w + C].indirect(o[:])), keys + [ok], ["w1"])
+            gap()
+            V(lambda q: q.transpose(T.w2[:, a:a + 64], T.w1[:]), ["w1"], ["w2.%d" % s])
+            gap()
+            if onward is not None:
+                V(lambda q: q.tensor_scalar(T.ov[:], T.w2[:, a + onward:a + 64:16], 192.0, None, ALU.add), ["w2.%d" % s], ["ov"])
+                gap()
+            moves = [(grp, slot, Q) for grp, slot in found for Q in range(4) if grp > 0 or r == 0]
+            for k, (grp, slot, Q) in enumerate(moves):
+                p, c = 32 * (grp // 2), 16 * (grp % 2) + 4 * Q
+                copy("v" if onward is None and k % 2 else "s", T.coll[p:p + 32, c:c + 4], T.w2[32 * Q:32 * Q + 32, a + slot:a + 64:16],
+                     ["w2.%d" % s], ["coll.%d.%d" % (grp, Q)])
+            if s == 0 and not last:
+                lay_table(r + 1, T["far%d" % (r + 1)][:], "far%d" % (r + 1))
+        V(lambda q: q.transpose(T.lt[:], T.coll[:]), ["coll.%d.%d" % (grp, Q) for grp in range(8) for Q in range(4)], ["lt"])
+        V(lambda q: q.tensor_scalar(T["vl%d" % r][:], T.lt[:, 0:24], 192.0, None, ALU.add), ["lt"], ["vl%d" % r])
+        lists = "vl0" if r == 0 else "vland%d" % r
+        if r > 0:
+            send(r, T[lists][:], T["vl%d" % r][:], "arrl%d" % r, ["vl%d" % r])
+            for b in range(4):
+                unpack(b)
+                larger(b, 0, C)
 
         def pick(e, h, b):
             a, c = PIECES[h]
-            copy(e, T.z[:, 4 * a + b:4 * c:4], T.m[:, C * b:C * b + C].indirect(T["vland%d" % r][:, a // 16:c // 16]),
-                 ["m.%d" % b, "vland%d" % r], ["z.%d.%d" % (b, h)])
+            copy(e, T.z[:, 4 * a + b:4 * c:4], T.m[:, C * b:C * b + C].indirect(T[lists][:, a // 16:c // 16]),
+                 ["m.%d.0" % b, "m.%d.1" % b, lists], ["z.%d.%d" % (b, h)])
 
         def product(h):
             a, c = PIECES[h]
@@ -334,15 +393,16 @@ def rank_program(g, core, T, topo):
         def state(h):
             quantise_state(r + 1, h)
             if last:
-                score(h, T.vq, T.vs, ["vq"])
+                score(r + 1, h, T.vq, T.vs, ["vq"])
             else:
-                score(h, T.uqr, T.usr, ["uqr", "usr"])
+                score(r + 1, h, T.uq, T.us, ["uq"])
 
         def store(h):
             a, c = PIECES[h]
-            dma("y", "st%d" % h, 6, T.oc[:, 4 * a:4 * c], T.xq[:, a:c].bitcast(dt.uint8), ["xq.%d" % h], [])
+            key = ["xq3.%d" % h]
+            dma("y", "st%d" % h, 6, T.oc[:, 4 * a:4 * c], T.xq3[:, a:c].bitcast(dt.uint8), key, [])
             for k in range(4):
-                dma("y", "st%d" % h, 6, T.osc[4 * k:4 * k + 4, a:c], T.xs[32 * k:32 * k + 4, a:c], ["xq.%d" % h], [])
+                dma("y", "st%d" % h, 6, T.osc[4 * k:4 * k + 4, a:c], T.xs3[32 * k:32 * k + 4, a:c], key, [])
 
         def read(h):
             if not last:
@@ -372,12 +432,15 @@ def rank_program(g, core, T, topo):
         add(1, 3)
         for b in range(4):
             scale("s" if b < 3 else "v", 1, b)
+        read(0)
         state(1)
         if last:
             S(lambda q: q.activation(T.plb[:], T.fland[:].indirect(T.vland2[:]), ActivationFunctionType.Identity, bias=192.0),
               ["fland", "vland2"], ["plb"])
             dma("s", "stp", 1, T.pl[:], T.plb[0:128:16, :], ["plb"], [])
             store(1)
-        read(0)
+        else:
+            for t in range(4):
+                lay("s", r + 1, t)
         read(1)
     finish()

@@ -1,8 +1,12 @@
 from concourse.mybir import dt, AluOpType, ActivationFunctionType
 
 C = 384
-PIECES = [(0, 192), (192, 384)]
+PIECES = [(0, 128), (128, 256), (256, 384)]
+HALVES = [(0, C // 2), (C // 2, C)]
+PARTS = [(0, 256), (256, C)]
 STEP = [1, 2, 4]
+ORDER = ("p00s p01s p02v p03v p10s p11s p12v w0 p13v p20s p21s p22s w1 p23v a00 a01 a02 a03 w2 s00s s01s s02s s03s "
+         "a10 a11 a12 a13 s10s s11s s12s s13s q0 a20 a21 a22 a23 s20s s21s q1 s22v s23v r0 q2 e0 r1 r2")
 FIRST = 2
 WALK = [(0, [(1, 0), (0, 8)]), (1, []), (3, [(2, 8), (3, 2), (4, 3)]), (4, []), (None, [(5, 8), (6, 5), (7, 6)])]
 ALU = AluOpType
@@ -20,12 +24,12 @@ SCRATCH = {
     "m": ("sbuf", [128, 4 * C], "bfloat16"), "z": ("sbuf", [128, 4 * C], "bfloat16"),
     "zq": ("sbuf", [128, C], "float8_e4m3fn_x4"), "zs": ("sbuf", [128, C], "uint8"),
     "gli": ("sbuf", [128, 48], "int32"), "glb": ("sbuf", [128, 48], "int32"), "hti": ("sbuf", [128, 24], "int32"),
-    "gt": ("sbuf", [128, 48], "float32"), "gu": ("sbuf", [128, 48], "float32"), "own": ("sbuf", [128, 72], "uint16"),
+    "gt": ("sbuf", [128, 48], "float32"), "gu": ("sbuf", [128, 48], "float32"), "ht16": ("sbuf", [128, 24], "uint16"),
     "bits": ("sbuf", [128, C], "bfloat16"), "bl": ("sbuf", [128, C], "bfloat16"), "bland": ("sbuf", [128, C], "bfloat16"),
     "t1": ("sbuf", [128, C], "float32"), "ft": ("sbuf", [128, C + 32], "bfloat16"), "tab": ("sbuf", [128, 2 * C], "bfloat16"),
     "ta": ("sbuf", [128, C], "bfloat16"), "tb": ("sbuf", [128, C + 32], "bfloat16"), "fl": ("sbuf", [128, 24], "uint16"),
     "fg": ("sbuf", [128, C], "bfloat16"),
-    "gout": ("dram", [128, 48], "int32"), "gin": ("dram", [128, 48], "int32"),
+    "hout": ("dram", [128, 24], "int32"), "hland": ("sbuf", [128, 24], "int32"), "hfar": ("sbuf", [128, 24], "uint16"),
     "fout": ("dram", [128, 24], "bfloat16"), "fin": ("dram", [128, 24], "bfloat16"),
     "upi": ("sbuf", [128, 8], "int32"), "up": ("sbuf", [128, 8], "uint16"),
     "uq0": ("sbuf", [128, 128], "float8_e4m3fn_x4"), "us0": ("sbuf", [128, 128], "uint8"),
@@ -51,11 +55,11 @@ for _r in range(4):
     SCRATCH["xq%d" % _r] = ("sbuf", [128, C], "float8_e4m3fn_x4")
     SCRATCH["xs%d" % _r] = ("sbuf", [128, C], "uint8")
 
-SEMAPHORES = ["cv", "cs", "ct", "cg", "sent", "arrf", "arrb", "fo", "fi", "ld_go", "ld_g2",
-              "ld_gl", "ld_ht", "ld_u", "ld_w", "ld_v", "ld_x0", "ld_x1",
-              "st0", "st1", "st2", "stp"]
+SEMAPHORES = ["cv", "cs", "ct", "cg", "sent", "arrf", "arrb", "fo", "fi", "ld_ho", "arrh",
+              "ld_gl", "ld_ht", "ld_u", "ld_w", "ld_v", "ld_x0", "ld_x1", "ld_x2",
+              "st0", "st1", "st2", "sty0", "sty1", "sts", "stp"]
 for _r in range(3):
-    SEMAPHORES += ["arrq%d" % _r, "arrl%d" % _r, "arrg%d" % _r, "fa%d" % _r, "fb%d" % _r, "fc%d" % _r]
+    SEMAPHORES += ["arrq%d0" % _r, "arrq%d1" % _r, "arrl%d" % _r, "arrg%d" % _r, "fa%d" % _r, "fb%d" % _r, "fc%d" % _r]
 
 
 def tracker(g, T):
@@ -144,19 +148,22 @@ def rank_program(g, core, T, topo):
     partner = [T.cores[rank ^ s] for s in STEP]
     NP = len(PIECES)
 
-    engines = [topo.engines(core, p)[:8] for p in partner]
+    every = [topo.engines(core, p) for p in partner]
+    engines = [e[:8] for e in every]
 
-    def send(r, out, in_, sem, keys):
+    def send(r, out, in_, sem, keys, use=engines):
         before("g", keys)
         rid, pid = topo.addr(partner[r])[:2]
-        g.remote_dma(out, in_, T.sem[sem], T.sem.sent, pid, rid, sum(1 << k for k in engines[r]))
-        total["sent"] = total.get("sent", 0) + len(engines[r])
+        g.remote_dma(out, in_, T.sem[sem], T.sem.sent, pid, rid, sum(1 << k for k in use[r]))
+        total["sent"] = total.get("sent", 0) + len(use[r])
 
     for r in range(3):
-        arrives("arrq%d" % r, 2 * len(engines[r]), ["landq%d" % r])
+        arrives("arrq%d0" % r, 2 * len(every[r]), ["landq%d.0" % r])
+        arrives("arrq%d1" % r, len(every[r]), ["landq%d.1" % r])
         if r > 0:
             arrives("arrl%d" % r, len(engines[r]), ["vland%d" % r])
-            arrives("arrg%d" % r, len(engines[r]), ["far1" if r == 1 else "gin"])
+            arrives("arrg%d" % r, len(engines[r]), ["far%d" % r])
+    arrives("arrh", len(engines[0]), ["hland"])
     arrives("arrb", len(engines[0]), ["bland"])
     arrives("arrf", len(engines[2]), ["fin"])
 
@@ -172,18 +179,14 @@ def rank_program(g, core, T, topo):
     def copy(e, out, in_, r, w):
         op(e, {"v": lambda q: q.tensor_copy(out, in_), "s": lambda q: q.activation(out, in_, COPY)}[e], r, w)
 
-    cut = 4 * PIECES[0][1]
-    def load_table(e, sem, src, keys):
-        dma(e, sem, 3, T.gli[:], src[:], keys, ["gli"])
-        dma(e, sem, 3, T.glb[1:128, :], src[0:127, :], keys, ["glb"])
-        dma(e, sem, 3, T.glb[0:1, :], src[0:1, :], keys, ["glb0"])
-
-    dma("y", "ld_go", 1, T.gout[:], T.gl[:], [], ["gout"])
-    dma("s", "ld_u", 1, T.ut[:], T.u[:], [], ["ut"])
+    dma("y", "ld_ho", 1, T.hout[:], T.ht[:], [], ["hout"])
+    dma("y", "ld_u", 1, T.ut[:], T.u[:], [], ["ut"])
+    for h, (a, b) in enumerate(PIECES):
+        dma("y", "ld_x%d" % h, 1, T.x_0[:, 4 * a:4 * b], T.x[:, 4 * a:4 * b], [], piece("x_0", h))
     dma("y", "ld_ht", 1, T.hti[:], T.ht[:], [], ["hti"])
-    dma("s", "ld_x0", 1, T.x_0[:, 0:cut], T.x[:, 0:cut], [], piece("x_0", 0))
-    dma("y", "ld_x1", 1, T.x_0[:, cut:], T.x[:, cut:], [], [k for h in range(1, NP) for k in piece("x_0", h)])
-    load_table("y", "ld_gl", T.gl, [])
+    dma("y", "ld_gl", 3, T.gli[:], T.gl[:], [], ["gli"])
+    dma("y", "ld_gl", 3, T.glb[1:128, :], T.gl[0:127, :], [], ["glb"])
+    dma("y", "ld_gl", 3, T.glb[0:1, :], T.gl[0:1, :], [], ["glb0"])
 
     op("g", lambda q: q.iota(T.upi[:], [[16, 8]], 0, 0), [], ["upi"])
     op("g", lambda q: q.iota(T.ip[:], [[0, 1]], 0, 1), [], ["ip"])
@@ -192,7 +195,7 @@ def rank_program(g, core, T, topo):
     for k in (1, 2):
         S(lambda q: q.activation(T.ident[:, 256 * k:256 * k + 256], T.ident[:, 0:256], COPY, bias=256.0 * k), ["ident.0"], ["ident.%d" % k])
     ik = ["ident.%d" % k for k in range(3)]
-    send(2, T.gin[:], T.gout[:], "arrg2", ["gout"])
+    send(0, T.hland[:], T.hout[:], "arrh", ["hout"])
     V(lambda q: q.memset(T.e0[:], 1.0), [], ["e0"])
     V(lambda q: q.memset(T.fland[:], 0.0), [], ["fland"])
     V(lambda q: q.memset(T.ft[:, 0:16], 0.0), [], ["pad0"])
@@ -210,20 +213,18 @@ def rank_program(g, core, T, topo):
     V(lambda q: q.tensor_scalar(T.fa[:, 2:3], T.ia[:, 2:3], T.fa[:, 1:2], None, ALU.add), ["ia2", "fa1"], ["fa2"])
     V(lambda q: q.tensor_scalar(T.ov0[:], T.kcol[:], T.fa[:, 2:3], float(C - 1), ALU.add, ALU.min), ["kcol", "fa2"], ["ov0"])
 
-    def places(out, key):
-        V(lambda q: q.tensor_scalar(T.gt[:], T.glb[:], T.fa[:, 3:4], T.fa[:, 4:5], ALU.mult, ALU.add), ["glb", "glb0", "fa3", "fa4"], ["gt"])
-        V(lambda q: q.tensor_tensor(T.gu[:], T.gt[:], T.gli[:], ALU.add), ["gt", "gli"], ["gu"])
-        V(lambda q: q.tensor_copy(out, T.gu[:]), ["gu"], [key])
-
     V(lambda q: q.quantize_mx(T.uq0[:], T.us0[:], T.ut[:]), ["ut"], ["uq0"])
     V(lambda q: q.tensor_copy(T.uq[:].bitcast(dt.uint32), T.uq0[:].bitcast(dt.uint32).indirect(T.up[:])), ["uq0", "up"], ["uq"])
     copy("s", T.us[:], T.us0[:].indirect(T.up[:]), ["uq0", "up"], ["us"])
-    for t in range(4):
-        V(lambda q: q.tensor_scalar(T.ht4[:, 24 * t:24 * t + 24], T.hti[:], 4.0, float(t), ALU.mult, ALU.add), ["hti"], ["ht4.%d" % t])
-    V(lambda q: q.tensor_copy(T.own[:, 48:72], T.hti[:]), ["hti"], ["ht16"])
 
     def bank(h):
         return (T.psb, "psb") if h % 2 == 0 else (T.psa, "psa")
+
+    def score_bank(h):
+        a, b = PIECES[h]
+        ps, pn = bank(NP - 2 if h < NP - 1 else NP - 1)
+        k = h if h < NP - 1 else 0
+        return ps[:, 512 * k:512 * k + b - a], "%s.%d" % (pn, k)
 
     def quantise_state(r, h):
         a, b = PIECES[h]
@@ -232,27 +233,35 @@ def rank_program(g, core, T, topo):
 
     def score(r, h, wq, ws, keys):
         a, b = PIECES[h]
-        ps, pn = bank(h)
-        op("t", lambda q: q.matmul_mx(ps[:, 0:b - a], wq[:], ws[:], T["xq%d" % r][:, a:b], T["xs%d" % r][:, a:b], True, True),
-           keys + ["xq%d.%d" % (r, h)], [pn + ".0"])
+        ps, pn = score_bank(h)
+        op("t", lambda q: q.matmul_mx(ps, wq[:], ws[:], T["xq%d" % r][:, a:b], T["xs%d" % r][:, a:b], True, True),
+           keys + ["xq%d.%d" % (r, h)], [pn])
 
-    def signs(h):
+    def signs(h, out):
         a, b = PIECES[h]
-        ps, pn = bank(h)
-        V(lambda q: q.tensor_scalar(T.bits[:, a:b], ps[:, 0:b - a], 0.0, None, ALU.is_gt), [pn + ".0"], ["bits.%d" % h])
+        ps, pn = score_bank(h)
+        V(lambda q: q.tensor_scalar(out[:, a:b], ps, 0.0, None, ALU.is_gt), [pn], ["bits.%d" % h])
 
-    def lay_table(r, at, key):
-        copy("s", T["glf%d" % r][:], T.ident[:].indirect(at), ik + [key], ["glf%d" % r])
+    def lay_table(r):
+        copy("s", T["glf%d" % r][:], T.ident[:].indirect(T["far%d" % r][:]), ik + ["far%d" % r], ["glf%d" % r])
 
     def lay(e, r, t):
-        copy(e, T.lx[:, t:4 * C:4], T["x_%d" % r][:].indirect(T.ht4[:, 24 * t:24 * t + 24]), whole("x_%d" % r) + ["ht4.%d" % t],
-             ["lx.%d" % t])
+        out, at = T.lx[:, t:4 * C:4], T.ht4[:, 24 * t:24 * t + 24]
+        if r == 0:
+            copy(e, out, T.x_0[:].indirect(at), whole("x_0") + ["ht4.%d" % t], ["lx.%d" % t])
+        else:
+            S(lambda q: q.activation(out, T.x64[:].indirect(at), COPY, scale=0.015625), whole("x64") + ["ht4.%d" % t], ["lx.%d" % t])
+
+    def quantise_laid(r, k):
+        a, c = PARTS[k]
+        V(lambda q: q.quantize_mx(T["lq%d" % r][:, a:c], T["ls%d" % r][:, a:c], T.lx[:, 4 * a:4 * c]), ["lx.%d" % t for t in range(4)],
+          ["lq%d.%d" % (r, k)])
 
     def send_laid(r, after):
         lq, ls = T["lq%d" % r], T["ls%d" % r]
-        V(lambda q: q.quantize_mx(lq[:], ls[:], T.lx[:]), ["lx.%d" % t for t in range(4)], ["lq%d" % r])
-        send(r, T["landq%d" % r][:].bitcast(dt.uint8), lq[:].bitcast(dt.uint8), "arrq%d" % r, ["lq%d" % r] + after)
-        send(r, T["lands%d" % r][:], ls[:], "arrq%d" % r, ["lq%d" % r])
+        send(r, T["lands%d" % r][:], ls[:], "arrq%d0" % r, ["lq%d.0" % r, "lq%d.1" % r] + after, every)
+        for k, (a, c) in enumerate(PARTS):
+            send(r, T["landq%d" % r][:, a:c].bitcast(dt.uint8), lq[:, a:c].bitcast(dt.uint8), "arrq%d%d" % (r, k), [], every)
 
     def constants(codes, scales, tile, keys, name):
         for b in range(4):
@@ -262,43 +271,60 @@ def rank_program(g, core, T, topo):
     for h in range(NP):
         quantise_state(0, h)
         score(0, h, T.uq, T.us, ["uq", "us"])
-    for t in range(3):
+    for t in range(4):
+        V(lambda q: q.tensor_scalar(T.ht4[:, 24 * t:24 * t + 24], T.hti[:], 4.0, float(t), ALU.mult, ALU.add), ["hti"], ["ht4.%d" % t])
+    for t in range(2):
         lay("s", 0, t)
     for h in range(NP):
-        signs(h)
+        signs(h, T.bl)
+    V(lambda q: q.tensor_copy(T.ht16[:], T.hti[:]), ["hti"], ["ht16"])
 
     for r in range(3):
         last = r == 2
         xn, X, Y = "x_%d" % r, T["x_%d" % r], T["x_%d" % (r + 1)]
-        signed, sk = T.bits[:].indirect(T.own[:, 48:72]), ["bits.%d" % h for h in range(NP)] + ["ht16"]
+        sk = ["bits.%d" % h for h in range(NP)]
         tk = ["tab.%d" % s for s in range(7)]
         glf, gk = T["glf%d" % r], ["glf%d" % r]
 
-        def unpack(b):
-            op("t", lambda q: q.matmul_mx(T.psa[:, 512 * b:512 * b + C], T.eq[:, 128 * b:128 * b + 128], T.es[:, 128 * b:128 * b + 128],
-                                          T["landq%d" % r][:], T["lands%d" % r][:], True, True), ["eq.%d" % b, "landq%d" % r], ["psa.%d" % b])
+        def unpack(k, b):
+            a, c = PARTS[k]
+            ps, pn = bank(k)
+            op("t", lambda q: q.matmul_mx(ps[:, 512 * b:512 * b + c - a], T.eq[:, 128 * b:128 * b + 128], T.es[:, 128 * b:128 * b + 128],
+                                          T["landq%d" % r][:, a:c], T["lands%d" % r][:, a:c], True, True),
+               ["eq.%d" % b, "landq%d.0" % r, "landq%d.%d" % (r, k)], ["%s.%d" % (pn, b)])
 
         def larger(b, a, c):
-            V(lambda q: q.tensor_tensor(T.m[:, C * b + a:C * b + c], T.psa[:, 512 * b + a:512 * b + c], X[:, 4 * a + b:4 * c:4], ALU.max),
-              ["psa.%d" % b] + whole(xn), ["m.%d.%d" % (b, k) for k in range(2 * a // C, 2 * c // C)])
+            k = 0 if a < PARTS[1][0] else 1
+            ps, pn = bank(k)
+            at = 512 * b - PARTS[k][0]
+            V(lambda q: q.tensor_tensor(T.m[:, C * b + a:C * b + c], ps[:, at + a:at + c], X[:, 4 * a + b:4 * c:4], ALU.max),
+              ["%s.%d" % (pn, b)] + whole(xn), ["m.%d.%d" % (b, j) for j in range(a // 128, c // 128)])
 
+        sign, host, keys = T.bits, T.ht16, sk + ["ht16"]
         if r == 0:
-            V(lambda q: q.tensor_copy(T.bl[:], signed), sk, ["bl"])
-            send(r, T.bland[:], T.bl[:], "arrb", ["bl"])
+            sign, host, keys = T.bland, T.hfar, ["bland", "hfar"]
+            send(r, T.bland[:], T.bl[:], "arrb", sk)
             op("g", lambda q: q.affine_select(T.et[:], T.e0[:], [[1, 516]], ALU.is_equal, 0.0, -3, -4), ["e0"], ["et"])
-            places(T.own[:, 0:48], "gl16")
-            lay_table(0, T.own[:, 0:48], "gl16")
-            lay("v", r, 3)
+            V(lambda q: q.tensor_scalar(T.gt[:], T.glb[:], T.fa[:, 3:4], T.fa[:, 4:5], ALU.mult, ALU.add), ["glb", "glb0", "fa3", "fa4"], ["gt"])
+            lay("v", 0, 2)
+            V(lambda q: q.tensor_tensor(T.gu[:], T.gt[:], T.gli[:], ALU.add), ["gt", "gli"], ["gu"])
+            lay("v", 0, 3)
+            V(lambda q: q.tensor_copy(T.far0[:], T.gu[:]), ["gu"], ["far0"])
+            lay_table(0)
+            send(1, T.far1[:], T.far0[:], "arrg1", ["far0"])
+            for k in range(2):
+                quantise_laid(r, k)
             send_laid(r, [])
-            send(1, T.far1[:], T.own[:, 0:48], "arrg1", ["gl16"])
             for w in range(2):
                 copy("v", T.tab[:, C * w:C * w + C], T.ident[:, 191:191 + C], ik, tk[:FIRST] if w == 0 else tk[FIRST:])
-            constants(T.eq, T.es, T.et, ["et"], "eq")
+            V(lambda q: q.tensor_copy(T.hfar[:], T.hland[:]), ["hland"], ["hfar"])
             S(lambda q: q.activation(T.x64[:], T.x_0[:], COPY, scale=64.0), whole("x_0"), whole("x64"))
-            V(lambda q: q.tensor_tensor(T.t1[:], T.bland[:], glf[:, 1:2 * C:2], ALU.mult), ["bland"] + gk, ["t1"])
-        else:
-            V(lambda q: q.tensor_tensor(T.t1[:], signed, glf[:, 1:2 * C:2], ALU.mult), sk + gk, ["t1"])
-        V(lambda q: q.tensor_tensor(T.ft[:, 16:16 + C], T.t1[:], glf[:, 0:2 * C:2], ALU.add), ["t1"] + gk, ["ft"])
+        for a, c in HALVES:
+            V(lambda q: q.tensor_tensor(T.t1[:, a:c], sign[:].indirect(host[:, a // 16:c // 16]), glf[:, 2 * a + 1:2 * c:2], ALU.mult),
+              keys + gk, ["t1.%d" % a])
+        for a, c in HALVES:
+            V(lambda q: q.tensor_tensor(T.ft[:, 16 + a:16 + c], T.t1[:, a:c], glf[:, 2 * a:2 * c:2], ALU.add), ["t1.%d" % a] + gk,
+              ["ft0" if a == 0 else "ft"])
 
         def spread(s, key, a, sem, n):
             w = 0 if s < FIRST else C
@@ -307,12 +333,19 @@ def rank_program(g, core, T, topo):
             spread(s, "ft", 16, "fa%d" % r, 2)
         for s in (2, 4, 5):
             spread(s, "ft", 16, "fb%d" % r, 3)
-        V(lambda q: q.transpose(T.ta[:], T.ft[:, 16:16 + C]), ["ft"], ["ta"])
-        V(lambda q: q.transpose(T.tb[:], T.ft[:]), ["ft", "pad0", "pad1"], ["tb"])
+        V(lambda q: q.transpose(T.ta[:, 0:C // 2], T.ft[:, 16:16 + C // 2]), ["ft0"], ["ta0"])
+        V(lambda q: q.transpose(T.tb[:, 0:C // 2], T.ft[:, 0:C // 2]), ["ft0", "pad0"], ["tb0"])
+        V(lambda q: q.transpose(T.ta[:, C // 2:], T.ft[:, 16 + C // 2:16 + C]), ["ft"], ["ta"])
+        V(lambda q: q.transpose(T.tb[:, C // 2:], T.ft[:, C // 2:]), ["ft", "pad1"], ["tb"])
         for k, (out, in_) in enumerate(((T.fl[32:64, 1:24:2], T.ta[32:64, 0:C:32]), (T.fl[96:128, 0:24:2], T.ta[64:96, 16:C:32]),
                                         (T.fl[32:64, 0:24:2], T.tb[32:64, 0:C:32]), (T.fl[96:128, 1:24:2], T.tb[64:96, 48:C + 32:32]))):
             V(lambda q: q.tensor_scalar(out, in_, 192.0, None, ALU.add), ["ta" if k < 2 else "tb"], ["fl.%d" % k])
-        copy("s", T.fg[:], T.ft[:, 16:16 + C].indirect(T.fl[:]), ["ft", "fl"] + ["fl.%d" % k for k in range(4)], ["fg"])
+        if r > 0:
+            quantise_laid(r, 0)
+        for e, (a, c) in zip("vs", HALVES):
+            copy(e, T.fg[:, a:c], T.ft[:, 16:16 + C].indirect(T.fl[:, a // 16:c // 16]), ["ft", "fl"] + ["fl.%d" % k for k in range(4)],
+                 ["fg" if a else "fg0"])
+        before("y", ["fg0"])
         for s in (3, 6):
             spread(s, "fg", 0, "fc%d" % r, 2)
         fill = []
@@ -320,14 +353,15 @@ def rank_program(g, core, T, topo):
             dma("y", "ld_w", 2, T.wq[:].bitcast(dt.uint8), T.wc[:], tk, ["wq"])
             dma("y", "ld_w", 2, T.wsp[:], T.ws[:], [], ["wsp"])
             dma("y", "ld_v", 1, T.vt[:], T.v[:], [], ["vt"])
-            load_table("y", "ld_g2", T.gin, ["gin"])
-            for b in range(4):
-                unpack(b)
-                fill += [lambda b=b: larger(b, 0, C // 2), lambda b=b: larger(b, C // 2, C)]
+            send(2, T.far2[:], T.far0[:], "arrg2", ["fg0", "fg"])
+            constants(T.eq, T.es, T.et, ["et"], "eq")
+            for k in range(2):
+                for b in range(4):
+                    unpack(k, b)
+            fill += 2 * [lambda: None] + [lambda b=b, a=a, c=c: larger(b, a, c) for a, c in PIECES for b in range(4)]
         else:
-            send_laid(r, ["fg"])
-        if r == 1:
-            places(T.far2[:], "far2")
+            quantise_laid(r, 1)
+            send_laid(r, ["fg0", "fg"])
         if last:
             dma("y", "fo", 1, T.fout[:], T.ft[0:128:16, 16:16 + C], ["ft"], ["fout"])
             send(r, T.fin[:], T.fout[:], "arrf", ["fout"])
@@ -335,7 +369,7 @@ def rank_program(g, core, T, topo):
             fill.append(lambda: V(lambda q: q.quantize_mx(T.vq[:], T.vs[:], T.vt[:]), ["vt"], ["vq"]))
         for s, (onward, found) in enumerate(WALK):
             def gap():
-                if s > 0 and fill:
+                if fill:
                     fill.pop(0)()
             o, ok = (T.ov0, "ov0") if s == 0 else (T.ov, "ov")
             a = 64 * s
@@ -353,20 +387,21 @@ def rank_program(g, core, T, topo):
                 copy("v" if onward is None and k % 2 else "s", T.coll[p:p + 32, c:c + 4], T.w2[32 * Q:32 * Q + 32, a + slot:a + 64:16],
                      ["w2.%d" % s], ["coll.%d.%d" % (grp, Q)])
             if s == 0 and not last:
-                lay_table(r + 1, T["far%d" % (r + 1)][:], "far%d" % (r + 1))
+                lay_table(r + 1)
         V(lambda q: q.transpose(T.lt[:], T.coll[:]), ["coll.%d.%d" % (grp, Q) for grp in range(8) for Q in range(4)], ["lt"])
         V(lambda q: q.tensor_scalar(T["vl%d" % r][:], T.lt[:, 0:24], 192.0, None, ALU.add), ["lt"], ["vl%d" % r])
         lists = "vl0" if r == 0 else "vland%d" % r
         if r > 0:
             send(r, T[lists][:], T["vl%d" % r][:], "arrl%d" % r, ["vl%d" % r])
-            for b in range(4):
-                unpack(b)
-                larger(b, 0, C)
+            for k in range(2):
+                for b in range(4):
+                    unpack(k, b)
+                    larger(b, *PARTS[k])
 
         def pick(e, h, b):
             a, c = PIECES[h]
             copy(e, T.z[:, 4 * a + b:4 * c:4], T.m[:, C * b:C * b + C].indirect(T[lists][:, a // 16:c // 16]),
-                 ["m.%d.0" % b, "m.%d.1" % b, lists], ["z.%d.%d" % (b, h)])
+                 ["m.%d.%d" % (b, j) for j in range(3)] + [lists], ["z.%d.%d" % (b, h)])
 
         def product(h):
             a, c = PIECES[h]
@@ -394,53 +429,44 @@ def rank_program(g, core, T, topo):
             quantise_state(r + 1, h)
             if last:
                 score(r + 1, h, T.vq, T.vs, ["vq"])
+                store(h)
             else:
                 score(r + 1, h, T.uq, T.us, ["uq"])
 
         def store(h):
             a, c = PIECES[h]
-            key = ["xq3.%d" % h]
-            dma("y", "st%d" % h, 6, T.oc[:, 4 * a:4 * c], T.xq3[:, a:c].bitcast(dt.uint8), key, [])
-            for k in range(4):
-                dma("y", "st%d" % h, 6, T.osc[4 * k:4 * k + 4, a:c], T.xs3[32 * k:32 * k + 4, a:c], key, [])
+            dma("y", "st%d" % h, 1, T.oc[:, 4 * a:4 * c], T.xq3[:, a:c].bitcast(dt.uint8), ["xq3.%d" % h], [])
+
 
         def read(h):
             if not last:
-                return signs(h)
+                return signs(h, T.bits)
             a, c = PIECES[h]
-            ps, pn = bank(h)
-            copy("v", T.ysb[:, a:c], ps[:, 0:c - a], [pn + ".0"], ["ysb.%d" % h])
-            dma("s", "st%d" % h, 6, T.y[:, a:c], T.ysb[:, a:c], ["ysb.%d" % h], [])
+            ps, pn = score_bank(h)
+            copy("v", T.ysb[:, a:c], ps, [pn], ["ysb.%d" % h])
+            if h != NP - 2:
+                a = PIECES[max(h - 1, 0)][0]
+                dma("y", "sty%d" % min(h, 1), 1, T.y[:, a:c], T.ysb[:, a:c], ["ysb.%d" % max(h - 1, 0), "ysb.%d" % h], [])
 
-        for b in range(4):
-            pick("sv"[b // 2], 0, b)
-        product(0)
-        for b in range(4):
-            pick("v" if b == 0 else "s", 1, b)
-        for b in range(3):
-            add(0, b)
-        product(1)
-        add(0, 3)
-        for b in range(4):
-            scale("s", 0, b)
-        add(1, 0)
-        add(1, 1)
-        state(0)
-        if last:
-            store(0)
-        add(1, 2)
-        add(1, 3)
-        for b in range(4):
-            scale("s" if b < 3 else "v", 1, b)
-        read(0)
-        state(1)
-        if last:
-            S(lambda q: q.activation(T.plb[:], T.fland[:].indirect(T.vland2[:]), ActivationFunctionType.Identity, bias=192.0),
-              ["fland", "vland2"], ["plb"])
-            dma("s", "stp", 1, T.pl[:], T.plb[0:128:16, :], ["plb"], [])
-            store(1)
-        else:
-            for t in range(4):
-                lay("s", r + 1, t)
-        read(1)
+        def rest():
+            if last:
+                S(lambda q: q.activation(T.plb[:], T.fland[:].indirect(T.vland2[:]), ActivationFunctionType.Identity, bias=192.0),
+                  ["fland", "vland2"], ["plb"])
+                for k in range(4):
+                    dma("s", "sts", 4, T.osc[4 * k:4 * k + 4, :], T.xs3[32 * k:32 * k + 4, :], ["xq3.%d" % j for j in range(NP)], [])
+                dma("s", "stp", 1, T.pl[:], T.plb[0:128:16, :], ["plb"], [])
+            else:
+                for t in range(4):
+                    lay("s", r + 1, t)
+
+        for word in ORDER.split():
+            kind, h, more = word[0], int(word[1]), word[2:]
+            if kind == "p":
+                pick(more[1], h, int(more[0]))
+            elif kind == "a":
+                add(h, int(more))
+            elif kind == "s":
+                scale(more[1], h, int(more[0]))
+            else:
+                {"w": product, "q": state, "r": read, "e": lambda h: rest()}[kind](h)
     finish()

@@ -4,11 +4,13 @@ C = 384
 PIECES = [(0, 128), (128, 256), (256, 384)]
 HALVES = [(0, C // 2), (C // 2, C)]
 PARTS = [(0, 256), (256, C)]
+SENT = [(0, 304), (304, C)]
+UNPACKED = [(0, 304), (256, C)]
 STEP = [1, 2, 4]
 ORDER = ("p00s p01s p02v p03v p10s p11s p12v w0 p13v p20s p21s p22s w1 p23v a00 a01 a02 a03 w2 s00s s01s s02s s03s "
          "a10 a11 a12 a13 s10s s11s s12s s13s q0 a20 a21 a22 a23 s20s s21s q1 s22v s23v r0 q2 e0 r1 r2")
-FIRST = 2
-WALK = [(0, [(1, 0), (0, 8)]), (1, []), (3, [(2, 8), (3, 2), (4, 3)]), (4, []), (None, [(5, 8), (6, 5), (7, 6)])]
+WINDOW = [0, 1, 1, 2, 2, 3, 3]
+WALK = [(0, []), (2, [(1, 8), (2, 1), (3, 2)]), (4, []), (None, [(5, 8), (6, 5), (7, 6)])]
 ALU = AluOpType
 COPY = ActivationFunctionType.Copy
 
@@ -26,13 +28,14 @@ SCRATCH = {
     "gli": ("sbuf", [128, 48], "int32"), "glb": ("sbuf", [128, 48], "int32"), "hti": ("sbuf", [128, 24], "int32"),
     "gt": ("sbuf", [128, 48], "float32"), "gu": ("sbuf", [128, 48], "float32"), "ht16": ("sbuf", [128, 24], "uint16"),
     "bits": ("sbuf", [128, C], "bfloat16"), "bl": ("sbuf", [128, C], "bfloat16"), "bland": ("sbuf", [128, C], "bfloat16"),
-    "t1": ("sbuf", [128, C], "float32"), "ft": ("sbuf", [128, C + 32], "bfloat16"), "tab": ("sbuf", [128, 2 * C], "bfloat16"),
+    "t1": ("sbuf", [128, C], "float32"), "ft": ("sbuf", [128, C + 32], "bfloat16"), "tab": ("sbuf", [128, 5 * C], "bfloat16"),
     "ta": ("sbuf", [128, C], "bfloat16"), "tb": ("sbuf", [128, C + 32], "bfloat16"), "fl": ("sbuf", [128, 24], "uint16"),
-    "fg": ("sbuf", [128, C], "bfloat16"),
+    "fg": ("sbuf", [128, C], "bfloat16"), "fh": ("sbuf", [128, C], "bfloat16"), "fm": ("sbuf", [128, 24], "uint16"),
     "hout": ("dram", [128, 24], "int32"), "hland": ("sbuf", [128, 24], "int32"), "hfar": ("sbuf", [128, 24], "uint16"),
     "fout": ("dram", [128, 24], "bfloat16"), "fin": ("dram", [128, 24], "bfloat16"),
     "upi": ("sbuf", [128, 8], "int32"), "up": ("sbuf", [128, 8], "uint16"),
     "uq0": ("sbuf", [128, 128], "float8_e4m3fn_x4"), "us0": ("sbuf", [128, 128], "uint8"),
+    "w3": ("sbuf", [128, 64], "bfloat16"), "ov4": ("sbuf", [128, 4], "uint16"), "j0": ("sbuf", [128, 4], "float32"),
     "w1": ("sbuf", [128, 64], "bfloat16"), "w2": ("sbuf", [128, 7 * 64], "bfloat16"),
     "coll": ("sbuf", [128, 32], "bfloat16"), "lt": ("sbuf", [128, 32], "bfloat16"),
     "ov0": ("sbuf", [128, 4], "uint16"), "ov": ("sbuf", [128, 4], "uint16"),
@@ -59,7 +62,7 @@ SEMAPHORES = ["cv", "cs", "ct", "cg", "sent", "arrf", "arrb", "fo", "fi", "ld_ho
               "ld_gl", "ld_ht", "ld_u", "ld_w", "ld_v", "ld_x0", "ld_x1", "ld_x2",
               "st0", "st1", "st2", "sty0", "sty1", "sts", "stp"]
 for _r in range(3):
-    SEMAPHORES += ["arrq%d0" % _r, "arrq%d1" % _r, "arrl%d" % _r, "arrg%d" % _r, "fa%d" % _r, "fb%d" % _r, "fc%d" % _r]
+    SEMAPHORES += ["arrq%d0" % _r, "arrq%d1" % _r, "arrl%d" % _r, "arrg%d" % _r] + ["f%d%d" % (_r, _s) for _s in range(7)]
 
 
 def tracker(g, T):
@@ -181,41 +184,57 @@ def rank_program(g, core, T, topo):
 
     dma("y", "ld_ho", 1, T.hout[:], T.ht[:], [], ["hout"])
     dma("y", "ld_u", 1, T.ut[:], T.u[:], [], ["ut"])
-    for h, (a, b) in enumerate(PIECES):
-        dma("y", "ld_x%d" % h, 1, T.x_0[:, 4 * a:4 * b], T.x[:, 4 * a:4 * b], [], piece("x_0", h))
     dma("y", "ld_ht", 1, T.hti[:], T.ht[:], [], ["hti"])
+    cut = 4 * PIECES[-1][0]
+    dma("y", "ld_x0", 1, T.x_0[:, 0:cut], T.x[:, 0:cut], [], [k for h in range(NP - 1) for k in piece("x_0", h)])
+    dma("y", "ld_x1", 1, T.x_0[:, cut:], T.x[:, cut:], [], piece("x_0", NP - 1))
     dma("y", "ld_gl", 3, T.gli[:], T.gl[:], [], ["gli"])
     dma("y", "ld_gl", 3, T.glb[1:128, :], T.gl[0:127, :], [], ["glb"])
     dma("y", "ld_gl", 3, T.glb[0:1, :], T.gl[0:1, :], [], ["glb0"])
+    dma("y", "ld_w", 2, T.wq[:].bitcast(dt.uint8), T.wc[:], [], ["wq"])
 
     op("g", lambda q: q.iota(T.upi[:], [[16, 8]], 0, 0), [], ["upi"])
     op("g", lambda q: q.iota(T.ip[:], [[0, 1]], 0, 1), [], ["ip"])
-    op("g", lambda q: q.iota(T.kcol[:], [[2, 2], [256, 2]], 0, 0, allow_small_or_imprecise_dtypes=True), [], ["kcol"])
+    op("g", lambda q: q.iota(T.kcol[:], [[1, 4]], 0, 0, allow_small_or_imprecise_dtypes=True), [], ["kcol"])
     op("g", lambda q: q.iota(T.ident[:, 0:256], [[1, 256]], 1 - C, 0, allow_small_or_imprecise_dtypes=True), [], ["ident.0"])
     for k in (1, 2):
         S(lambda q: q.activation(T.ident[:, 256 * k:256 * k + 256], T.ident[:, 0:256], COPY, bias=256.0 * k), ["ident.0"], ["ident.%d" % k])
     ik = ["ident.%d" % k for k in range(3)]
-    send(0, T.hland[:], T.hout[:], "arrh", ["hout"])
     V(lambda q: q.memset(T.e0[:], 1.0), [], ["e0"])
+    send(0, T.hland[:], T.hout[:], "arrh", ["hout"])
+    tk = ["tab.%d" % s for s in range(7)]
+
+    def window(w):
+        return [tk[s] for s in range(7) if WINDOW[s] == w]
+
+    def identity(w):
+        copy("s", T.tab[:, C * w:C * w + C], T.ident[:, 191:191 + C], ik, window(w))
+    identity(1)
+    identity(3)
+    for w in (0, 2):
+        V(lambda q: q.memset(T.tab[:, C * w:C * w + C], 0.0), [], window(w))
     V(lambda q: q.memset(T.fland[:], 0.0), [], ["fland"])
     V(lambda q: q.memset(T.ft[:, 0:16], 0.0), [], ["pad0"])
     V(lambda q: q.memset(T.ft[:, 16 + C:], 0.0), [], ["pad1"])
-    V(lambda q: q.memset(T.fl[:], 0), [], ["fl"] + ["fl.%d" % k for k in range(4)])
+    V(lambda q: q.memset(T.fm[:], 0), [], ["fl.%d" % k for k in range(2, 6)])
+    V(lambda q: q.memset(T.fl[:], 0), [], ["fl", "fl.0", "fl.1"])
     V(lambda q: q.tensor_copy(T.up[:], T.upi[:]), ["upi"], ["up"])
     V(lambda q: q.tensor_scalar(T.ia[:, 3:4], T.ip[:], 1, None, ALU.bitwise_and), ["ip"], ["ia3"])
-    V(lambda q: q.tensor_scalar(T.ia[:, 0:1], T.ip[:], 15, None, ALU.bitwise_and), ["ip"], ["ia0"])
+    V(lambda q: q.tensor_scalar(T.ia[:, 0:1], T.ip[:], 31, None, ALU.bitwise_and), ["ip"], ["ia0"])
     V(lambda q: q.tensor_scalar(T.ia[:, 1:2], T.ip[:], 5, None, ALU.arith_shift_right), ["ip"], ["ia1"])
-    V(lambda q: q.tensor_scalar(T.ia[:, 2:3], T.ip[:], 4, 1, ALU.arith_shift_right, ALU.bitwise_and), ["ip"], ["ia2"])
     V(lambda q: q.tensor_scalar(T.fa[:, 3:4], T.ia[:, 3:4], -1.0, None, ALU.mult), ["ia3"], ["fa3"])
     V(lambda q: q.tensor_scalar(T.fa[:, 4:5], T.ia[:, 3:4], 192.0, 191.0, ALU.mult, ALU.add), ["ia3"], ["fa4"])
     V(lambda q: q.tensor_scalar(T.fa[:, 0:1], T.ia[:, 0:1], 16.0, None, ALU.mult), ["ia0"], ["fa0"])
     V(lambda q: q.tensor_scalar(T.fa[:, 1:2], T.ia[:, 1:2], 4.0, T.fa[:, 0:1], ALU.mult, ALU.add), ["ia1", "fa0"], ["fa1"])
-    V(lambda q: q.tensor_scalar(T.fa[:, 2:3], T.ia[:, 2:3], T.fa[:, 1:2], None, ALU.add), ["ia2", "fa1"], ["fa2"])
-    V(lambda q: q.tensor_scalar(T.ov0[:], T.kcol[:], T.fa[:, 2:3], float(C - 1), ALU.add, ALU.min), ["kcol", "fa2"], ["ov0"])
+    V(lambda q: q.tensor_scalar(T.ov0[:], T.kcol[:], T.fa[:, 1:2], float(C - 1), ALU.add, ALU.min), ["kcol", "fa1"], ["ov0"])
+    V(lambda q: q.tensor_scalar(T.j0[:], T.kcol[:], T.fa[:, 1:2], float(C - 1), ALU.add, ALU.min), ["kcol", "fa1"], ["j0"])
 
     V(lambda q: q.quantize_mx(T.uq0[:], T.us0[:], T.ut[:]), ["ut"], ["uq0"])
     V(lambda q: q.tensor_copy(T.uq[:].bitcast(dt.uint32), T.uq0[:].bitcast(dt.uint32).indirect(T.up[:])), ["uq0", "up"], ["uq"])
     copy("s", T.us[:], T.us0[:].indirect(T.up[:]), ["uq0", "up"], ["us"])
+    S(lambda q: q.activation(T.w2[:, 0:64:16], T.j0[:], COPY, bias=-192.0), ["j0"], ["w2.0"])
+    for Q in range(4):
+        copy("s", T.coll[0:32, 4 * Q:4 * Q + 4], T.w2[32 * Q:32 * Q + 32, 0:64:16], ["w2.0"], ["coll.0.%d" % Q])
 
     def bank(h):
         return (T.psb, "psb") if h % 2 == 0 else (T.psa, "psa")
@@ -245,22 +264,24 @@ def rank_program(g, core, T, topo):
     def lay_table(r):
         copy("s", T["glf%d" % r][:], T.ident[:].indirect(T["far%d" % r][:]), ik + ["far%d" % r], ["glf%d" % r])
 
-    def lay(e, r, t):
-        out, at = T.lx[:, t:4 * C:4], T.ht4[:, 24 * t:24 * t + 24]
+    def lay(e, r, t, a=0, c=C):
+        out, at = T.lx[:, 4 * a + t:4 * c:4], T.ht4[:, 24 * t + a // 16:24 * t + c // 16]
         if r == 0:
-            copy(e, out, T.x_0[:].indirect(at), whole("x_0") + ["ht4.%d" % t], ["lx.%d" % t])
+            copy(e, out, T.x_0[:].indirect(at), whole("x_0") + ["ht4.%d" % t], ["lx.%d" % t if a == 0 else "lx.4"])
+        elif e == "v":
+            copy(e, out, T["x_%d" % r][:].indirect(at), whole("x_%d" % r) + ["ht4.%d" % t], ["lx.4"])
         else:
             S(lambda q: q.activation(out, T.x64[:].indirect(at), COPY, scale=0.015625), whole("x64") + ["ht4.%d" % t], ["lx.%d" % t])
 
     def quantise_laid(r, k):
         a, c = PARTS[k]
-        V(lambda q: q.quantize_mx(T["lq%d" % r][:, a:c], T["ls%d" % r][:, a:c], T.lx[:, 4 * a:4 * c]), ["lx.%d" % t for t in range(4)],
+        V(lambda q: q.quantize_mx(T["lq%d" % r][:, a:c], T["ls%d" % r][:, a:c], T.lx[:, 4 * a:4 * c]), ["lx.%d" % t for t in range(5)],
           ["lq%d.%d" % (r, k)])
 
     def send_laid(r, after):
         lq, ls = T["lq%d" % r], T["ls%d" % r]
         send(r, T["lands%d" % r][:], ls[:], "arrq%d0" % r, ["lq%d.0" % r, "lq%d.1" % r] + after, every)
-        for k, (a, c) in enumerate(PARTS):
+        for k, (a, c) in enumerate(SENT):
             send(r, T["landq%d" % r][:, a:c].bitcast(dt.uint8), lq[:, a:c].bitcast(dt.uint8), "arrq%d%d" % (r, k), [], every)
 
     def constants(codes, scales, tile, keys, name):
@@ -268,11 +289,11 @@ def rank_program(g, core, T, topo):
             V(lambda q: q.quantize_mx(codes[:, 128 * b:128 * b + 128], scales[:, 128 * b:128 * b + 128], tile[:, 3 - b:515 - b]),
               keys, ["%s.%d" % (name, b)])
 
+    for t in range(4):
+        V(lambda q: q.tensor_scalar(T.ht4[:, 24 * t:24 * t + 24], T.hti[:], 4.0, float(t), ALU.mult, ALU.add), ["hti"], ["ht4.%d" % t])
     for h in range(NP):
         quantise_state(0, h)
         score(0, h, T.uq, T.us, ["uq", "us"])
-    for t in range(4):
-        V(lambda q: q.tensor_scalar(T.ht4[:, 24 * t:24 * t + 24], T.hti[:], 4.0, float(t), ALU.mult, ALU.add), ["hti"], ["ht4.%d" % t])
     for t in range(2):
         lay("s", 0, t)
     for h in range(NP):
@@ -283,20 +304,19 @@ def rank_program(g, core, T, topo):
         last = r == 2
         xn, X, Y = "x_%d" % r, T["x_%d" % r], T["x_%d" % (r + 1)]
         sk = ["bits.%d" % h for h in range(NP)]
-        tk = ["tab.%d" % s for s in range(7)]
         glf, gk = T["glf%d" % r], ["glf%d" % r]
 
         def unpack(k, b):
-            a, c = PARTS[k]
+            a, c = UNPACKED[k]
             ps, pn = bank(k)
             op("t", lambda q: q.matmul_mx(ps[:, 512 * b:512 * b + c - a], T.eq[:, 128 * b:128 * b + 128], T.es[:, 128 * b:128 * b + 128],
                                           T["landq%d" % r][:, a:c], T["lands%d" % r][:, a:c], True, True),
                ["eq.%d" % b, "landq%d.0" % r, "landq%d.%d" % (r, k)], ["%s.%d" % (pn, b)])
 
         def larger(b, a, c):
-            k = 0 if a < PARTS[1][0] else 1
+            k = 0 if a < UNPACKED[1][0] else 1
             ps, pn = bank(k)
-            at = 512 * b - PARTS[k][0]
+            at = 512 * b - UNPACKED[k][0]
             V(lambda q: q.tensor_tensor(T.m[:, C * b + a:C * b + c], ps[:, at + a:at + c], X[:, 4 * a + b:4 * c:4], ALU.max),
               ["%s.%d" % (pn, b)] + whole(xn), ["m.%d.%d" % (b, j) for j in range(a // 128, c // 128)])
 
@@ -306,19 +326,19 @@ def rank_program(g, core, T, topo):
             send(r, T.bland[:], T.bl[:], "arrb", sk)
             op("g", lambda q: q.affine_select(T.et[:], T.e0[:], [[1, 516]], ALU.is_equal, 0.0, -3, -4), ["e0"], ["et"])
             V(lambda q: q.tensor_scalar(T.gt[:], T.glb[:], T.fa[:, 3:4], T.fa[:, 4:5], ALU.mult, ALU.add), ["glb", "glb0", "fa3", "fa4"], ["gt"])
-            lay("v", 0, 2)
+            lay("v", 0, 3, *HALVES[0])
             V(lambda q: q.tensor_tensor(T.gu[:], T.gt[:], T.gli[:], ALU.add), ["gt", "gli"], ["gu"])
-            lay("v", 0, 3)
+            lay("v", 0, 3, *HALVES[1])
             V(lambda q: q.tensor_copy(T.far0[:], T.gu[:]), ["gu"], ["far0"])
+            lay("v", 0, 2)
             lay_table(0)
-            send(1, T.far1[:], T.far0[:], "arrg1", ["far0"])
+            S(lambda q: q.activation(T.x64[:], T.x_0[:], COPY, scale=64.0), whole("x_0"), whole("x64"))
+            V(lambda q: q.tensor_copy(T.hfar[:], T.hland[:]), ["hland"], ["hfar"])
             for k in range(2):
                 quantise_laid(r, k)
+            send(1, T.far1[:], T.far0[:], "arrg1", ["far0"])
             send_laid(r, [])
-            for w in range(2):
-                copy("v", T.tab[:, C * w:C * w + C], T.ident[:, 191:191 + C], ik, tk[:FIRST] if w == 0 else tk[FIRST:])
-            V(lambda q: q.tensor_copy(T.hfar[:], T.hland[:]), ["hland"], ["hfar"])
-            S(lambda q: q.activation(T.x64[:], T.x_0[:], COPY, scale=64.0), whole("x_0"), whole("x64"))
+            constants(T.eq, T.es, T.et, ["et"], "eq")
         for a, c in HALVES:
             V(lambda q: q.tensor_tensor(T.t1[:, a:c], sign[:].indirect(host[:, a // 16:c // 16]), glf[:, 2 * a + 1:2 * c:2], ALU.mult),
               keys + gk, ["t1.%d" % a])
@@ -326,69 +346,95 @@ def rank_program(g, core, T, topo):
             V(lambda q: q.tensor_tensor(T.ft[:, 16 + a:16 + c], T.t1[:, a:c], glf[:, 2 * a:2 * c:2], ALU.add), ["t1.%d" % a] + gk,
               ["ft0" if a == 0 else "ft"])
 
-        def spread(s, key, a, sem, n):
-            w = 0 if s < FIRST else C
-            dma("y", sem, n, T.tab[s:128:16, w:w + C], T[key][16 * s:16 * s + 8, a:a + C], [key], ["tab.%d" % s])
-        for s in (0, 1):
-            spread(s, "ft", 16, "fa%d" % r, 2)
-        for s in (2, 4, 5):
-            spread(s, "ft", 16, "fb%d" % r, 3)
+        def spread(e, s, name, a, keys):
+            w = C * WINDOW[s]
+            dma(e, "f%d%d" % (r, s), 1, T.tab[s:128:16, w:w + C], T[name][16 * s:16 * s + 8, a:a + C], keys, ["tab.%d" % s])
+        for e, s in zip("yyyy", (0, 1, 3, 5)):
+            spread(e, s, "ft", 16, ["ft"])
+        if last:
+            dma("y", "fo", 1, T.fout[:], T.ft[0:128:16, 16:16 + C], ["ft"], ["fout"])
         V(lambda q: q.transpose(T.ta[:, 0:C // 2], T.ft[:, 16:16 + C // 2]), ["ft0"], ["ta0"])
         V(lambda q: q.transpose(T.tb[:, 0:C // 2], T.ft[:, 0:C // 2]), ["ft0", "pad0"], ["tb0"])
         V(lambda q: q.transpose(T.ta[:, C // 2:], T.ft[:, 16 + C // 2:16 + C]), ["ft"], ["ta"])
         V(lambda q: q.transpose(T.tb[:, C // 2:], T.ft[:, C // 2:]), ["ft", "pad1"], ["tb"])
-        for k, (out, in_) in enumerate(((T.fl[32:64, 1:24:2], T.ta[32:64, 0:C:32]), (T.fl[96:128, 0:24:2], T.ta[64:96, 16:C:32]),
-                                        (T.fl[32:64, 0:24:2], T.tb[32:64, 0:C:32]), (T.fl[96:128, 1:24:2], T.tb[64:96, 48:C + 32:32]))):
-            V(lambda q: q.tensor_scalar(out, in_, 192.0, None, ALU.add), ["ta" if k < 2 else "tb"], ["fl.%d" % k])
+        def as_list(name, Q):
+            for odd in range(2):
+                p = 32 * Q
+                in_ = T.tb[p:p + 32, 48:C + 32:32] if odd else T.ta[p:p + 32, 16:C:32]
+                V(lambda q: q.tensor_scalar(T[name][p + 32:p + 64, odd:24:2], in_, 192.0, None, ALU.add), ["tb" if odd else "ta"],
+                  ["fl.%d" % (2 * Q + odd)])
+
+        def compose(out, name, keys, shares=HALVES):
+            for e, (a, c) in zip("vs", shares):
+                copy(e, T[out][:, a:c], T.ft[:, 16:16 + C].indirect(T[name][:, a // 16:c // 16]), ["ft", "fl"] + keys,
+                     [out if a else out + "0"])
+        as_list("fl", 0)
+        as_list("fm", 1)
+        as_list("fm", 2)
+        compose("fh", "fl", ["fl.0", "fl.1"], [(0, 160), (160, C)])
+        spread("y", 2, "fh", 0, ["fh0", "fh"])
         if r > 0:
             quantise_laid(r, 0)
-        for e, (a, c) in zip("vs", HALVES):
-            copy(e, T.fg[:, a:c], T.ft[:, 16:16 + C].indirect(T.fl[:, a // 16:c // 16]), ["ft", "fl"] + ["fl.%d" % k for k in range(4)],
-                 ["fg" if a else "fg0"])
-        before("y", ["fg0"])
-        for s in (3, 6):
-            spread(s, "fg", 0, "fc%d" % r, 2)
+        compose("fg", "fm", ["fl.%d" % k for k in range(2, 6)], HALVES if r == 0 else [(0, 96), (96, C)])
+        for e, s in zip("ys", (4, 6)):
+            spread(e, s, "fg", 0, ["fg0", "fg"])
+        if r > 0:
+            quantise_laid(r, 1)
         fill = []
         if r == 0:
-            dma("y", "ld_w", 2, T.wq[:].bitcast(dt.uint8), T.wc[:], tk, ["wq"])
-            dma("y", "ld_w", 2, T.wsp[:], T.ws[:], [], ["wsp"])
+            dma("y", "ld_w", 2, T.wsp[:], T.ws[:], tk, ["wsp"])
             dma("y", "ld_v", 1, T.vt[:], T.v[:], [], ["vt"])
             send(2, T.far2[:], T.far0[:], "arrg2", ["fg0", "fg"])
-            constants(T.eq, T.es, T.et, ["et"], "eq")
             for k in range(2):
                 for b in range(4):
                     unpack(k, b)
-            fill += 2 * [lambda: None] + [lambda b=b, a=a, c=c: larger(b, a, c) for a, c in PIECES for b in range(4)]
+            fill += [lambda: None] + [lambda b=b, a=a, c=c: larger(b, a, c) for a, c in PIECES for b in range(4)]
         else:
-            quantise_laid(r, 1)
             send_laid(r, ["fg0", "fg"])
         if last:
-            dma("y", "fo", 1, T.fout[:], T.ft[0:128:16, 16:16 + C], ["ft"], ["fout"])
             send(r, T.fin[:], T.fout[:], "arrf", ["fout"])
             dma("y", "fi", 1, T.fland[0:128:16, :], T.fin[:], ["fin"], ["fland"])
             fill.append(lambda: V(lambda q: q.quantize_mx(T.vq[:], T.vs[:], T.vt[:]), ["vt"], ["vq"]))
+        def gap():
+            if fill:
+                fill.pop(0)()
+
+        def collect(e, grp, a, key, Q):
+            p, c = 32 * (grp // 2), 16 * (grp % 2) + 4 * Q
+            copy(e, T.coll[p:p + 32, c:c + 4], T.w2[32 * Q:32 * Q + 32, a:a // 64 * 64 + 64:16], [key], ["coll.%d.%d" % (grp, Q)])
+
         for s, (onward, found) in enumerate(WALK):
-            def gap():
-                if fill:
-                    fill.pop(0)()
             o, ok = (T.ov0, "ov0") if s == 0 else (T.ov, "ov")
             a = 64 * s
-            w, keys = (0, tk[:FIRST]) if s < FIRST else (C, tk[FIRST:])
-            V(lambda q: q.tensor_copy(T.w1[:], T.tab[:, w:w + C].indirect(o[:])), keys + [ok], ["w1"])
-            gap()
-            V(lambda q: q.transpose(T.w2[:, a:a + 64], T.w1[:]), ["w1"], ["w2.%d" % s])
-            gap()
-            if onward is not None:
-                V(lambda q: q.tensor_scalar(T.ov[:], T.w2[:, a + onward:a + 64:16], 192.0, None, ALU.add), ["w2.%d" % s], ["ov"])
+            end = onward is None
+            V(lambda q: q.tensor_copy(T.w1[:], T.tab[:, C * s:C * s + C].indirect(o[:])), window(s) + [ok], ["w1"])
+            if end:
+                V(lambda q: q.tensor_copy(T.w3[:], T.tab[:, C * s:C * s + C].indirect(T.ov4[:])), window(s) + ["ov4"], ["w3"])
+            else:
                 gap()
-            moves = [(grp, slot, Q) for grp, slot in found for Q in range(4) if grp > 0 or r == 0]
-            for k, (grp, slot, Q) in enumerate(moves):
-                p, c = 32 * (grp // 2), 16 * (grp % 2) + 4 * Q
-                copy("v" if onward is None and k % 2 else "s", T.coll[p:p + 32, c:c + 4], T.w2[32 * Q:32 * Q + 32, a + slot:a + 64:16],
-                     ["w2.%d" % s], ["coll.%d.%d" % (grp, Q)])
-            if s == 0 and not last:
-                lay_table(r + 1)
+            V(lambda q: q.transpose(T.w2[:, a:a + 64], T.w1[:]), ["w1"], ["w2.%d" % s])
+            if end:
+                V(lambda q: q.transpose(T.w2[:, a + 64:a + 128], T.w3[:]), ["w3"], ["w2.4"])
+            else:
+                gap()
+                V(lambda q: q.tensor_scalar(T.ov[:], T.w2[:, a + onward:a + 64:16], 192.0, None, ALU.add), ["w2.%d" % s], ["ov"])
+                if s == 2:
+                    V(lambda q: q.tensor_scalar(T.ov4[:], T.w2[:, a + 3:a + 64:16], 192.0, None, ALU.add), ["w2.%d" % s], ["ov4"])
+                for k in range(3 if s == 0 else 1):
+                    gap()
+            moves = [(grp, a + slot, "w2.%d" % s, Q) for grp, slot in found for Q in range(4)]
+            if end:
+                moves += [(4, a + 64 + 8, "w2.4", Q) for Q in range(4)]
+            for k, move in enumerate(moves):
+                collect("v" if end and k % 2 else "s", *move)
+            if s == 0 and r == 0:
+                lay_table(1)
+        if r == 1:
+            lay_table(2)
+        while len(fill) > 1:
+            gap()
         V(lambda q: q.transpose(T.lt[:], T.coll[:]), ["coll.%d.%d" % (grp, Q) for grp in range(8) for Q in range(4)], ["lt"])
+        gap()
         V(lambda q: q.tensor_scalar(T["vl%d" % r][:], T.lt[:, 0:24], 192.0, None, ALU.add), ["lt"], ["vl%d" % r])
         lists = "vl0" if r == 0 else "vland%d" % r
         if r > 0:
@@ -396,7 +442,7 @@ def rank_program(g, core, T, topo):
             for k in range(2):
                 for b in range(4):
                     unpack(k, b)
-                    larger(b, *PARTS[k])
+                    larger(b, *SENT[k])
 
         def pick(e, h, b):
             a, c = PIECES[h]
@@ -452,12 +498,12 @@ def rank_program(g, core, T, topo):
             if last:
                 S(lambda q: q.activation(T.plb[:], T.fland[:].indirect(T.vland2[:]), ActivationFunctionType.Identity, bias=192.0),
                   ["fland", "vland2"], ["plb"])
-                for k in range(4):
-                    dma("s", "sts", 4, T.osc[4 * k:4 * k + 4, :], T.xs3[32 * k:32 * k + 4, :], ["xq3.%d" % j for j in range(NP)], [])
                 dma("s", "stp", 1, T.pl[:], T.plb[0:128:16, :], ["plb"], [])
+                for k in range(4):
+                    dma("sy"[k % 2], "sts", 4, T.osc[4 * k:4 * k + 4, :], T.xs3[32 * k:32 * k + 4, :], ["xq3.%d" % j for j in range(NP)], [])
             else:
                 for t in range(4):
-                    lay("s", r + 1, t)
+                    lay("s", r + 1, t, 0, C if t < 3 else PARTS[1][0])
 
         for word in ORDER.split():
             kind, h, more = word[0], int(word[1]), word[2:]
@@ -468,5 +514,7 @@ def rank_program(g, core, T, topo):
             elif kind == "s":
                 scale(more[1], h, int(more[0]))
             else:
+                if word == "r2" and not last:
+                    lay("v", r + 1, 3, *PARTS[1])
                 {"w": product, "q": state, "r": read, "e": lambda h: rest()}[kind](h)
     finish()

from concourse.mybir import dt, AluOpType, ActivationFunctionType

C = 384
PIECES = [(0, 128), (128, 256), (256, 384)]
HALVES = [(0, C // 2), (C // 2, C)]
PARTS = [(0, 256), (256, C)]
SENT = [(0, 304), (304, C)]
UNPACKED = [(0, 304), (256, C)]
STEP = [1, 2, 4]
ORDER = ("p00s p01s p02v p03v p10s p11s p12v w0 p13v p20s p21s p22s w1 p23v a00 a01 a02 a03 w2 s00s s01s s02s s03s "
         "a10 a11 a12 a13 s10s s11s s12s s13s q0 a20 a21 a22 a23 s20s s21s q1 s22v s23v r0 q2 e0 r1 r2")
WINDOW = [0, 1, 1, 2, 2, 3, 3]
WALK = [(0, []), (2, [(1, 8), (2, 1), (3, 2)]), (4, []), (None, [(5, 8), (6, 5), (7, 6)])]
ALU = AluOpType
COPY = ActivationFunctionType.Copy

SCRATCH = {
    "ut": ("sbuf", [128, 512], "bfloat16"), "vt": ("sbuf", [128, 512], "bfloat16"),
    "uq": ("sbuf", [128, 128], "float8_e4m3fn_x4"), "us": ("sbuf", [128, 128], "uint8"),
    "vq": ("sbuf", [128, 128], "float8_e4m3fn_x4"), "vs": ("sbuf", [128, 128], "uint8"),
    "wq": ("sbuf", [128, 512], "float8_e4m3fn_x4"), "wsp": ("sbuf", [128, 512], "uint8"),
    "e0": ("sbuf", [128, 516], "bfloat16"), "et": ("sbuf", [128, 516], "bfloat16"),
    "eq": ("sbuf", [128, 512], "float8_e4m3fn_x4"), "es": ("sbuf", [128, 512], "uint8"),
    "x64": ("sbuf", [128, 4 * C], "bfloat16"), "lx": ("sbuf", [128, 4 * C], "bfloat16"),
    "ht4": ("sbuf", [128, 96], "uint16"),
    "m": ("sbuf", [128, 4 * C], "bfloat16"), "z": ("sbuf", [128, 4 * C], "bfloat16"),
    "zq": ("sbuf", [128, C], "float8_e4m3fn_x4"), "zs": ("sbuf", [128, C], "uint8"),
    "gli": ("sbuf", [128, 48], "int32"), "glb": ("sbuf", [128, 48], "int32"), "hti": ("sbuf", [128, 24], "int32"),
    "gt": ("sbuf", [128, 48], "float32"), "gu": ("sbuf", [128, 48], "float32"), "ht16": ("sbuf", [128, 24], "uint16"),
    "bits": ("sbuf", [128, C], "bfloat16"), "bl": ("sbuf", [128, C], "bfloat16"), "bland": ("sbuf", [128, C], "bfloat16"),
    "t1": ("sbuf", [128, C], "float32"), "ft": ("sbuf", [128, C + 32], "bfloat16"), "tab": ("sbuf", [128, 5 * C], "bfloat16"),
    "ta": ("sbuf", [128, C], "bfloat16"), "tb": ("sbuf", [128, C + 32], "bfloat16"), "fl": ("sbuf", [128, 24], "uint16"),
    "fg": ("sbuf", [128, C], "bfloat16"), "fh": ("sbuf", [128, C], "bfloat16"), "fm": ("sbuf", [128, 24], "uint16"),
    "hout": ("dram", [128, 24], "int32"), "hland": ("sbuf", [128, 24], "int32"), "hfar": ("sbuf", [128, 24], "uint16"),
    "fout": ("dram", [128, 24], "bfloat16"), "fin": ("dram", [128, 24], "bfloat16"),
    "upi": ("sbuf", [128, 8], "int32"), "up": ("sbuf", [128, 8], "uint16"),
    "uq0": ("sbuf", [128, 128], "float8_e4m3fn_x4"), "us0": ("sbuf", [128, 128], "uint8"),
    "w3": ("sbuf", [128, 64], "bfloat16"), "ov4": ("sbuf", [128, 4], "uint16"), "j0": ("sbuf", [128, 4], "float32"),
    "w1": ("sbuf", [128, 64], "bfloat16"), "w2": ("sbuf", [128, 7 * 64], "bfloat16"),
    "coll": ("sbuf", [128, 32], "bfloat16"), "lt": ("sbuf", [128, 32], "bfloat16"),
    "ov0": ("sbuf", [128, 4], "uint16"), "ov": ("sbuf", [128, 4], "uint16"),
    "ident": ("sbuf", [128, 2 * C], "float32"), "ip": ("sbuf", [128, 1], "int32"),
    "kcol": ("sbuf", [128, 4], "float32"), "ia": ("sbuf", [128, 4], "int32"), "fa": ("sbuf", [128, 8], "float32"),
    "ysb": ("sbuf", [128, C], "float32"), "plb": ("sbuf", [128, C], "float32"), "fland": ("sbuf", [128, C], "bfloat16"),
    "psa": ("psum", [128, 2048], "float32"), "psb": ("psum", [128, 2048], "float32"),
}
for _r in range(3):
    SCRATCH["landq%d" % _r] = ("sbuf", [128, C], "float8_e4m3fn_x4")
    SCRATCH["lands%d" % _r] = ("sbuf", [128, C], "uint8")
    SCRATCH["lq%d" % _r] = ("sbuf", [128, C], "float8_e4m3fn_x4")
    SCRATCH["ls%d" % _r] = ("sbuf", [128, C], "uint8")
    SCRATCH["far%d" % _r] = ("sbuf", [128, 48], "uint16")
    SCRATCH["glf%d" % _r] = ("sbuf", [128, 2 * C], "float32")
    SCRATCH["vl%d" % _r] = ("sbuf", [128, 24], "uint16")
    SCRATCH["vland%d" % _r] = ("sbuf", [128, 24], "uint16")
for _r in range(4):
    SCRATCH["x_%d" % _r] = ("sbuf", [128, 4 * C], "bfloat16")
    SCRATCH["xq%d" % _r] = ("sbuf", [128, C], "float8_e4m3fn_x4")
    SCRATCH["xs%d" % _r] = ("sbuf", [128, C], "uint8")

SEMAPHORES = ["cv", "cs", "ct", "cg", "sent", "arrf", "arrb", "fo", "fi", "ld_ho", "arrh",
              "ld_gl", "ld_ht", "ld_u", "ld_w", "ld_v", "ld_x0", "ld_x1", "ld_x2",
              "st0", "st1", "st2", "sty0", "sty1", "sts", "stp"]
for _r in range(3):
    SEMAPHORES += ["arrq%d0" % _r, "arrq%d1" % _r, "arrl%d" % _r, "arrg%d" % _r] + ["f%d%d" % (_r, _s) for _s in range(7)]


def tracker(g, T):
    queue = {"v": g.vector, "s": g.scalar, "t": g.tensor, "g": g, "y": g.sync}
    csem = {"v": "cv", "s": "cs", "t": "ct", "g": "cg"}
    count = {k: 0 for k in csem}
    know = {k: {} for k in queue}
    clock, writer, readers = {}, {}, {}
    total, waited = {}, {}

    def merge(a, b):
        for s, n in b.items():
            if a.get(s, 0) < n:
                a[s] = n

    def need(e, toks):
        todo = {}
        for s, n in toks:
            if know[e].get(s, 0) < n:
                todo[s] = max(todo.get(s, 0), n)
        for s in list(todo):
            for s2 in list(todo):
                if s2 != s and s in todo and clock.get((s2, todo[s2]), {}).get(s, 0) >= todo[s]:
                    del todo[s]
        for s, n in todo.items():
            queue[e].wait_ge(T.sem[s], n)
            waited[s] = max(waited.get(s, 0), n)
            merge(know[e], clock.get((s, n), {}))
            merge(know[e], {s: n})

    def deps(e, reads, writes):
        own = csem.get(e)
        toks = [writer[k] for k in list(reads) + list(writes) if k in writer]
        for k in writes:
            toks += [t for t in readers.get(k, []) if t[0] != own]
        return toks

    def record(tok, reads, writes):
        for k in reads:
            readers.setdefault(k, []).append(tok)
        for k in writes:
            writer[k] = tok
            readers[k] = []

    def op(e, fn, reads, writes):
        need(e, deps(e, reads, writes))
        count[e] += 1
        tok = (csem[e], count[e])
        fn(queue[e]).then_inc(T.sem[csem[e]], 1)
        total[csem[e]] = count[e]
        clock[tok] = dict(know[e])
        clock[tok][tok[0]] = tok[1]
        record(tok, reads, writes)

    def dma(e, sem, n, out, in_, reads, writes):
        d = deps(e, reads, writes)
        need(e, [t for t in d if t[0] != sem])
        tok = (sem, 16 * n)
        queue[e].dma_start(out, in_).then_inc(T.sem[sem], 16)
        total[sem] = 16 * n
        c = clock.setdefault(tok, dict(know[e]))
        for s in list(c):
            c[s] = max(c[s], know[e].get(s, 0))
        record(tok, reads, writes)

    def arrives(sem, n, keys):
        total[sem] = n
        for k in keys:
            writer[k] = (sem, n)

    def before(e, reads):
        need(e, [writer[k] for k in reads])

    def finish():
        for s, n in total.items():
            if waited.get(s, 0) < n:
                g.wait_ge(T.sem[s], n)
    return op, dma, arrives, before, finish, total


def rank_program(g, core, T, topo):
    rank = T.rank_of(core)
    if rank is None:
        return
    op, dma, arrives, before, finish, total = tracker(g, T)
    partner = [T.cores[rank ^ s] for s in STEP]
    NP = len(PIECES)

    every = [topo.engines(core, p) for p in partner]
    engines = [e[:8] for e in every]

    def send(r, out, in_, sem, keys, use=engines):
        before("g", keys)
        rid, pid = topo.addr(partner[r])[:2]
        g.remote_dma(out, in_, T.sem[sem], T.sem.sent, pid, rid, sum(1 << k for k in use[r]))
        total["sent"] = total.get("sent", 0) + len(use[r])

    for r in range(3):
        arrives("arrq%d0" % r, 2 * len(every[r]), ["landq%d.0" % r])
        arrives("arrq%d1" % r, len(every[r]), ["landq%d.1" % r])
        if r > 0:
            arrives("arrl%d" % r, len(engines[r]), ["vland%d" % r])
            arrives("arrg%d" % r, len(engines[r]), ["far%d" % r])
    arrives("arrh", len(engines[0]), ["hland"])
    arrives("arrb", len(engines[0]), ["bland"])
    arrives("arrf", len(engines[2]), ["fin"])

    def piece(name, h):
        return ["%s.%d.%d" % (name, b, h) for b in range(4)]

    def whole(name):
        return [k for h in range(NP) for k in piece(name, h)]

    V = lambda fn, r, w: op("v", fn, r, w)
    S = lambda fn, r, w: op("s", fn, r, w)

    def copy(e, out, in_, r, w):
        op(e, {"v": lambda q: q.tensor_copy(out, in_), "s": lambda q: q.activation(out, in_, COPY)}[e], r, w)

    dma("y", "ld_ho", 1, T.hout[:], T.ht[:], [], ["hout"])
    dma("y", "ld_u", 1, T.ut[:], T.u[:], [], ["ut"])
    dma("y", "ld_ht", 1, T.hti[:], T.ht[:], [], ["hti"])
    cut = 4 * PIECES[-1][0]
    dma("y", "ld_x0", 1, T.x_0[:, 0:cut], T.x[:, 0:cut], [], [k for h in range(NP - 1) for k in piece("x_0", h)])
    dma("y", "ld_x1", 1, T.x_0[:, cut:], T.x[:, cut:], [], piece("x_0", NP - 1))
    dma("y", "ld_gl", 3, T.gli[:], T.gl[:], [], ["gli"])
    dma("y", "ld_gl", 3, T.glb[1:128, :], T.gl[0:127, :], [], ["glb"])
    dma("y", "ld_gl", 3, T.glb[0:1, :], T.gl[0:1, :], [], ["glb0"])
    dma("y", "ld_w", 2, T.wq[:].bitcast(dt.uint8), T.wc[:], [], ["wq"])

    op("g", lambda q: q.iota(T.upi[:], [[16, 8]], 0, 0), [], ["upi"])
    op("g", lambda q: q.iota(T.ip[:], [[0, 1]], 0, 1), [], ["ip"])
    op("g", lambda q: q.iota(T.kcol[:], [[1, 4]], 0, 0, allow_small_or_imprecise_dtypes=True), [], ["kcol"])
    op("g", lambda q: q.iota(T.ident[:, 0:256], [[1, 256]], 1 - C, 0, allow_small_or_imprecise_dtypes=True), [], ["ident.0"])
    for k in (1, 2):
        S(lambda q: q.activation(T.ident[:, 256 * k:256 * k + 256], T.ident[:, 0:256], COPY, bias=256.0 * k), ["ident.0"], ["ident.%d" % k])
    ik = ["ident.%d" % k for k in range(3)]
    V(lambda q: q.memset(T.e0[:], 1.0), [], ["e0"])
    send(0, T.hland[:], T.hout[:], "arrh", ["hout"])
    tk = ["tab.%d" % s for s in range(7)]

    def window(w):
        return [tk[s] for s in range(7) if WINDOW[s] == w]

    def identity(w):
        copy("s", T.tab[:, C * w:C * w + C], T.ident[:, 191:191 + C], ik, window(w))
    identity(1)
    identity(3)
    for w in (0, 2):
        V(lambda q: q.memset(T.tab[:, C * w:C * w + C], 0.0), [], window(w))
    V(lambda q: q.memset(T.fland[:], 0.0), [], ["fland"])
    V(lambda q: q.memset(T.ft[:, 0:16], 0.0), [], ["pad0"])
    V(lambda q: q.memset(T.ft[:, 16 + C:], 0.0), [], ["pad1"])
    V(lambda q: q.memset(T.fm[:], 0), [], ["fl.%d" % k for k in range(2, 6)])
    V(lambda q: q.memset(T.fl[:], 0), [], ["fl", "fl.0", "fl.1"])
    V(lambda q: q.tensor_copy(T.up[:], T.upi[:]), ["upi"], ["up"])
    V(lambda q: q.tensor_scalar(T.ia[:, 3:4], T.ip[:], 1, None, ALU.bitwise_and), ["ip"], ["ia3"])
    V(lambda q: q.tensor_scalar(T.ia[:, 0:1], T.ip[:], 31, None, ALU.bitwise_and), ["ip"], ["ia0"])
    V(lambda q: q.tensor_scalar(T.ia[:, 1:2], T.ip[:], 5, None, ALU.arith_shift_right), ["ip"], ["ia1"])
    V(lambda q: q.tensor_scalar(T.fa[:, 3:4], T.ia[:, 3:4], -1.0, None, ALU.mult), ["ia3"], ["fa3"])
    V(lambda q: q.tensor_scalar(T.fa[:, 4:5], T.ia[:, 3:4], 192.0, 191.0, ALU.mult, ALU.add), ["ia3"], ["fa4"])
    V(lambda q: q.tensor_scalar(T.fa[:, 0:1], T.ia[:, 0:1], 16.0, None, ALU.mult), ["ia0"], ["fa0"])
    V(lambda q: q.tensor_scalar(T.fa[:, 1:2], T.ia[:, 1:2], 4.0, T.fa[:, 0:1], ALU.mult, ALU.add), ["ia1", "fa0"], ["fa1"])
    V(lambda q: q.tensor_scalar(T.ov0[:], T.kcol[:], T.fa[:, 1:2], float(C - 1), ALU.add, ALU.min), ["kcol", "fa1"], ["ov0"])
    V(lambda q: q.tensor_scalar(T.j0[:], T.kcol[:], T.fa[:, 1:2], float(C - 1), ALU.add, ALU.min), ["kcol", "fa1"], ["j0"])

    V(lambda q: q.quantize_mx(T.uq0[:], T.us0[:], T.ut[:]), ["ut"], ["uq0"])
    V(lambda q: q.tensor_copy(T.uq[:].bitcast(dt.uint32), T.uq0[:].bitcast(dt.uint32).indirect(T.up[:])), ["uq0", "up"], ["uq"])
    copy("s", T.us[:], T.us0[:].indirect(T.up[:]), ["uq0", "up"], ["us"])
    S(lambda q: q.activation(T.w2[:, 0:64:16], T.j0[:], COPY, bias=-192.0), ["j0"], ["w2.0"])
    for Q in range(4):
        copy("s", T.coll[0:32, 4 * Q:4 * Q + 4], T.w2[32 * Q:32 * Q + 32, 0:64:16], ["w2.0"], ["coll.0.%d" % Q])

    def bank(h):
        return (T.psb, "psb") if h % 2 == 0 else (T.psa, "psa")

    def score_bank(h):
        a, b = PIECES[h]
        ps, pn = bank(NP - 2 if h < NP - 1 else NP - 1)
        k = h if h < NP - 1 else 0
        return ps[:, 512 * k:512 * k + b - a], "%s.%d" % (pn, k)

    def quantise_state(r, h):
        a, b = PIECES[h]
        V(lambda q: q.quantize_mx(T["xq%d" % r][:, a:b], T["xs%d" % r][:, a:b], T["x_%d" % r][:, 4 * a:4 * b]),
          piece("x_%d" % r, h), ["xq%d.%d" % (r, h)])

    def score(r, h, wq, ws, keys):
        a, b = PIECES[h]
        ps, pn = score_bank(h)
        op("t", lambda q: q.matmul_mx(ps, wq[:], ws[:], T["xq%d" % r][:, a:b], T["xs%d" % r][:, a:b], True, True),
           keys + ["xq%d.%d" % (r, h)], [pn])

    def signs(h, out):
        a, b = PIECES[h]
        ps, pn = score_bank(h)
        V(lambda q: q.tensor_scalar(out[:, a:b], ps, 0.0, None, ALU.is_gt), [pn], ["bits.%d" % h])

    def lay_table(r):
        copy("s", T["glf%d" % r][:], T.ident[:].indirect(T["far%d" % r][:]), ik + ["far%d" % r], ["glf%d" % r])

    def lay(e, r, t, a=0, c=C):
        out, at = T.lx[:, 4 * a + t:4 * c:4], T.ht4[:, 24 * t + a // 16:24 * t + c // 16]
        if r == 0:
            copy(e, out, T.x_0[:].indirect(at), whole("x_0") + ["ht4.%d" % t], ["lx.%d" % t if a == 0 else "lx.4"])
        elif e == "v":
            copy(e, out, T["x_%d" % r][:].indirect(at), whole("x_%d" % r) + ["ht4.%d" % t], ["lx.4"])
        else:
            S(lambda q: q.activation(out, T.x64[:].indirect(at), COPY, scale=0.015625), whole("x64") + ["ht4.%d" % t], ["lx.%d" % t])

    def quantise_laid(r, k):
        a, c = PARTS[k]
        V(lambda q: q.quantize_mx(T["lq%d" % r][:, a:c], T["ls%d" % r][:, a:c], T.lx[:, 4 * a:4 * c]), ["lx.%d" % t for t in range(5)],
          ["lq%d.%d" % (r, k)])

    def send_laid(r, after):
        lq, ls = T["lq%d" % r], T["ls%d" % r]
        send(r, T["lands%d" % r][:], ls[:], "arrq%d0" % r, ["lq%d.0" % r, "lq%d.1" % r] + after, every)
        for k, (a, c) in enumerate(SENT):
            send(r, T["landq%d" % r][:, a:c].bitcast(dt.uint8), lq[:, a:c].bitcast(dt.uint8), "arrq%d%d" % (r, k), [], every)

    def constants(codes, scales, tile, keys, name):
        for b in range(4):
            V(lambda q: q.quantize_mx(codes[:, 128 * b:128 * b + 128], scales[:, 128 * b:128 * b + 128], tile[:, 3 - b:515 - b]),
              keys, ["%s.%d" % (name, b)])

    for t in range(4):
        V(lambda q: q.tensor_scalar(T.ht4[:, 24 * t:24 * t + 24], T.hti[:], 4.0, float(t), ALU.mult, ALU.add), ["hti"], ["ht4.%d" % t])
    for h in range(NP):
        quantise_state(0, h)
        score(0, h, T.uq, T.us, ["uq", "us"])
    for t in range(2):
        lay("s", 0, t)
    for h in range(NP):
        signs(h, T.bl)
    V(lambda q: q.tensor_copy(T.ht16[:], T.hti[:]), ["hti"], ["ht16"])

    for r in range(3):
        last = r == 2
        xn, X, Y = "x_%d" % r, T["x_%d" % r], T["x_%d" % (r + 1)]
        sk = ["bits.%d" % h for h in range(NP)]
        glf, gk = T["glf%d" % r], ["glf%d" % r]

        def unpack(k, b):
            a, c = UNPACKED[k]
            ps, pn = bank(k)
            op("t", lambda q: q.matmul_mx(ps[:, 512 * b:512 * b + c - a], T.eq[:, 128 * b:128 * b + 128], T.es[:, 128 * b:128 * b + 128],
                                          T["landq%d" % r][:, a:c], T["lands%d" % r][:, a:c], True, True),
               ["eq.%d" % b, "landq%d.0" % r, "landq%d.%d" % (r, k)], ["%s.%d" % (pn, b)])

        def larger(b, a, c):
            k = 0 if a < UNPACKED[1][0] else 1
            ps, pn = bank(k)
            at = 512 * b - UNPACKED[k][0]
            V(lambda q: q.tensor_tensor(T.m[:, C * b + a:C * b + c], ps[:, at + a:at + c], X[:, 4 * a + b:4 * c:4], ALU.max),
              ["%s.%d" % (pn, b)] + whole(xn), ["m.%d.%d" % (b, j) for j in range(a // 128, c // 128)])

        sign, host, keys = T.bits, T.ht16, sk + ["ht16"]
        if r == 0:
            sign, host, keys = T.bland, T.hfar, ["bland", "hfar"]
            send(r, T.bland[:], T.bl[:], "arrb", sk)
            op("g", lambda q: q.affine_select(T.et[:], T.e0[:], [[1, 516]], ALU.is_equal, 0.0, -3, -4), ["e0"], ["et"])
            V(lambda q: q.tensor_scalar(T.gt[:], T.glb[:], T.fa[:, 3:4], T.fa[:, 4:5], ALU.mult, ALU.add), ["glb", "glb0", "fa3", "fa4"], ["gt"])
            lay("v", 0, 3, *HALVES[0])
            V(lambda q: q.tensor_tensor(T.gu[:], T.gt[:], T.gli[:], ALU.add), ["gt", "gli"], ["gu"])
            lay("v", 0, 3, *HALVES[1])
            V(lambda q: q.tensor_copy(T.far0[:], T.gu[:]), ["gu"], ["far0"])
            lay("v", 0, 2)
            lay_table(0)
            S(lambda q: q.activation(T.x64[:], T.x_0[:], COPY, scale=64.0), whole("x_0"), whole("x64"))
            V(lambda q: q.tensor_copy(T.hfar[:], T.hland[:]), ["hland"], ["hfar"])
            for k in range(2):
                quantise_laid(r, k)
            send(1, T.far1[:], T.far0[:], "arrg1", ["far0"])
            send_laid(r, [])
            constants(T.eq, T.es, T.et, ["et"], "eq")
        for a, c in HALVES:
            V(lambda q: q.tensor_tensor(T.t1[:, a:c], sign[:].indirect(host[:, a // 16:c // 16]), glf[:, 2 * a + 1:2 * c:2], ALU.mult),
              keys + gk, ["t1.%d" % a])
        for a, c in HALVES:
            V(lambda q: q.tensor_tensor(T.ft[:, 16 + a:16 + c], T.t1[:, a:c], glf[:, 2 * a:2 * c:2], ALU.add), ["t1.%d" % a] + gk,
              ["ft0" if a == 0 else "ft"])

        def spread(e, s, name, a, keys):
            w = C * WINDOW[s]
            dma(e, "f%d%d" % (r, s), 1, T.tab[s:128:16, w:w + C], T[name][16 * s:16 * s + 8, a:a + C], keys, ["tab.%d" % s])
        for e, s in zip("yyyy", (0, 1, 3, 5)):
            spread(e, s, "ft", 16, ["ft"])
        if last:
            dma("y", "fo", 1, T.fout[:], T.ft[0:128:16, 16:16 + C], ["ft"], ["fout"])
        V(lambda q: q.transpose(T.ta[:, 0:C // 2], T.ft[:, 16:16 + C // 2]), ["ft0"], ["ta0"])
        V(lambda q: q.transpose(T.tb[:, 0:C // 2], T.ft[:, 0:C // 2]), ["ft0", "pad0"], ["tb0"])
        V(lambda q: q.transpose(T.ta[:, C // 2:], T.ft[:, 16 + C // 2:16 + C]), ["ft"], ["ta"])
        V(lambda q: q.transpose(T.tb[:, C // 2:], T.ft[:, C // 2:]), ["ft", "pad1"], ["tb"])
        def as_list(name, Q):
            for odd in range(2):
                p = 32 * Q
                in_ = T.tb[p:p + 32, 48:C + 32:32] if odd else T.ta[p:p + 32, 16:C:32]
                V(lambda q: q.tensor_scalar(T[name][p + 32:p + 64, odd:24:2], in_, 192.0, None, ALU.add), ["tb" if odd else "ta"],
                  ["fl.%d" % (2 * Q + odd)])

        def compose(out, name, keys, shares=HALVES):
            for e, (a, c) in zip("vs", shares):
                copy(e, T[out][:, a:c], T.ft[:, 16:16 + C].indirect(T[name][:, a // 16:c // 16]), ["ft", "fl"] + keys,
                     [out if a else out + "0"])
        as_list("fl", 0)
        as_list("fm", 1)
        as_list("fm", 2)
        compose("fh", "fl", ["fl.0", "fl.1"], [(0, 160), (160, C)])
        spread("y", 2, "fh", 0, ["fh0", "fh"])
        if r > 0:
            quantise_laid(r, 0)
        compose("fg", "fm", ["fl.%d" % k for k in range(2, 6)], HALVES if r == 0 else [(0, 96), (96, C)])
        for e, s in zip("ys", (4, 6)):
            spread(e, s, "fg", 0, ["fg0", "fg"])
        if r > 0:
            quantise_laid(r, 1)
        fill = []
        if r == 0:
            dma("y", "ld_w", 2, T.wsp[:], T.ws[:], tk, ["wsp"])
            dma("y", "ld_v", 1, T.vt[:], T.v[:], [], ["vt"])
            send(2, T.far2[:], T.far0[:], "arrg2", ["fg0", "fg"])
            for k in range(2):
                for b in range(4):
                    unpack(k, b)
            fill += [lambda: None] + [lambda b=b, a=a, c=c: larger(b, a, c) for a, c in PIECES for b in range(4)]
        else:
            send_laid(r, ["fg0", "fg"])
        if last:
            send(r, T.fin[:], T.fout[:], "arrf", ["fout"])
            dma("y", "fi", 1, T.fland[0:128:16, :], T.fin[:], ["fin"], ["fland"])
            fill.append(lambda: V(lambda q: q.quantize_mx(T.vq[:], T.vs[:], T.vt[:]), ["vt"], ["vq"]))
        def gap():
            if fill:
                fill.pop(0)()

        def collect(e, grp, a, key, Q):
            p, c = 32 * (grp // 2), 16 * (grp % 2) + 4 * Q
            copy(e, T.coll[p:p + 32, c:c + 4], T.w2[32 * Q:32 * Q + 32, a:a // 64 * 64 + 64:16], [key], ["coll.%d.%d" % (grp, Q)])

        for s, (onward, found) in enumerate(WALK):
            o, ok = (T.ov0, "ov0") if s == 0 else (T.ov, "ov")
            a = 64 * s
            end = onward is None
            V(lambda q: q.tensor_copy(T.w1[:], T.tab[:, C * s:C * s + C].indirect(o[:])), window(s) + [ok], ["w1"])
            if end:
                V(lambda q: q.tensor_copy(T.w3[:], T.tab[:, C * s:C * s + C].indirect(T.ov4[:])), window(s) + ["ov4"], ["w3"])
            else:
                gap()
            V(lambda q: q.transpose(T.w2[:, a:a + 64], T.w1[:]), ["w1"], ["w2.%d" % s])
            if end:
                V(lambda q: q.transpose(T.w2[:, a + 64:a + 128], T.w3[:]), ["w3"], ["w2.4"])
            else:
                gap()
                V(lambda q: q.tensor_scalar(T.ov[:], T.w2[:, a + onward:a + 64:16], 192.0, None, ALU.add), ["w2.%d" % s], ["ov"])
                if s == 2:
                    V(lambda q: q.tensor_scalar(T.ov4[:], T.w2[:, a + 3:a + 64:16], 192.0, None, ALU.add), ["w2.%d" % s], ["ov4"])
                for k in range(3 if s == 0 else 1):
                    gap()
            moves = [(grp, a + slot, "w2.%d" % s, Q) for grp, slot in found for Q in range(4)]
            if end:
                moves += [(4, a + 64 + 8, "w2.4", Q) for Q in range(4)]
            for k, move in enumerate(moves):
                collect("v" if end and k % 2 else "s", *move)
            if s == 0 and r == 0:
                lay_table(1)
        if r == 1:
            lay_table(2)
        while len(fill) > 1:
            gap()
        V(lambda q: q.transpose(T.lt[:], T.coll[:]), ["coll.%d.%d" % (grp, Q) for grp in range(8) for Q in range(4)], ["lt"])
        gap()
        V(lambda q: q.tensor_scalar(T["vl%d" % r][:], T.lt[:, 0:24], 192.0, None, ALU.add), ["lt"], ["vl%d" % r])
        lists = "vl0" if r == 0 else "vland%d" % r
        if r > 0:
            send(r, T[lists][:], T["vl%d" % r][:], "arrl%d" % r, ["vl%d" % r])
            for k in range(2):
                for b in range(4):
                    unpack(k, b)
                    larger(b, *SENT[k])

        def pick(e, h, b):
            a, c = PIECES[h]
            copy(e, T.z[:, 4 * a + b:4 * c:4], T.m[:, C * b:C * b + C].indirect(T[lists][:, a // 16:c // 16]),
                 ["m.%d.%d" % (b, j) for j in range(3)] + [lists], ["z.%d.%d" % (b, h)])

        def product(h):
            a, c = PIECES[h]
            ps, pn = bank(h)
            V(lambda q: q.quantize_mx(T.zq[:, a:c], T.zs[:, a:c], T.z[:, 4 * a:4 * c]), piece("z", h), ["zq.%d" % h])
            for b in range(4):
                op("t", lambda q: q.matmul_mx(ps[:, 512 * b:512 * b + c - a], T.wq[:, 128 * b:128 * b + 128], T.wsp[:, 128 * b:128 * b + 128],
                                              T.zq[:, a:c], T.zs[:, a:c], True, True), ["wq", "wsp", "zq.%d" % h], ["%s.%d" % (pn, b)])

        def add(h, b):
            a, c = PIECES[h]
            ps, pn = bank(h)
            key = ["x64.%d.%d" % (b, h)]
            V(lambda q: q.tensor_tensor(T.x64[:, 4 * a + b:4 * c:4], ps[:, 512 * b:512 * b + c - a], T.x64[:, 4 * a + b:4 * c:4], ALU.add),
              ["%s.%d" % (pn, b)] + key, key)

        def scale(e, h, b):
            a, c = PIECES[h]
            out, in_ = Y[:, 4 * a + b:4 * c:4], T.x64[:, 4 * a + b:4 * c:4]
            op(e, {"v": lambda q: q.tensor_scalar(out, in_, 0.015625, None, ALU.mult),
                   "s": lambda q: q.activation(out, in_, COPY, scale=0.015625)}[e],
               ["x64.%d.%d" % (b, h)], ["x_%d.%d.%d" % (r + 1, b, h)])

        def state(h):
            quantise_state(r + 1, h)
            if last:
                score(r + 1, h, T.vq, T.vs, ["vq"])
                store(h)
            else:
                score(r + 1, h, T.uq, T.us, ["uq"])

        def store(h):
            a, c = PIECES[h]
            dma("y", "st%d" % h, 1, T.oc[:, 4 * a:4 * c], T.xq3[:, a:c].bitcast(dt.uint8), ["xq3.%d" % h], [])


        def read(h):
            if not last:
                return signs(h, T.bits)
            a, c = PIECES[h]
            ps, pn = score_bank(h)
            copy("v", T.ysb[:, a:c], ps, [pn], ["ysb.%d" % h])
            if h != NP - 2:
                a = PIECES[max(h - 1, 0)][0]
                dma("y", "sty%d" % min(h, 1), 1, T.y[:, a:c], T.ysb[:, a:c], ["ysb.%d" % max(h - 1, 0), "ysb.%d" % h], [])

        def rest():
            if last:
                S(lambda q: q.activation(T.plb[:], T.fland[:].indirect(T.vland2[:]), ActivationFunctionType.Identity, bias=192.0),
                  ["fland", "vland2"], ["plb"])
                dma("s", "stp", 1, T.pl[:], T.plb[0:128:16, :], ["plb"], [])
                for k in range(4):
                    dma("sy"[k % 2], "sts", 4, T.osc[4 * k:4 * k + 4, :], T.xs3[32 * k:32 * k + 4, :], ["xq3.%d" % j for j in range(NP)], [])
            else:
                for t in range(4):
                    lay("s", r + 1, t, 0, C if t < 3 else PARTS[1][0])

        for word in ORDER.split():
            kind, h, more = word[0], int(word[1]), word[2:]
            if kind == "p":
                pick(more[1], h, int(more[0]))
            elif kind == "a":
                add(h, int(more))
            elif kind == "s":
                scale(more[1], h, int(more[0]))
            else:
                if word == "r2" and not last:
                    lay("v", r + 1, 3, *PARTS[1])
                {"w": product, "q": state, "r": read, "e": lambda h: rest()}[kind](h)
    finish()
